import numpy as np, ml_dtypes
CORES = [40,41,42,43,44,45,46,47]
N = 8
import mx_ref
BF = ml_dtypes.bfloat16
def cols(t, e):
    v = np.concatenate([t.reshape(128, -1, 4), np.zeros((128, 1, 4), BF)], axis=1)
    return np.ascontiguousarray(v[:, e]).reshape(128, -1)
def cut(t, i, w=512):
    return t[:, w * i:w * i + w]
def pick(q, e):
    c = np.concatenate([q[0].reshape(128, -1, 4), np.zeros((128, 1, 4), np.uint8)], axis=1); s = np.concatenate([q[1], np.ones((16, 1), np.uint8)], axis=1)
    return (np.ascontiguousarray(c[:, e].reshape(128, -1)), np.ascontiguousarray(s[:, e]))
def join(*qs):
    return (np.concatenate([q[0] for q in qs], axis=1), np.concatenate([q[1] for q in qs], axis=1))
def put(q, e, v):
    c, s = q[0].reshape(128, -1, 4).copy(), q[1].copy(); c[:, e] = v[0].reshape(128, -1, 4); s[:, e] = v[1]
    return (c.reshape(128, -1), s)
def pk(c, s):
    return (np.ascontiguousarray(c), mx_ref.live(s))
def emit(q):
    return q[0], q[1]
def decode(q):
    o = []
    for b in range(4):
        e = np.zeros((128, 128, 4), np.float32); e[np.arange(128), np.arange(128), b] = 1
        o.append(mx_ref.matmul(mx_ref.quantize(e.reshape(128, 512).astype(BF)), q))
    return np.stack(o, axis=2).reshape(128, -1)
def f(rng, *shape):
    return mx_ref.flush((rng.standard_normal(shape, dtype=np.float32) * np.exp2(rng.integers(-2, 3, shape[:-1] + (1,)))).astype(BF))
def wide(rng, *shape, cols=0):
    v = rng.standard_normal(shape, dtype=np.float32) * np.exp2(rng.integers(-12, 13, shape)).astype(np.float32)
    if cols: v *= np.repeat(np.exp2(rng.integers(-cols, cols + 1, shape[:-2] + (1, shape[-1] // 4))) * (rng.random(shape[:-2] + (1, shape[-1] // 4)) > 0.0625), 4, axis=-1).astype(np.float32)
    return mx_ref.flush(v.astype(BF))
T, C = 256, 64
def best(s):
    return np.argsort(-(s + np.float32(0)), kind="stable")[:C]
def quant(u, v):
    qu = [mx_ref.quantize(np.ascontiguousarray(u[r])) for r in range(N)]
    return qu, [[mx_ref.quantize(np.ascontiguousarray(cut(v[r], i))) for i in range(4)] for r in range(N)]
def layer(q, qu, qv):
    e = best(mx_ref.matmul(qu, q)[0])
    old = pick(q, e)
    a = np.stack([mx_ref.matmul(t, old) for t in qv], axis=2)
    new = np.maximum(a, np.float32(0)) * np.float32(0.05) + decode(old).reshape(128, C, 4)
    return e, new.reshape(128, -1).astype(BF)
def setup_inputs(rng):
    u = np.zeros((N, 128, 512), BF)
    u[:, :, :4] = f(rng, N, 128, 4)
    return {"x": f(rng, N, 128, 4 * T), "u": u, "v": f(rng, N, 128, 2048), "w": f(rng, N, 128, 512)}
def setup_inputs_spread(rng):
    d = setup_inputs(rng)
    d["x"] = wide(rng, N, 128, 4 * T, cols=3)
    return d
def setup_inputs_ties(rng):
    d = setup_inputs(rng)
    d["x"] = np.stack([cols(d["x"][r], rng.permutation(T) % 5 - 1) for r in range(N)])
    d["u"][1::2] = 0
    return d
def setup_inputs_again(rng):
    d = setup_inputs(rng)
    x, u = d["x"].astype(np.float32).reshape(N, 128, T, 4), np.zeros((N, 128, 512), np.float32)
    good = np.stack([rng.permutation(T) < C for r in range(N)])
    x[:, :32] = (1 + rng.random((N, 32, T, 4))) * np.where(good, 1.0, -1.0)[:, None, :, None]
    u[:, :32, :4] = 1 + rng.random((N, 32, 4))
    d["x"], d["u"] = x.reshape(N, 128, 4 * T).astype(BF), u.astype(BF)
    return d
def setup_inputs_other(rng):
    d = setup_inputs(rng)
    x, u = d["x"].astype(np.float32).reshape(N, 128, T, 4), np.zeros((N, 128, 512), np.float32)
    v = d["v"].astype(np.float32).reshape(N, 128, 4, 128, 4)
    large = np.stack([rng.permutation(T) < C for r in range(N)])
    x[:, :16] = (1 + rng.random((N, 16, T, 4))) * np.where(large, 16.0, 1.0)[:, None, :, None]
    x[:, 16:32] = (0.25 + 0.25 * rng.random((N, 16, T, 4))) * rng.choice([-1.0, 1.0], (N, 16, T, 4))
    u[:, :16, :4] = 1 + rng.random((N, 16, 4))
    u[:, 16:32, :4] = -1 - rng.random((N, 16, 4))
    v[:, :, :, 16:32] = 0
    v[:, :16, :, 16:32] = 256 * (1 + rng.random((N, 16, 4, 16, 4)))
    d["x"], d["u"], d["v"] = x.reshape(N, 128, 4 * T).astype(BF), u.astype(BF), v.reshape(N, 128, 2048).astype(BF)
    return d
def setup_inputs_neg(rng):
    d = setup_inputs(rng)
    d["x"] = np.abs(d["x"].astype(np.float32)).astype(BF)
    d["v"] = (-np.abs(d["v"].astype(np.float32))).astype(BF)
    return d
def check_inputs(d):
    b = []
    for k in ("x", "u", "v", "w"):
        a = np.abs(d[k].astype(np.float32))
        if not (np.isfinite(a).all() and ((a == 0) | (a >= 2.0 ** -30) & (a <= 2.0 ** 30)).all()): b.append("a value of " + k)
    if (d["u"][:, :, 4:].astype(np.float32) != 0).any(): b.append("u has numbers behind its column 0")
    if b: return b
    qu, qv = quant(d["u"], d["v"])
    for r in range(N):
        q = mx_ref.quantize(np.ascontiguousarray(d["x"][r]))
        for k in (1, 2):
            e, new = layer(q, qu[(r + k) % N], qv[(r + k) % N])
            a = np.abs(new.astype(np.float32)).reshape(16, 8, C, 4).max(axis=(1, 3))
            if not ((a == 0) | (a >= 2.0 ** -30) & (a <= 2.0 ** 30)).all(): return ["a number of a made column"]
            q = put(q, e, mx_ref.quantize(new))
    return b
def reference(x, u, v, w):
    oc, osc = np.zeros((N, 128, 4 * T), np.uint8), np.zeros((N, 16, T), np.uint8)
    li, y = np.zeros((N, 2, C), np.float32), np.zeros((N, 128, T), np.float32)
    qu, qv = quant(u, v)
    for d in range(N):
        r = (d - 2) % N
        q = mx_ref.quantize(np.ascontiguousarray(x[r]))
        for k in (1, 2):
            s = (r + k) % N
            e, new = layer(q, qu[s], qv[s])
            q = put(q, e, mx_ref.quantize(new))
            li[d, k - 1] = e
        oc[d], osc[d] = emit(q)
        y[d] = mx_ref.matmul(mx_ref.quantize(np.ascontiguousarray(w[d])), q)
    return {"oc": oc, "osc": osc, "li": li, "y": y}

@@ -1,0 +1,333 @@
+from concourse.bass import DstId, RemoteDMATransfer
+from concourse.mybir import dt, AluOpType, AxisListType, ActivationFunctionType
+
+A = AluOpType
+AF = ActivationFunctionType
+F8, U8, BF, F32, I32, U16 = "float8_e4m3fn_x4", "uint8", "bfloat16", "float32", "int32", "uint16"
+EPS = 2.0 ** -110
+XC = 48
+TC = 64
+W2 = 576
+
+SCRATCH = {}
+
+
+def _pair(n, w):
+    SCRATCH[n] = ("sbuf", [128, w], F8)
+    SCRATCH[n + "s"] = ("sbuf", [128, w], U8)
+
+
+for _n, _w in (("uq", 128), ("vq", 512), ("wq", 128), ("eq", 512), ("kq", 128), ("jq", 128), ("tq", 256), ("ul", 8),
+               ("ub", 128), ("nb", 256), ("aw", W2), ("bw", W2), ("x1q", 128), ("x2q", 128), ("t1", 256), ("t2", 256),
+               ("oh1q", 128), ("oh2q", 128)):
+    _pair(_n, _w)
+for _n, _w, _d in (("xt", 1024, BF), ("ut", 512, BF), ("vt", 2048, BF), ("wt", 512, BF), ("zt", 520, BF), ("idn", 128, BF),
+                   ("kt", 512, BF), ("jt", 512, BF), ("x1b", 512, BF), ("x2b", 512, BF), ("oh1", 512, BF), ("oh2", 512, BF),
+                   ("rl1", 1024, F32), ("rl2", 1024, F32), ("n1b", 1024, BF), ("n2b", 1024, BF), ("g1", 512, BF), ("g2", 512, BF),
+                   ("sc1", 256, BF), ("sc2", 256, BF), ("tb", 384, F32), ("cx", 24, F32), ("x16", 16, F32), ("i16", 128, F32),
+                   ("rm", 128, F32), ("ii", 128, I32), ("ij", 128, I32), ("pc", 1, I32), ("pl", 1, I32), ("zo", 16, U16),
+                   ("oo", 16, U16), ("off1", 16, U16), ("off2", 16, U16), ("pl1", 1, F32), ("pl2", 1, F32), ("ll1", 1, F32),
+                   ("ll2", 1, F32), ("yt", 256, F32)):
+    SCRATCH[_n] = ("sbuf", [128, _w], _d)
+for _n, _w in (("pr", 1024), ("pm", 2048), ("po", 512), ("pp", 512)):
+    SCRATCH[_n] = ("psum", [128, _w], F32)
+
+NEV = 130
+SEMAPHORES = ["s%d" % _i for _i in range(NEV)] + ["lo", "ru", "rt0", "rx1", "rl1", "rt1", "rx2", "rl2", "gate", "gate2"]
+
+
+def rank_program(g, core, T, topo):
+    rank = T.rank_of(core)
+    if rank is None:
+        return
+    n = len(T.cores)
+    nxt, nx2, prv = T.cores[(rank + 1) % n], T.cores[(rank + 2) % n], T.cores[(rank - 1) % n]
+    Q = {"g": g, "v": g.vector, "a": g.scalar, "s": g.sync, "t": g.tensor}
+    V, S, P, Y = g.vector, g.scalar, g.tensor, g.sync
+    made, known, nloc = [], {}, [0]
+
+    def ev(ins, k=1, e=None):
+        if e is None:
+            e = ["s%d" % len(made), 0]
+            made.append(e)
+        ins.then_inc(T.sem[e[0]], k)
+        e[1] += k
+        return e
+
+    def evs(*ins):
+        e = None
+        for i in ins:
+            e = ev(i, 1, e)
+        return e
+
+    def wt(q, *es):
+        for e in es:
+            if e is not None and (q, e[0]) not in known:
+                known[(q, e[0])] = 1
+                Q[q].wait_ge(T.sem[e[0]], e[1])
+
+    def zero(*bufs):
+        return evs(*[V.memset(b[:], 0.0) for b in bufs])
+
+    def bits(es):
+        m = 0
+        for e in es:
+            m |= 1 << e
+        return m
+
+    def send(dst, out, in_, sem):
+        rid, pid, _ = topo.addr(dst)
+        g.remote_dma(out, in_, T.sem[sem], T.sem.lo, pid, rid, topo.mask(core, dst))
+        k = len(topo.engines(core, dst))
+        nloc[0] += k
+        return k
+
+    def send2(dst, pairs, sem):
+        rid, pid, _ = topo.addr(dst)
+        es = topo.engines(core, dst)
+        h = len(es) // 2
+        g.remote_dma_fused([RemoteDMATransfer(dst_ids=[DstId(rid=rid, pnc=pid)], dma_engine_mask=bits(es[i * h:i * h + h]),
+                                              remote_sem=T.sem[sem], srcs=[s], dsts=[d], alu_op=0)
+                            for i, (d, s) in enumerate(pairs)], local_sem=T.sem.lo)
+        nloc[0] += 2 * h
+        return (sem, 2 * h)
+
+    def u8(v):
+        return v.bitcast(dt.uint8)
+
+    def u32(v):
+        return v.bitcast(dt.uint32)
+
+    def load_v(i, j):
+        return ev(Y.dma_start(T.vt[:, 512 * i:512 * j], T.v[:, 512 * i:512 * j]), 16)
+
+    e_u = ev(S.dma_start(T.ut[:, 0:4], T.u[:, 0:4]), 16)
+    e_x = [ev(Y.dma_start(T.xt[:, 512 * i:512 * i + 512], T.x[:, 512 * i:512 * i + 512]), 16) for i in range(2)]
+    e_v = [load_v(0, 1)]
+
+    e_tb0 = evs(V.memset(T.tb[:, 128:384], 0.0))
+    e_cx = evs(V.memset(T.cx[:], 64.0))
+    e_id = evs(V.memset(T.idn[:], 1.0))
+    e_tb1 = evs(V.memset(T.tb[:, 0:128], -EPS))
+    e_u0 = evs(V.memset(T.ut[:, 8:512], 0.0))
+    e_zo = evs(V.memset(T.zo[:], 0), V.memset(T.oo[:], 1))
+    wt("g", e_tb0)
+    e_tb2 = ev(g.affine_select(T.tb[:, 128:256], T.tb[:, 128:256], [[1, 128]], A.is_ge, -EPS, 0, -1))
+    wt("g", e_cx)
+    e_cx = ev(g.affine_select(T.cx[:], T.cx[:], [[-16, 24]], A.is_ge, -1.0, 128, 1))
+    wt("g", e_cx)
+    e_cx = ev(g.affine_select(T.cx[:], T.cx[:], [[16, 24]], A.is_ge, -1.0, 15 - 128, -1))
+    e_16 = ev(g.iota(T.x16[:], [[16, 16]], 0, 0, allow_small_or_imprecise_dtypes=True))
+    wt("g", e_id)
+    e_id = ev(g.affine_select(T.idn[:], T.idn[:], [[1, 128]], A.is_equal, 0.0, 0, -1))
+    e_ii = ev(g.iota(T.ii[:], [[1, 128]], 128, -1))
+    e_xz = zero(T.x1b, T.x2b)
+    e_zz = zero(T.zt)
+
+    wt("v", e_u, e_u0)
+    e_nu = ev(V.tensor_scalar(T.ut[:, 4:8], T.ut[:, 0:4], -1.0, None, A.mult))
+    wt("v", e_nu)
+    e_uq = ev(V.quantize_mx(T.uq[:], T.uqs[:], T.ut[:]))
+    wt("g", e_uq)
+    r_u = send2(prv, [(u8(T.ul[:, 0:2]), u8(T.uq[:, 0:2])), (T.uls[:, 0:8], T.uqs[:, 0:8])], "ru")
+    e_kz = zero(T.kt, T.jt)
+
+    e_t = []
+    for i in range(2):
+        wt("v", e_x[i])
+        e_t.append(ev(V.quantize_mx(T.tq[:, 128 * i:128 * i + 128], T.tqs[:, 128 * i:128 * i + 128], T.xt[:, 512 * i:512 * i + 512])))
+    wt("g", *e_t)
+    k = send(nxt, T.aws[:, TC:TC + 256], T.tqs[:], "rt0")
+    g.sem_inc(T.sem.gate, 1)
+    k += send(nxt, u8(T.aw[:, TC:TC + 256]), u8(T.tq[:]), "rt0")
+    r_t0 = ("rt0", k)
+    wt("s", ("gate", 1))
+    e_v += [load_v(1, 2), load_v(2, 4)]
+    e_i6 = ev(g.iota(T.i16[:], [[0, 8], [1, 16]], 0, 0, allow_small_or_imprecise_dtypes=True))
+    e_pc = ev(g.iota(T.pc[:], [[1, 1]], 0, 1))
+    e_rm = ev(g.iota(T.rm[:], [[1, 128]], 0, 0, allow_small_or_imprecise_dtypes=True))
+
+    wt("v", e_id, e_zz)
+    e_zc = ev(V.tensor_copy(T.zt[:, 4:516:4], T.idn[:]))
+    wt("v", e_xz)
+    e_xc = evs(*[V.memset(b[0:2, 4 * XC + 2:4 * XC + 64:4], 1.0) for b in (T.x1b, T.x2b)])
+    wt("v", e_ii)
+    e_ij = ev(V.tensor_scalar(T.ij[:], T.ii[:], 15, None, A.bitwise_and))
+    wt("v", e_zc)
+    e_e = [ev(V.quantize_mx(T.eq[:, 128 * b:128 * b + 128], T.eqs[:, 128 * b:128 * b + 128], T.zt[:, 4 - b:516 - b])) for b in range(4)]
+    wt("v", e_16, e_xc)
+    e_xc = evs(*[V.tensor_copy(b[0:1, 4 * XC + 2:4 * XC + 64:4], T.x16[0:1, :]) for b in (T.x1b, T.x2b)])
+    wt("v", e_ij, e_kz)
+    e_k = evs(*[V.tensor_scalar(T.kt[:, t:512:4], T.ij[:], 0.0, 256.0, A.is_equal, A.mult) for t in range(2)])
+    wt("v", e_i6)
+    e_k6 = ev(V.tensor_copy(T.kt[0:2, 2:512:4], T.i16[0:2, :]))
+    wt("v", e_k6)
+    ev(V.memset(T.kt[0:1, 2:512:4], 1.0), 1, e_k)
+    wt("v", e_k)
+    e_kq = ev(V.quantize_mx(T.kq[:], T.kqs[:], T.kt[:]))
+
+    def quant_v(k, i, j):
+        wt("v", e_v[k])
+        return ev(V.quantize_mx(T.vq[:, 128 * i:128 * j], T.vqs[:, 128 * i:128 * j], T.vt[:, 512 * i:512 * j]))
+
+    e_vq = [quant_v(0, 0, 1)]
+
+    wt("v", r_u, e_zo)
+    wt("a", r_u, e_zo)
+    e_ub = evs(V.tensor_copy(u32(T.ub[:]), u32(T.ul[:, 0:2]).indirect(T.zo[:, 0:8])),
+               S.activation(T.ubs[:], T.uls[:, 0:2].indirect(T.zo[:, 0:8]), AF.Copy))
+    e_nb = evs(V.tensor_copy(u32(T.nb[:]), u32(T.ul[:, 0:2]).indirect(T.oo[:, 0:16])),
+               S.activation(T.nbs[:], T.uls[:, 0:2].indirect(T.oo[:, 0:16]), AF.Copy))
+
+    def ranking(q, qs, ready, free, gb, sc, xb, xq, xqs):
+        wt("t", *ready)
+        e_r = []
+        for h in range(2):
+            wt("t", free[h], e_ub)
+            o = T.pr[:, 512 * h:512 * h + 256]
+            P.matmul_mx(o, T.ub[:], T.ubs[:], q[:], qs[:], True, False)
+            wt("t", e_nb)
+            e_r.append(ev(P.matmul_mx(o, q[:, 128 * h:128 * h + 128], qs[:, 128 * h:128 * h + 128], T.nb[:], T.nbs[:], False, True)))
+        wt("v", e_tb1, e_tb2)
+        e_c = []
+        for h in range(2):
+            wt("v", e_r[h])
+            e_c.append(ev(V.tensor_tensor(gb[:, 256 * h:256 * h + 256], T.pr[:, 512 * h:512 * h + 256],
+                                          T.tb[:, 128 - 128 * h:384 - 128 * h], A.is_gt)))
+        e_s = []
+        for h in range(2):
+            wt("v", e_c[h])
+            e_s.append(ev(V.tensor_tensor_scan(sc[:, 128 * h:128 * h + 128], gb[:, 256 * h:256 * h + 128],
+                                               gb[:, 256 * h + 128:256 * h + 256], 0.0, A.add, A.add)))
+        wt("v", e_cx, e_xc)
+        e_f = None
+        for h in range(2):
+            wt("v", e_s[h])
+            e_f = ev(V.tensor_scalar(xb[:, 4 * XC + h:4 * XC + 64:4], T.cx[:, 8 - 8 * h:24 - 8 * h],
+                                     sc[:, 128 * h + 127:128 * h + 128], None, A.is_gt), 1, e_f)
+        wt("v", e_f)
+        return ev(V.quantize_mx(xq[:], xqs[:], xb[:])), e_c, e_s
+
+    def send_flags(w, ws, xq, xqs, sem):
+        return send2(nxt, [(u8(w[:, XC:XC + 16]), u8(xq[:, XC:XC + 16])), (ws[:, 0:64], xqs[:, 0:64])], sem)
+
+    e_x1, e_c1, e_s1 = ranking(T.tq, T.tqs, e_t, (None, None), T.g1, T.sc1, T.x1b, T.x1q, T.x1qs)
+    wt("g", e_x1)
+    r_x1 = send_flags(T.aw, T.aws, T.x1q, T.x1qs, "rx1")
+    e_vq += [quant_v(1, 1, 2), quant_v(2, 2, 4)]
+
+    def make(w, ws, arrived, rl, nb, free, between=None):
+        e_a, e_r = [], []
+        wt("t", arrived)
+        for i in range(4):
+            b = 1024 * (i % 2)
+            wt("t", e_vq[min(i, 2)], *(free[i] if i < 2 else (e_r[i - 2], e_a[i - 2])))
+            e_1 = ev(P.matmul_mx(T.pm[:, b:b + 256], T.vq[:, 128 * i:128 * i + 128], T.vqs[:, 128 * i:128 * i + 128],
+                                 w[:, TC:TC + 256], ws[:, TC:TC + 256], True, True))
+            wt("t", e_e[i])
+            e_2 = ev(P.matmul_mx(T.pm[:, b + 512:b + 768], T.eq[:, 128 * i:128 * i + 128], T.eqs[:, 128 * i:128 * i + 128],
+                                 w[:, TC:TC + 256], ws[:, TC:TC + 256], True, True))
+            wt("a", e_1)
+            e_r.append(ev(S.activation(rl[:, 256 * i:256 * i + 256], T.pm[:, b:b + 256], AF.Relu, scale=0.05)))
+            wt("v", e_2, e_r[i])
+            e_a.append(ev(V.tensor_tensor(nb[:, i:1024:4], T.pm[:, b + 512:b + 768], rl[:, 256 * i:256 * i + 256], A.add)))
+            if i == 1 and between is not None:
+                between()
+        wt("v", *e_a)
+        e_n = ev(V.quantize_mx(w[:, TC + 256:TC + 512], ws[:, TC + 256:TC + 512], nb[:]))
+        return e_n, [(e_r[2], e_a[2]), (e_r[3], e_a[3])]
+
+    def choose(w, ws, e_n, r_x, off, t, ts, free):
+        wt("t", r_x, e_kq, free)
+        e_o = ev(P.matmul_mx(T.po[:, 0:128], T.kq[:], T.kqs[:], w[:, XC:XC + 128], ws[:, XC:XC + 128], True, True))
+        wt("v", e_o)
+        e_of = ev(V.tensor_copy(off[:], T.po[:, 0:16]))
+        wt("v", e_of, e_n)
+        wt("a", e_of, e_n)
+        e_c = ev(V.tensor_copy(u32(t[:]), u32(w[:, TC:TC + 512]).indirect(off[:, 0:16])))
+        e_p = ev(S.activation(ts[:], ws[:, TC:TC + 512].indirect(off[:, 0:16]), AF.Copy))
+        return [e_c, e_p], e_of
+
+    e_n1, fr = make(T.aw, T.aws, r_t0, T.rl1, T.n1b, [(), ()])
+    e_t1, e_o1 = choose(T.aw, T.aws, e_n1, r_x1, T.off1, T.t1, T.t1s, None)
+    wt("g", e_t1[0])
+    k = send(nxt, u8(T.bw[:, TC:TC + 256]), u8(T.t1[:]), "rt1")
+    wt("g", e_t1[1])
+    k += send(nxt, T.bws[:, TC:TC + 256], T.t1s[:], "rt1")
+    r_t1 = ("rt1", k)
+
+    g.sem_inc(T.sem.gate2, 1)
+    wt("s", ("gate2", 1))
+    e_w = ev(Y.dma_start(T.wt[:], T.w[:]), 16)
+
+    e_x2, e_c2, e_s2 = ranking(T.t1, T.t1s, e_t1, e_c1, T.g2, T.sc2, T.x2b, T.x2q, T.x2qs)
+    wt("g", e_x2)
+    r_x2 = send_flags(T.bw, T.bws, T.x2q, T.x2qs, "rx2")
+
+    wt("v", e_pc, e_kz)
+    e_pl = ev(V.tensor_scalar(T.pl[:], T.pc[:], 15, None, A.bitwise_and))
+    e_hz = zero(T.oh1, T.oh2)
+    wt("v", e_pl)
+    e_j = evs(V.tensor_copy(T.jt[:, 0:1], T.pl[:]), V.tensor_copy(T.jt[:, 1:2], T.pl[:]),
+              V.tensor_tensor(T.jt[:, 4:5], T.pc[:], T.pl[:], A.subtract))
+    wt("v", e_rm, e_hz, *e_s1)
+    e_h1 = evs(*[V.tensor_scalar(T.oh1[:, h:512:4], T.rm[:], T.sc1[:, 128 * h + 127:128 * h + 128], None, A.is_equal) for h in range(2)])
+    wt("v", e_j)
+    e_j = ev(V.tensor_scalar(T.jt[:, 5:6], T.jt[:, 4:5], 128.0, None, A.add))
+    wt("v", *e_s2)
+    e_h2 = evs(*[V.tensor_scalar(T.oh2[:, h:512:4], T.rm[:], T.sc2[:, 128 * h + 127:128 * h + 128], None, A.is_equal) for h in range(2)])
+    wt("v", e_j)
+    e_jq = ev(V.quantize_mx(T.jq[:], T.jqs[:], T.jt[:]))
+    wt("v", e_h1)
+    e_h1 = ev(V.quantize_mx(T.oh1q[:], T.oh1qs[:], T.oh1[:]))
+    wt("v", e_h2)
+    e_h2 = ev(V.quantize_mx(T.oh2q[:], T.oh2qs[:], T.oh2[:]))
+    wt("t", e_jq, e_h1)
+    e_p1 = ev(P.matmul_mx(T.pp[:, 0:128], T.oh1q[:], T.oh1qs[:], T.jq[:], T.jqs[:], True, True))
+    wt("v", e_p1)
+    e_l1 = ev(V.tensor_reduce(T.pl1[:], T.pp[:, 0:2], AxisListType.X, A.add))
+    wt("t", e_h2, e_l1)
+    e_p2 = ev(P.matmul_mx(T.pp[:, 0:128], T.oh2q[:], T.oh2qs[:], T.jq[:], T.jqs[:], True, True))
+    wt("v", e_p2)
+    e_l2 = ev(V.tensor_reduce(T.pl2[:], T.pp[:, 0:2], AxisListType.X, A.add))
+    wt("g", e_l1)
+    r_l1 = ("rl1", send(nx2, T.ll1[:], T.pl1[:], "rl1"))
+    wt("g", e_l2)
+    r_l2 = ("rl2", send(nxt, T.ll2[:], T.pl2[:], "rl2"))
+
+    e_wq = []
+
+    def quant_w():
+        wt("v", e_w)
+        e_wq.append(ev(V.quantize_mx(T.wq[:], T.wqs[:], T.wt[:])))
+
+    e_n2, fr = make(T.bw, T.bws, r_t1, T.rl2, T.n2b, fr, quant_w)
+    e_t2, e_o2 = choose(T.bw, T.bws, e_n2, r_x2, T.off2, T.t2, T.t2s, e_o1)
+
+    wt("s", e_t2[0])
+    e_out = ev(Y.dma_start(T.oc[:], u8(T.t2[:])), 16)
+    e_y = []
+    wt("t", *e_wq, *e_t2)
+    for h in range(2):
+        wt("t", e_c2[h])
+        e_y.append(ev(P.matmul_mx(T.pr[:, 512 * h:512 * h + 128], T.wq[:], T.wqs[:], T.t2[:, 128 * h:128 * h + 128],
+                                  T.t2s[:, 128 * h:128 * h + 128], True, True)))
+    wt("v", e_y[0])
+    e_z0 = ev(V.tensor_copy(T.yt[:, 0:128], T.pr[:, 0:128]))
+    wt("a", e_y[1])
+    e_z1 = ev(S.activation(T.yt[:, 128:256], T.pr[:, 512:640], AF.Copy))
+    wt("s", e_t2[1])
+    for q in range(4):
+        ev(Y.dma_start(T.osc[4 * q:4 * q + 4, :], T.t2s[32 * q:32 * q + 4, :]), 16, e_out)
+    wt("s", e_z0)
+    ev(Y.dma_start(T.y[:, 0:128], T.yt[:, 0:128]), 16, e_out)
+    wt("a", e_z1)
+    ev(S.dma_start(T.y[:, 128:256], T.yt[:, 128:256]), 16, e_out)
+    wt("a", r_l1)
+    ev(S.dma_start(T.li[0:1, :], T.ll1[0:64, 0:1]), 16, e_out)
+    wt("a", r_l2)
+    ev(S.dma_start(T.li[1:2, :], T.ll2[0:64, 0:1]), 16, e_out)
+
+    done = {e for (_, e) in known}
+    wt("s", *[e for e in made if e[0] not in done])
+    g.wait_ge(T.sem.lo, nloc[0])

@@ -1,13 +1,13 @@
 from concourse.bass import DstId, RemoteDMATransfer
-from concourse.mybir import dt, AluOpType, AxisListType, ActivationFunctionType
+from concourse.mybir import dt, AluOpType, ActivationFunctionType
 
 A = AluOpType
 AF = ActivationFunctionType
 F8, U8, BF, F32, I32, U16 = "float8_e4m3fn_x4", "uint8", "bfloat16", "float32", "int32", "uint16"
 EPS = 2.0 ** -110
-XC = 48
-TC = 64
-W2 = 576
+CM, CT, CX, CN, WW = 192, 256, 512, 640, 896
+CP = 192
+C2 = 176
 
 SCRATCH = {}
 
@@ -17,23 +17,23 @@ def _pair(n, w):
     SCRATCH[n + "s"] = ("sbuf", [128, w], U8)
 
 
-for _n, _w in (("uq", 128), ("vq", 512), ("wq", 128), ("eq", 512), ("kq", 128), ("jq", 128), ("tq", 256), ("ul", 8),
-               ("ub", 128), ("nb", 256), ("aw", W2), ("bw", W2), ("x1q", 128), ("x2q", 128), ("t1", 256), ("t2", 256),
-               ("oh1q", 128), ("oh2q", 128)):
+for _n, _w in (("uq", 128), ("ul", 8), ("un1", 256), ("un2", 256), ("vq", 512), ("wq", 128), ("eq", 576), ("pw", 384),
+               ("mq", 256), ("tq", 256), ("ww", WW), ("ohq", 128), ("flq", 128), ("t1", 256), ("t2", 256)):
     _pair(_n, _w)
-for _n, _w, _d in (("xt", 1024, BF), ("ut", 512, BF), ("vt", 2048, BF), ("wt", 512, BF), ("zt", 520, BF), ("idn", 128, BF),
-                   ("kt", 512, BF), ("jt", 512, BF), ("x1b", 512, BF), ("x2b", 512, BF), ("oh1", 512, BF), ("oh2", 512, BF),
-                   ("rl1", 1024, F32), ("rl2", 1024, F32), ("n1b", 1024, BF), ("n2b", 1024, BF), ("g1", 512, BF), ("g2", 512, BF),
-                   ("sc1", 256, BF), ("sc2", 256, BF), ("tb", 384, F32), ("cx", 24, F32), ("x16", 16, F32), ("i16", 128, F32),
-                   ("rm", 128, F32), ("ii", 128, I32), ("ij", 128, I32), ("pc", 1, I32), ("pl", 1, I32), ("zo", 16, U16),
-                   ("oo", 16, U16), ("off1", 16, U16), ("off2", 16, U16), ("pl1", 1, F32), ("pl2", 1, F32), ("ll1", 1, F32),
-                   ("ll2", 1, F32), ("yt", 256, F32)):
+for _n, _w, _d in (("xt", 1024, BF), ("ut", 512, BF), ("vt", 2048, BF), ("wt", 512, BF), ("zt", 520, BF), ("kt", 512, BF),
+                   ("jt", 512, BF), ("oh", 512, BF), ("fl", 512, BF), ("nm", 512, BF), ("n0", 1024, BF), ("tb", 128, BF),
+                   ("mk", 128, BF), ("aa", 256, BF), ("mp", 128, BF), ("c2", 2 * C2, BF), ("g1", 256, BF), ("g2", 256, BF),
+                   ("sc1", 256, BF), ("sc2", 256, BF), ("jk1", 256, BF), ("jk2", 256, BF), ("sg1", 2, F32), ("sg2", 2, F32),
+                   ("r1", 256, F32), ("r2", 256, F32), ("r0", 1024, F32), ("ii", 128, I32), ("ij", 128, I32),
+                   ("pc", 1, I32), ("pl", 1, I32), ("hl", 4, F32), ("zo", 16, U16), ("sl", 64, F32), ("l1", 4, U16),
+                   ("ll", 4, U16), ("lf", 4, F32), ("jr", 256, F32), ("vl", 64, F32), ("so", 256, F32), ("o1f", 16, F32),
+                   ("o1", 16, U16), ("o2f", 16, F32), ("o2", 16, U16), ("la", 64, F32), ("lb", 64, F32), ("yt", 256, F32)):
     SCRATCH[_n] = ("sbuf", [128, _w], _d)
-for _n, _w in (("pr", 1024), ("pm", 2048), ("po", 512), ("pp", 512)):
+for _n, _w in (("pr", 2048), ("pm", 2048)):
     SCRATCH[_n] = ("psum", [128, _w], F32)
 
-NEV = 130
-SEMAPHORES = ["s%d" % _i for _i in range(NEV)] + ["lo", "ru", "rt0", "rx1", "rl1", "rt1", "rx2", "rl2", "gate", "gate2"]
+NEV = 140
+SEMAPHORES = ["s%d" % _i for _i in range(NEV)] + ["lo", "lu", "lp", "ru", "rt", "rp", "rl", "rm"]
 
 
 def rank_program(g, core, T, topo):
@@ -66,31 +66,22 @@ def rank_program(g, core, T, topo):
                 known[(q, e[0])] = 1
                 Q[q].wait_ge(T.sem[e[0]], e[1])
 
-    def zero(*bufs):
-        return evs(*[V.memset(b[:], 0.0) for b in bufs])
-
     def bits(es):
         m = 0
         for e in es:
             m |= 1 << e
         return m
 
-    def send(dst, out, in_, sem):
-        rid, pid, _ = topo.addr(dst)
-        g.remote_dma(out, in_, T.sem[sem], T.sem.lo, pid, rid, topo.mask(core, dst))
-        k = len(topo.engines(core, dst))
-        nloc[0] += k
-        return k
-
-    def send2(dst, pairs, sem):
+    def send(dst, pairs, sem, loc="lo"):
         rid, pid, _ = topo.addr(dst)
         es = topo.engines(core, dst)
-        h = len(es) // 2
+        h = len(es) // len(pairs)
         g.remote_dma_fused([RemoteDMATransfer(dst_ids=[DstId(rid=rid, pnc=pid)], dma_engine_mask=bits(es[i * h:i * h + h]),
                                               remote_sem=T.sem[sem], srcs=[s], dsts=[d], alu_op=0)
-                            for i, (d, s) in enumerate(pairs)], local_sem=T.sem.lo)
-        nloc[0] += 2 * h
-        return (sem, 2 * h)
+                            for i, (d, s) in enumerate(pairs)], local_sem=T.sem[loc])
+        if loc == "lo":
+            nloc[0] += len(pairs) * h
+        return len(pairs) * h
 
     def u8(v):
         return v.bitcast(dt.uint8)
@@ -98,235 +89,291 @@ def rank_program(g, core, T, topo):
     def u32(v):
         return v.bitcast(dt.uint32)
 
-    def load_v(i, j):
-        return ev(Y.dma_start(T.vt[:, 512 * i:512 * j], T.v[:, 512 * i:512 * j]), 16)
+    def pair(name, a, b):
+        return T[name][:, a:b], T[name + "s"][:, a:b]
+
+    def quant(dst, src):
+        return ev(V.quantize_mx(dst[0], dst[1], src))
+
+    def mm(out, lhs, rhs, start=True, stop=True):
+        return P.matmul_mx(out, lhs[0], lhs[1], rhs[0], rhs[1], start, stop)
+
+    def pick_c(dst, win, off):
+        return V.tensor_copy(u32(dst[0]), u32(win[0]).indirect(off))
+
+    def pick_s(dst, win, off):
+        return S.activation(dst[1], win[1].indirect(off), AF.Copy)
 
     e_u = ev(S.dma_start(T.ut[:, 0:4], T.u[:, 0:4]), 16)
     e_x = [ev(Y.dma_start(T.xt[:, 512 * i:512 * i + 512], T.x[:, 512 * i:512 * i + 512]), 16) for i in range(2)]
-    e_v = [load_v(0, 1)]
 
-    e_tb0 = evs(V.memset(T.tb[:, 128:384], 0.0))
-    e_cx = evs(V.memset(T.cx[:], 64.0))
-    e_id = evs(V.memset(T.idn[:], 1.0))
-    e_tb1 = evs(V.memset(T.tb[:, 0:128], -EPS))
-    e_u0 = evs(V.memset(T.ut[:, 8:512], 0.0))
-    e_zo = evs(V.memset(T.zo[:], 0), V.memset(T.oo[:], 1))
-    wt("g", e_tb0)
-    e_tb2 = ev(g.affine_select(T.tb[:, 128:256], T.tb[:, 128:256], [[1, 128]], A.is_ge, -EPS, 0, -1))
-    wt("g", e_cx)
-    e_cx = ev(g.affine_select(T.cx[:], T.cx[:], [[-16, 24]], A.is_ge, -1.0, 128, 1))
-    wt("g", e_cx)
-    e_cx = ev(g.affine_select(T.cx[:], T.cx[:], [[16, 24]], A.is_ge, -1.0, 15 - 128, -1))
-    e_16 = ev(g.iota(T.x16[:], [[16, 16]], 0, 0, allow_small_or_imprecise_dtypes=True))
-    wt("g", e_id)
-    e_id = ev(g.affine_select(T.idn[:], T.idn[:], [[1, 128]], A.is_equal, 0.0, 0, -1))
     e_ii = ev(g.iota(T.ii[:], [[1, 128]], 128, -1))
-    e_xz = zero(T.x1b, T.x2b)
-    e_zz = zero(T.zt)
+    e_pc = ev(g.iota(T.pc[:], [[1, 1]], 0, 1))
+    e_mp = ev(g.iota(T.mp[:], [[2, 4], [8, 16], [0, 2]], -128, 0, allow_small_or_imprecise_dtypes=True))
+
+    e_u0 = ev(V.memset(T.ut[:, 8:512], 0.0))
+    e_zo = evs(V.memset(T.zo[:, 0:8], 0), V.memset(T.zo[:, 8:16], 1))
+    e_z = evs(V.memset(T.oh[:, 256:512], 0.0), V.memset(T.zt[:], 0.0))
+    wt("v", e_ii, e_pc)
+    e_i = evs(V.tensor_scalar(T.ij[:], T.ii[:], 15, None, A.bitwise_and),
+              V.tensor_scalar(T.pl[:], T.pc[:], 15, None, A.bitwise_and))
 
     wt("v", e_u, e_u0)
     e_nu = ev(V.tensor_scalar(T.ut[:, 4:8], T.ut[:, 0:4], -1.0, None, A.mult))
     wt("v", e_nu)
-    e_uq = ev(V.quantize_mx(T.uq[:], T.uqs[:], T.ut[:]))
+    e_uq = quant(pair("uq", 0, 128), T.ut[:])
     wt("g", e_uq)
-    r_u = send2(prv, [(u8(T.ul[:, 0:2]), u8(T.uq[:, 0:2])), (T.uls[:, 0:8], T.uqs[:, 0:8])], "ru")
-    e_kz = zero(T.kt, T.jt)
+    r_u = ("ru", send(prv, [(u8(T.ul[:, 0:2]), u8(T.uq[:, 0:2])), (T.uls[:, 0:8], T.uqs[:, 0:8])], "ru", "lu"))
+    l_u = ("lu", r_u[1])
+
+    wt("v", e_i)
+    e_h = evs(V.tensor_copy(T.hl[:, 0:1], T.pl[:]), V.tensor_tensor(T.hl[:, 1:2], T.pc[:], T.pl[:], A.subtract))
+    e_mk = ev(V.tensor_scalar(T.mk[:], T.ij[:], 0.0, None, A.is_equal))
+    e_tb = ev(V.tensor_scalar(T.tb[:], T.ii[:], 128.0, -EPS, A.is_lt, A.mult))
 
     e_t = []
     for i in range(2):
         wt("v", e_x[i])
-        e_t.append(ev(V.quantize_mx(T.tq[:, 128 * i:128 * i + 128], T.tqs[:, 128 * i:128 * i + 128], T.xt[:, 512 * i:512 * i + 512])))
+        e_t.append(quant(pair("tq", 128 * i, 128 * i + 128), T.xt[:, 512 * i:512 * i + 512]))
     wt("g", *e_t)
-    k = send(nxt, T.aws[:, TC:TC + 256], T.tqs[:], "rt0")
-    g.sem_inc(T.sem.gate, 1)
-    k += send(nxt, u8(T.aw[:, TC:TC + 256]), u8(T.tq[:]), "rt0")
-    r_t0 = ("rt0", k)
-    wt("s", ("gate", 1))
-    e_v += [load_v(1, 2), load_v(2, 4)]
-    e_i6 = ev(g.iota(T.i16[:], [[0, 8], [1, 16]], 0, 0, allow_small_or_imprecise_dtypes=True))
-    e_pc = ev(g.iota(T.pc[:], [[1, 1]], 0, 1))
-    e_rm = ev(g.iota(T.rm[:], [[1, 128]], 0, 0, allow_small_or_imprecise_dtypes=True))
+    k = send(nx2, [(u8(T.ww[:, CT:CT + 256]), u8(T.tq[:]))], "rt")
+    k += send(nx2, [(T.wws[:, CT:CT + 256], T.tqs[:])], "rt")
+    r_t = ("rt", k)
+    wt("s", l_u)
+    e_v = [ev(Y.dma_start(T.vt[:, 1024 * i:1024 * i + 1024], T.v[:, 1024 * i:1024 * i + 1024]), 16) for i in range(2)]
 
-    wt("v", e_id, e_zz)
-    e_zc = ev(V.tensor_copy(T.zt[:, 4:516:4], T.idn[:]))
-    wt("v", e_xz)
-    e_xc = evs(*[V.memset(b[0:2, 4 * XC + 2:4 * XC + 64:4], 1.0) for b in (T.x1b, T.x2b)])
-    wt("v", e_ii)
-    e_ij = ev(V.tensor_scalar(T.ij[:], T.ii[:], 15, None, A.bitwise_and))
+    zeros = T.oh[:, 256:384]
+    wt("v", e_h, e_z, e_mk)
+    wt("a", e_h, e_z)
+    e_j = evs(S.activation(T.jt[:, 0:512:4], zeros, AF.Identity, bias=T.hl[:, 1:2]),
+              S.activation(T.jt[:, 2:512:4], zeros, AF.Identity, bias=T.hl[:, 0:1]),
+              S.activation(T.jt[:, 3:512:4], zeros, AF.Identity, bias=T.hl[:, 0:1]),
+              V.tensor_scalar(T.jt[:, 1:512:4], zeros, T.hl[:, 1:2], 128.0, A.add, A.add))
+    e_a = evs(V.tensor_scalar(T.hl[:, 2:3], T.hl[:, 0:1], -1024.0, 15360.0, A.mult, A.add),
+              *[V.tensor_scalar(T.aa[:, 128 * h:128 * h + 128], T.mk[:], 66560.0, -1024.0, A.mult, A.add) for h in range(2)])
+    e_zc = ev(V.tensor_scalar(T.zt[:, 4:516:4], T.ii[:], 128.0, None, A.is_equal))
+    e_k = ev(V.memset(T.kt[:], 0.0))
+    e_c2 = ev(V.memset(T.c2[:], -1.0))
+    e_z2 = evs(V.memset(T.nm[:, 0:256], 0.0), V.memset(T.fl[:, 324:512], 0.0))
+    wt("v", e_j)
+    e_jq = quant(pair("mq", 0, 128), T.jt[:])
     wt("v", e_zc)
-    e_e = [ev(V.quantize_mx(T.eq[:, 128 * b:128 * b + 128], T.eqs[:, 128 * b:128 * b + 128], T.zt[:, 4 - b:516 - b])) for b in range(4)]
-    wt("v", e_16, e_xc)
-    e_xc = evs(*[V.tensor_copy(b[0:1, 4 * XC + 2:4 * XC + 64:4], T.x16[0:1, :]) for b in (T.x1b, T.x2b)])
-    wt("v", e_ij, e_kz)
-    e_k = evs(*[V.tensor_scalar(T.kt[:, t:512:4], T.ij[:], 0.0, 256.0, A.is_equal, A.mult) for t in range(2)])
-    wt("v", e_i6)
-    e_k6 = ev(V.tensor_copy(T.kt[0:2, 2:512:4], T.i16[0:2, :]))
-    wt("v", e_k6)
-    ev(V.memset(T.kt[0:1, 2:512:4], 1.0), 1, e_k)
+    e_e = evs(*[V.quantize_mx(T.eq[:, 128 * b:128 * b + 128], T.eqs[:, 128 * b:128 * b + 128], T.zt[:, 4 - b:516 - b])
+                for b in range(4)])
     wt("v", e_k)
-    e_kq = ev(V.quantize_mx(T.kq[:], T.kqs[:], T.kt[:]))
+    e_k = evs(*[V.tensor_scalar(T.kt[:, t:512:4], T.mk[:], 384.0, None, A.mult) for t in range(2)])
+    wt("v", e_zo)
+    wt("a", e_zo, e_uq)
+    wt("v", e_uq)
+    e_n2 = evs(pick_c(pair("un2", 0, 256), pair("uq", 0, 2), T.zo[:]), pick_s(pair("un2", 0, 256), pair("uq", 0, 2), T.zo[:]))
+    wt("v", e_k)
+    e_kq = quant(pair("pw", 256, 384), T.kt[:])
 
-    def quant_v(k, i, j):
-        wt("v", e_v[k])
-        return ev(V.quantize_mx(T.vq[:, 128 * i:128 * j], T.vqs[:, 128 * i:128 * j], T.vt[:, 512 * i:512 * j]))
+    wt("g", e_c2)
+    e_c = [ev(g.affine_select(T.c2[:, C2 * h:C2 * h + 32], T.c2[:, C2 * h:C2 * h + 32], [[-16, 16], [0, 2]], A.is_ge, -256.0,
+                              128 * h, 1)) for h in range(2)]
+    e_c2 = evs(*[g.iota(T.c2[:, C2 * h + 32:C2 * h + 162], [[2, 65], [0, 2]], -129, 0, allow_small_or_imprecise_dtypes=True)
+                 for h in range(2)])
+    for h in range(2):
+        wt("g", e_c[h])
+        ev(g.affine_select(T.c2[:, C2 * h:C2 * h + 32], T.c2[:, C2 * h:C2 * h + 32], [[16, 16], [0, 2]], A.is_ge, -256.0,
+                           15 - 128 * h, -1), 1, e_c2)
+    e_jr = evs(g.iota(T.jr[:], [[1, 256]], 64, 0, allow_small_or_imprecise_dtypes=True),
+               g.iota(T.vl[:], [[1, 64]], 0, 0, allow_small_or_imprecise_dtypes=True))
 
-    e_vq = [quant_v(0, 0, 1)]
+    BLK = ((0, 0), (0, 1), (1, 1), (1, 0))
 
-    wt("v", r_u, e_zo)
-    wt("a", r_u, e_zo)
-    e_ub = evs(V.tensor_copy(u32(T.ub[:]), u32(T.ul[:, 0:2]).indirect(T.zo[:, 0:8])),
-               S.activation(T.ubs[:], T.uls[:, 0:2].indirect(T.zo[:, 0:8]), AF.Copy))
-    e_nb = evs(V.tensor_copy(u32(T.nb[:]), u32(T.ul[:, 0:2]).indirect(T.oo[:, 0:16])),
-               S.activation(T.nbs[:], T.uls[:, 0:2].indirect(T.oo[:, 0:16]), AF.Copy))
+    def bank(i, a=0, b=128):
+        return T.pr[:, 512 * i + a:512 * i + b]
 
-    def ranking(q, qs, ready, free, gb, sc, xb, xq, xqs):
-        wt("t", *ready)
-        e_r = []
-        for h in range(2):
-            wt("t", free[h], e_ub)
-            o = T.pr[:, 512 * h:512 * h + 256]
-            P.matmul_mx(o, T.ub[:], T.ubs[:], q[:], qs[:], True, False)
-            wt("t", e_nb)
-            e_r.append(ev(P.matmul_mx(o, q[:, 128 * h:128 * h + 128], qs[:, 128 * h:128 * h + 128], T.nb[:], T.nbs[:], False, True)))
-        wt("v", e_tb1, e_tb2)
-        e_c = []
-        for h in range(2):
-            wt("v", e_r[h])
-            e_c.append(ev(V.tensor_tensor(gb[:, 256 * h:256 * h + 256], T.pr[:, 512 * h:512 * h + 256],
-                                          T.tb[:, 128 - 128 * h:384 - 128 * h], A.is_gt)))
-        e_s = []
-        for h in range(2):
-            wt("v", e_c[h])
-            e_s.append(ev(V.tensor_tensor_scan(sc[:, 128 * h:128 * h + 128], gb[:, 256 * h:256 * h + 128],
-                                               gb[:, 256 * h + 128:256 * h + 256], 0.0, A.add, A.add)))
-        wt("v", e_cx, e_xc)
-        e_f = None
-        for h in range(2):
-            wt("v", e_s[h])
-            e_f = ev(V.tensor_scalar(xb[:, 4 * XC + h:4 * XC + 64:4], T.cx[:, 8 - 8 * h:24 - 8 * h],
-                                     sc[:, 128 * h + 127:128 * h + 128], None, A.is_gt), 1, e_f)
-        wt("v", e_f)
-        return ev(V.quantize_mx(xq[:], xqs[:], xb[:])), e_c, e_s
+    def row(i, un, q):
+        mm(bank(i), pair(un, 0, 128), pair(q, 128 * BLK[i][1], 128 * BLK[i][1] + 128), True, False)
 
-    def send_flags(w, ws, xq, xqs, sem):
-        return send2(nxt, [(u8(w[:, XC:XC + 16]), u8(xq[:, XC:XC + 16])), (ws[:, 0:64], xqs[:, 0:64])], sem)
+    def col(i, un, q):
+        return ev(mm(bank(i), pair(q, 128 * BLK[i][0], 128 * BLK[i][0] + 128), pair(un, 128, 256), False, True))
 
-    e_x1, e_c1, e_s1 = ranking(T.tq, T.tqs, e_t, (None, None), T.g1, T.sc1, T.x1b, T.x1q, T.x1qs)
-    wt("g", e_x1)
-    r_x1 = send_flags(T.aw, T.aws, T.x1q, T.x1qs, "rx1")
-    e_vq += [quant_v(1, 1, 2), quant_v(2, 2, 4)]
+    def cmp_own(h, e, gb):
+        wt("v", e, e_tb)
+        return ev(V.tensor_tensor(gb[:, 128 * h:128 * h + 128], bank(2 * h), T.tb[:], A.is_gt))
 
-    def make(w, ws, arrived, rl, nb, free, between=None):
-        e_a, e_r = [], []
-        wt("t", arrived)
-        for i in range(4):
-            b = 1024 * (i % 2)
-            wt("t", e_vq[min(i, 2)], *(free[i] if i < 2 else (e_r[i - 2], e_a[i - 2])))
-            e_1 = ev(P.matmul_mx(T.pm[:, b:b + 256], T.vq[:, 128 * i:128 * i + 128], T.vqs[:, 128 * i:128 * i + 128],
-                                 w[:, TC:TC + 256], ws[:, TC:TC + 256], True, True))
-            wt("t", e_e[i])
-            e_2 = ev(P.matmul_mx(T.pm[:, b + 512:b + 768], T.eq[:, 128 * i:128 * i + 128], T.eqs[:, 128 * i:128 * i + 128],
-                                 w[:, TC:TC + 256], ws[:, TC:TC + 256], True, True))
-            wt("a", e_1)
-            e_r.append(ev(S.activation(rl[:, 256 * i:256 * i + 256], T.pm[:, b:b + 256], AF.Relu, scale=0.05)))
-            wt("v", e_2, e_r[i])
-            e_a.append(ev(V.tensor_tensor(nb[:, i:1024:4], T.pm[:, b + 512:b + 768], rl[:, 256 * i:256 * i + 256], A.add)))
-            if i == 1 and between is not None:
-                between()
-        wt("v", *e_a)
-        e_n = ev(V.quantize_mx(w[:, TC + 256:TC + 512], ws[:, TC + 256:TC + 512], nb[:]))
-        return e_n, [(e_r[2], e_a[2]), (e_r[3], e_a[3])]
+    def count_own(h, e, gb, sc, e_o, sg):
+        wt("v", e, e_o)
+        s = slice(128 * h, 128 * h + 128)
+        return ev(V.tensor_tensor_scan(sc[:, s], gb[:, s], gb[:, s], sg[:, h:h + 1], A.add, A.add))
 
-    def choose(w, ws, e_n, r_x, off, t, ts, free):
-        wt("t", r_x, e_kq, free)
-        e_o = ev(P.matmul_mx(T.po[:, 0:128], T.kq[:], T.kqs[:], w[:, XC:XC + 128], ws[:, XC:XC + 128], True, True))
-        wt("v", e_o)
-        e_of = ev(V.tensor_copy(off[:], T.po[:, 0:16]))
-        wt("v", e_of, e_n)
-        wt("a", e_of, e_n)
-        e_c = ev(V.tensor_copy(u32(t[:]), u32(w[:, TC:TC + 512]).indirect(off[:, 0:16])))
-        e_p = ev(S.activation(ts[:], ws[:, TC:TC + 512].indirect(off[:, 0:16]), AF.Copy))
-        return [e_c, e_p], e_of
+    def count_other(h, e, jk, sg):
+        wt("a", e)
+        return ev(S.activation(jk[:, 128 * h:128 * h + 128], bank(2 * h + 1), AF.Sign, bias=(EPS if h else -EPS),
+                               accum_out=sg[:, h:h + 1]))
 
-    e_n1, fr = make(T.aw, T.aws, r_t0, T.rl1, T.n1b, [(), ()])
-    e_t1, e_o1 = choose(T.aw, T.aws, e_n1, r_x1, T.off1, T.t1, T.t1s, None)
-    wt("g", e_t1[0])
-    k = send(nxt, u8(T.bw[:, TC:TC + 256]), u8(T.t1[:]), "rt1")
-    wt("g", e_t1[1])
-    k += send(nxt, T.bws[:, TC:TC + 256], T.t1s[:], "rt1")
-    r_t1 = ("rt1", k)
-
-    g.sem_inc(T.sem.gate2, 1)
-    wt("s", ("gate2", 1))
+    wt("v", r_u)
+    wt("a", r_u)
+    e_n = [evs(pick_c(pair("un1", 128 * i, 128 * i + 128), pair("ul", 0, 2), T.zo[:, 8 * i:8 * i + 8]),
+               pick_s(pair("un1", 128 * i, 128 * i + 128), pair("ul", 0, 2), T.zo[:, 8 * i:8 * i + 8])) for i in range(2)]
+    wt("t", e_n[0], *e_t)
+    for i in range(4):
+        row(i, "un1", "tq")
+    wt("t", e_n[1])
+    e_d = {i: col(i, "un1", "tq") for i in (1, 0, 3, 2)}
+    e_g0 = cmp_own(0, e_d[0], T.g1)
+    e_g1 = cmp_own(1, e_d[2], T.g1)
+    e_o = [count_other(h, e_d[2 * h + 1], T.jk1, T.sg1) for h in range(2)]
+    e_s = [count_own(0, e_g0, T.g1, T.sc1, e_o[0], T.sg1), count_own(1, e_g1, T.g1, T.sc1, e_o[1], T.sg1)]
+    wt("v", e_mp)
+    e_oh = None
+    for h in range(2):
+        wt("v", e_s[h])
+        e_oh = ev(V.tensor_scalar(T.oh[:, h:256:2], T.mp[:], T.sc1[:, 128 * h + 127:128 * h + 128], None, A.is_equal), 1, e_oh)
+    wt("v", e_oh)
+    e_ohq = quant(pair("ohq", 0, 128), T.oh[:])
+    wt("t", e_ohq, e_jq)
+    e_l = ev(mm(bank(0), pair("mq", 0, 128), pair("ohq", 0, 128)))
+    wt("v", e_l, e_a)
+    e_l = ev(V.tensor_tensor_scan(T.sl[:], T.aa[:, 0:64], bank(0, 0, 64), 0.0, A.add, A.min))
+    wt("v", e_l)
+    e_l = ev(V.tensor_scalar(T.l1[:], T.sl[:, 15:64:16], T.hl[:, 2:3], None, A.add))
+    wt("v", e_l)
+    wt("a", e_l)
+    e_p = evs(pick_c(pair("eq", 512, 576), pair("tq", 0, 256), T.l1[:]), pick_s(pair("eq", 512, 576), pair("tq", 0, 256), T.l1[:]))
+    wt("g", e_p, e_e)
+    r_p = ("rp", send(nxt, [(u8(T.pw[:, CP:CP + 64]), u8(T.eq[:, 512:576])), (T.pws[:, 0:256], T.eqs[:, 320:576])], "rp", "lp"))
+    r_l = ("rl", send(nx2, [(T.ll[:], T.l1[:])], "rl"))
+    wt("s", ("lp", r_p[1]))
     e_w = ev(Y.dma_start(T.wt[:], T.w[:]), 16)
 
-    e_x2, e_c2, e_s2 = ranking(T.t1, T.t1s, e_t1, e_c1, T.g2, T.sc2, T.x2b, T.x2q, T.x2qs)
-    wt("g", e_x2)
-    r_x2 = send_flags(T.bw, T.bws, T.x2q, T.x2qs, "rx2")
+    free = [[], []]
 
-    wt("v", e_pc, e_kz)
-    e_pl = ev(V.tensor_scalar(T.pl[:], T.pc[:], 15, None, A.bitwise_and))
-    e_hz = zero(T.oh1, T.oh2)
-    wt("v", e_pl)
-    e_j = evs(V.tensor_copy(T.jt[:, 0:1], T.pl[:]), V.tensor_copy(T.jt[:, 1:2], T.pl[:]),
-              V.tensor_tensor(T.jt[:, 4:5], T.pc[:], T.pl[:], A.subtract))
-    wt("v", e_rm, e_hz, *e_s1)
-    e_h1 = evs(*[V.tensor_scalar(T.oh1[:, h:512:4], T.rm[:], T.sc1[:, 128 * h + 127:128 * h + 128], None, A.is_equal) for h in range(2)])
-    wt("v", e_j)
-    e_j = ev(V.tensor_scalar(T.jt[:, 5:6], T.jt[:, 4:5], 128.0, None, A.add))
-    wt("v", *e_s2)
-    e_h2 = evs(*[V.tensor_scalar(T.oh2[:, h:512:4], T.rm[:], T.sc2[:, 128 * h + 127:128 * h + 128], None, A.is_equal) for h in range(2)])
-    wt("v", e_j)
-    e_jq = ev(V.quantize_mx(T.jq[:], T.jqs[:], T.jt[:]))
-    wt("v", e_h1)
-    e_h1 = ev(V.quantize_mx(T.oh1q[:], T.oh1qs[:], T.oh1[:]))
-    wt("v", e_h2)
-    e_h2 = ev(V.quantize_mx(T.oh2q[:], T.oh2qs[:], T.oh2[:]))
-    wt("t", e_jq, e_h1)
-    e_p1 = ev(P.matmul_mx(T.pp[:, 0:128], T.oh1q[:], T.oh1qs[:], T.jq[:], T.jqs[:], True, True))
-    wt("v", e_p1)
-    e_l1 = ev(V.tensor_reduce(T.pl1[:], T.pp[:, 0:2], AxisListType.X, A.add))
-    wt("t", e_h2, e_l1)
-    e_p2 = ev(P.matmul_mx(T.pp[:, 0:128], T.oh2q[:], T.oh2qs[:], T.jq[:], T.jqs[:], True, True))
-    wt("v", e_p2)
-    e_l2 = ev(V.tensor_reduce(T.pl2[:], T.pp[:, 0:2], AxisListType.X, A.add))
-    wt("g", e_l1)
-    r_l1 = ("rl1", send(nx2, T.ll1[:], T.pl1[:], "rl1"))
-    wt("g", e_l2)
-    r_l2 = ("rl2", send(nxt, T.ll2[:], T.pl2[:], "rl2"))
+    def prods(i, src, w):
+        b = 1024 * (i % 2)
+        wt("t", e_vq[i // 2], *free[i % 2])
+        e_1 = ev(mm(T.pm[:, b:b + w], pair("vq", 128 * i, 128 * i + 128), src))
+        wt("t", e_e)
+        e_2 = ev(mm(T.pm[:, b + 512:b + 512 + w], pair("eq", 128 * i, 128 * i + 128), src))
+        return e_1, e_2
 
-    e_wq = []
+    def relu(i, e, rl, w):
+        b = 1024 * (i % 2)
+        wt("a", e[0])
+        return ev(S.activation(rl[:, w * i:w * i + w], T.pm[:, b:b + w], AF.Relu, scale=0.05))
 
-    def quant_w():
-        wt("v", e_w)
-        e_wq.append(ev(V.quantize_mx(T.wq[:], T.wqs[:], T.wt[:])))
+    def add(i, e, e_r, rl, nb, w):
+        b = 1024 * (i % 2) + 512
+        z = 4 * max(w, 128)
+        wt("v", e[1], e_r)
+        e_s = ev(V.tensor_tensor(nb[:, z - 4 * w + i:z:4], T.pm[:, b:b + w], rl[:, w * i:w * i + w], A.add))
+        free[i % 2] = [e_s]
+        return e_s
 
-    e_n2, fr = make(T.bw, T.bws, r_t1, T.rl2, T.n2b, fr, quant_w)
-    e_t2, e_o2 = choose(T.bw, T.bws, e_n2, r_x2, T.off2, T.t2, T.t2s, e_o1)
+    def make(i, src, rl, nb, w):
+        e = prods(i, src, max(w, 128))
+        return add(i, e, relu(i, e, rl, w), rl, nb, w)
 
-    wt("s", e_t2[0])
-    e_out = ev(Y.dma_start(T.oc[:], u8(T.t2[:])), 16)
-    e_y = []
-    wt("t", *e_wq, *e_t2)
+    e_vq = []
+    for i in range(2):
+        wt("v", e_v[i])
+        e_vq.append(quant(pair("vq", 256 * i, 256 * i + 256), T.vt[:, 1024 * i:1024 * i + 1024]))
+
+    wt("t", r_t)
+    e_0 = [make(i, pair("ww", CT, CT + 256), T.r0, T.n0, 256) for i in range(1)]
+
+    wt("t", r_p, e_kq)
+    e_m = [make(i, pair("pw", CP, CP + 128), T.r1, T.nm, 64) for i in range(4)]
+    wt("v", e_z2, *e_m)
+    e_m = quant(pair("mq", 128, 256), T.nm[:])
+    wt("g", e_m, e_jq)
+    r_m = ("rm", send(nxt, [(u8(T.ww[:, CM:CM + 64]), u8(T.mq[:, 192:256])), (T.wws[:, 0:256], T.mqs[:])], "rm"))
+
+    wt("v", r_l, e_jr)
+    e_sc = ev(V.tensor_copy(T.jr[:].indirect(T.ll[:]), T.vl[:]))
+    e_lf = ev(V.tensor_copy(T.lf[0:16, :], T.ll[0:16, :]))
+    wt("s", e_lf)
+    e_out = ev(Y.dma_start(T.li[0:1, :], T.lf[0:16, :]), 16)
+    e_0.append(make(1, pair("ww", CT, CT + 256), T.r0, T.n0, 256))
+    wt("v", e_sc)
+    e_sc = ev(V.tensor_tensor_scan(T.so[:], T.aa[:], T.jr[:], 0.0, A.add, A.min))
+    e_0.append(make(2, pair("ww", CT, CT + 256), T.r0, T.n0, 256))
+    wt("v", e_sc)
+    e_o1 = evs(V.tensor_scalar(T.o1[:], T.so[:, 15:256:16], T.hl[:, 2:3], None, A.add),
+               V.tensor_scalar(T.o1f[:], T.so[:, 15:256:16], T.hl[:, 2:3], None, A.add))
+    e_0.append(make(3, pair("ww", CT, CT + 256), T.r0, T.n0, 256))
+    wt("v", *e_0)
+    e_0 = quant(pair("ww", CN, CN + 256), T.n0[:])
+    wt("v", e_w)
+    e_wq = quant(pair("wq", 0, 128), T.wt[:])
+
+    src = pair("ww", CM, CM + 128)
+    wt("t", r_m)
+    e_pr = [prods(i, src, 128) for i in range(2)]
+    wt("v", r_m, r_t, e_o1)
+    wt("a", r_m, r_t, e_o1)
+    e_t1 = [evs(pick_c(pair("t1", 128 * h, 128 * h + 128), pair("ww", CM, CX), T.o1[:, 8 * h:8 * h + 8]),
+                pick_s(pair("t1", 128 * h, 128 * h + 128), pair("ww", CM, CX), T.o1[:, 8 * h:8 * h + 8])) for h in range(2)]
+    e_d = {}
+    wt("t", e_n2, e_l)
+    for i in (0, 1, 3, 2):
+        wt("t", e_t1[min(i, 1)])
+        row(i, "un2", "t1")
+        e_d[i] = col(i, "un2", "t1")
+    e_r = [relu(i, e_pr[i], T.r2, 64) for i in range(2)]
+    wt("v", e_m)
+    e_x = [add(0, e_pr[0], e_r[0], T.r2, T.nm, 64)]
+    e_g0 = cmp_own(0, e_d[0], T.g2)
+    e_x.append(add(1, e_pr[1], e_r[1], T.r2, T.nm, 64))
+    e_pr += [prods(i, src, 128) for i in range(2, 4)]
+    e_o = [count_other(h, e_d[2 * h + 1], T.jk2, T.sg2) for h in range(2)]
+    e_s = [count_own(0, e_g0, T.g2, T.sc2, e_o[0], T.sg2)]
+    e_g1 = cmp_own(1, e_d[2], T.g2)
+    e_s.append(count_own(1, e_g1, T.g2, T.sc2, e_o[1], T.sg2))
+    e_r += [relu(i, e_pr[i], T.r2, 64) for i in range(2, 4)]
+    wt("v", e_c2)
+    e_f = None
     for h in range(2):
-        wt("t", e_c2[h])
-        e_y.append(ev(P.matmul_mx(T.pr[:, 512 * h:512 * h + 128], T.wq[:], T.wqs[:], T.t2[:, 128 * h:128 * h + 128],
-                                  T.t2s[:, 128 * h:128 * h + 128], True, True)))
+        wt("v", e_s[h])
+        e_f = ev(V.tensor_scalar(T.fl[:, h:324:2], T.c2[:, C2 * h:C2 * h + 162], T.sc2[:, 128 * h + 127:128 * h + 128],
+                                 None, A.is_gt), 1, e_f)
+    wt("v", e_f)
+    e_f = quant(pair("flq", 0, 128), T.fl[:])
+    wt("t", e_f, e_kq)
+    e_k = ev(mm(bank(0), pair("pw", 256, 384), pair("flq", 0, 128)))
+    e_j = ev(mm(bank(1), pair("mq", 0, 128), pair("flq", 0, 128)))
+    e_x += [add(i, e_pr[i], e_r[i], T.r2, T.nm, 64) for i in range(2, 4)]
+    wt("v", e_k)
+    e_k = ev(V.tensor_tensor(T.o2f[:], bank(0, 0, 16), T.o1f[:], A.add))
+    wt("v", *e_x)
+    e_x = quant(pair("ww", CX, CX + 128), T.nm[:])
+    wt("v", e_k)
+    e_k = ev(V.tensor_copy(T.o2[:], T.o2f[:]))
+    wt("a", e_j)
+    e_la = ev(S.activation(T.la[0:1, :], T.pr[0:1, 512 + 16:512 + 80], AF.Copy))
+    wt("v", e_k, e_x, e_0)
+    wt("a", e_k, e_x, e_0)
+    e_tc, e_ts = [], []
+    for h in range(2):
+        e_tc.append(ev(pick_c(pair("t2", 128 * h, 128 * h + 128), pair("ww", CM, WW), T.o2[:, 8 * h:8 * h + 8])))
+        e_ts.append(ev(pick_s(pair("t2", 128 * h, 128 * h + 128), pair("ww", CM, WW), T.o2[:, 8 * h:8 * h + 8])))
+
+    e_y = []
+    wt("t", e_wq)
+    for h in range(2):
+        wt("t", e_tc[h], e_ts[h])
+        e_y.append(ev(mm(bank(2 + h), pair("wq", 0, 128), pair("t2", 128 * h, 128 * h + 128))))
+    wt("s", *e_tc)
+    ev(Y.dma_start(T.oc[:], u8(T.t2[:])), 16, e_out)
     wt("v", e_y[0])
-    e_z0 = ev(V.tensor_copy(T.yt[:, 0:128], T.pr[:, 0:128]))
+    e_z0 = ev(V.tensor_copy(T.yt[:, 0:128], bank(2)))
     wt("a", e_y[1])
-    e_z1 = ev(S.activation(T.yt[:, 128:256], T.pr[:, 512:640], AF.Copy))
-    wt("s", e_t2[1])
+    e_z1 = ev(S.activation(T.yt[:, 128:256], bank(3), AF.Copy))
+    wt("v", e_la)
+    e_lb = ev(V.tensor_tensor(T.lb[0:1, :], T.pr[0:1, 512 + 17:512 + 81], T.la[0:1, :], A.subtract))
+    wt("s", *e_ts)
     for q in range(4):
         ev(Y.dma_start(T.osc[4 * q:4 * q + 4, :], T.t2s[32 * q:32 * q + 4, :]), 16, e_out)
     wt("s", e_z0)
     ev(Y.dma_start(T.y[:, 0:128], T.yt[:, 0:128]), 16, e_out)
     wt("a", e_z1)
     ev(S.dma_start(T.y[:, 128:256], T.yt[:, 128:256]), 16, e_out)
-    wt("a", r_l1)
-    ev(S.dma_start(T.li[0:1, :], T.ll1[0:64, 0:1]), 16, e_out)
-    wt("a", r_l2)
-    ev(S.dma_start(T.li[1:2, :], T.ll2[0:64, 0:1]), 16, e_out)
+    wt("s", e_lb)
+    ev(Y.dma_start(T.li[1:2, :], T.lb[0:1, :]), 16, e_out)
 
     done = {e for (_, e) in known}
     wt("s", *[e for e in made if e[0] not in done])

@@ -5,9 +5,7 @@ A = AluOpType
 AF = ActivationFunctionType
 F8, U8, BF, F32, I32, U16 = "float8_e4m3fn_x4", "uint8", "bfloat16", "float32", "int32", "uint16"
 EPS = 2.0 ** -110
-CM, CT, CX, CN, WW = 192, 256, 512, 640, 896
-CP = 192
-C2 = 176
+ZT, UT, BB = 320, 840, 856
 
 SCRATCH = {}
 
@@ -17,31 +15,28 @@ def _pair(n, w):
     SCRATCH[n + "s"] = ("sbuf", [128, w], U8)
 
 
-for _n, _w in (("uq", 128), ("ul", 8), ("un1", 256), ("un2", 256), ("vq", 512), ("wq", 128), ("eq", 576), ("pw", 384),
-               ("mq", 256), ("tq", 256), ("ww", WW), ("ohq", 128), ("flq", 128), ("t1", 256), ("t2", 256)):
+for _n, _w in (("uq", 128), ("un", 256), ("vq", 512), ("wq", 128), ("eq", 512), ("kq", 128), ("tq", 256), ("aw", 512),
+               ("bw", 512), ("f1", 128), ("f2", 128), ("t1", 256), ("t2", 256)):
     _pair(_n, _w)
-for _n, _w, _d in (("xt", 1024, BF), ("ut", 512, BF), ("vt", 2048, BF), ("wt", 512, BF), ("zt", 520, BF), ("kt", 512, BF),
-                   ("jt", 512, BF), ("oh", 512, BF), ("fl", 512, BF), ("nm", 512, BF), ("n0", 1024, BF), ("tb", 128, BF),
-                   ("mk", 128, BF), ("aa", 256, BF), ("mp", 128, BF), ("c2", 2 * C2, BF), ("g1", 256, BF), ("g2", 256, BF),
+for _n, _w, _d in (("xt", 1024, BF), ("bb", BB, BF), ("vt", 2048, BF), ("wt", 512, BF), ("kt", 512, BF), ("n1", 1024, BF),
+                   ("n2", 1024, BF), ("tb", 128, BF), ("mk", 128, BF), ("c2", 320, BF), ("g1", 256, BF), ("g2", 256, BF),
                    ("sc1", 256, BF), ("sc2", 256, BF), ("jk1", 256, BF), ("jk2", 256, BF), ("sg1", 2, F32), ("sg2", 2, F32),
-                   ("r1", 256, F32), ("r2", 256, F32), ("r0", 1024, F32), ("ii", 128, I32), ("ij", 128, I32),
-                   ("pc", 1, I32), ("pl", 1, I32), ("hl", 4, F32), ("zo", 16, U16), ("sl", 64, F32), ("l1", 4, U16),
-                   ("ll", 4, U16), ("lf", 4, F32), ("jr", 256, F32), ("vl", 64, F32), ("so", 256, F32), ("o1f", 16, F32),
-                   ("o1", 16, U16), ("o2f", 16, F32), ("o2", 16, U16), ("la", 64, F32), ("lb", 64, F32), ("yt", 256, F32)):
+                   ("r1", 1024, F32), ("r2", 1024, F32), ("ii", 128, I32), ("ij", 128, I32), ("jj", 8, I32), ("ja", 8, I32),
+                   ("sp", 8, F32), ("i16", 24, F32), ("zo", 16, U16), ("o1", 16, U16), ("o2", 16, U16), ("p1", 1, F32),
+                   ("p2", 1, F32), ("ll", 1, F32), ("yt", 256, F32)):
     SCRATCH[_n] = ("sbuf", [128, _w], _d)
 for _n, _w in (("pr", 2048), ("pm", 2048)):
     SCRATCH[_n] = ("psum", [128, _w], F32)
 
 NEV = 140
-SEMAPHORES = ["s%d" % _i for _i in range(NEV)] + ["lo", "lu", "lp", "ru", "rt", "rp", "rl", "rm"]
+SEMAPHORES = ["s%d" % _i for _i in range(NEV)] + ["lo", "lt", "r0", "r1", "rl"]
 
 
 def rank_program(g, core, T, topo):
     rank = T.rank_of(core)
     if rank is None:
         return
-    n = len(T.cores)
-    nxt, nx2, prv = T.cores[(rank + 1) % n], T.cores[(rank + 2) % n], T.cores[(rank - 1) % n]
+    nxt = T.cores[(rank + 1) % len(T.cores)]
     Q = {"g": g, "v": g.vector, "a": g.scalar, "s": g.sync, "t": g.tensor}
     V, S, P, Y = g.vector, g.scalar, g.tensor, g.sync
     made, known, nloc = [], {}, [0]
@@ -66,22 +61,13 @@ def rank_program(g, core, T, topo):
                 known[(q, e[0])] = 1
                 Q[q].wait_ge(T.sem[e[0]], e[1])
 
-    def bits(es):
-        m = 0
-        for e in es:
-            m |= 1 << e
-        return m
-
-    def send(dst, pairs, sem, loc="lo"):
-        rid, pid, _ = topo.addr(dst)
-        es = topo.engines(core, dst)
-        h = len(es) // len(pairs)
-        g.remote_dma_fused([RemoteDMATransfer(dst_ids=[DstId(rid=rid, pnc=pid)], dma_engine_mask=bits(es[i * h:i * h + h]),
-                                              remote_sem=T.sem[sem], srcs=[s], dsts=[d], alu_op=0)
-                            for i, (d, s) in enumerate(pairs)], local_sem=T.sem[loc])
+    def send(out, in_, sem, loc="lo"):
+        rid, pid, _ = topo.addr(nxt)
+        g.remote_dma(out, in_, T.sem[sem], T.sem[loc], pid, rid, topo.mask(core, nxt))
+        k = len(topo.engines(core, nxt))
         if loc == "lo":
-            nloc[0] += len(pairs) * h
-        return len(pairs) * h
+            nloc[0] += k
+        return k
 
     def u8(v):
         return v.bitcast(dt.uint8)
@@ -104,276 +90,191 @@ def rank_program(g, core, T, topo):
     def pick_s(dst, win, off):
         return S.activation(dst[1], win[1].indirect(off), AF.Copy)
 
-    e_u = ev(S.dma_start(T.ut[:, 0:4], T.u[:, 0:4]), 16)
-    e_x = [ev(Y.dma_start(T.xt[:, 512 * i:512 * i + 512], T.x[:, 512 * i:512 * i + 512]), 16) for i in range(2)]
+    def iota(out, pattern, base, cm=0):
+        return g.iota(out, pattern, base, cm, allow_small_or_imprecise_dtypes=True)
 
-    e_ii = ev(g.iota(T.ii[:], [[1, 128]], 128, -1))
-    e_pc = ev(g.iota(T.pc[:], [[1, 1]], 0, 1))
-    e_mp = ev(g.iota(T.mp[:], [[2, 4], [8, 16], [0, 2]], -128, 0, allow_small_or_imprecise_dtypes=True))
-
-    e_u0 = ev(V.memset(T.ut[:, 8:512], 0.0))
-    e_zo = evs(V.memset(T.zo[:, 0:8], 0), V.memset(T.zo[:, 8:16], 1))
-    e_z = evs(V.memset(T.oh[:, 256:512], 0.0), V.memset(T.zt[:], 0.0))
-    wt("v", e_ii, e_pc)
-    e_i = evs(V.tensor_scalar(T.ij[:], T.ii[:], 15, None, A.bitwise_and),
-              V.tensor_scalar(T.pl[:], T.pc[:], 15, None, A.bitwise_and))
-
-    wt("v", e_u, e_u0)
-    e_nu = ev(V.tensor_scalar(T.ut[:, 4:8], T.ut[:, 0:4], -1.0, None, A.mult))
-    wt("v", e_nu)
-    e_uq = quant(pair("uq", 0, 128), T.ut[:])
-    wt("g", e_uq)
-    r_u = ("ru", send(prv, [(u8(T.ul[:, 0:2]), u8(T.uq[:, 0:2])), (T.uls[:, 0:8], T.uqs[:, 0:8])], "ru", "lu"))
-    l_u = ("lu", r_u[1])
-
-    wt("v", e_i)
-    e_h = evs(V.tensor_copy(T.hl[:, 0:1], T.pl[:]), V.tensor_tensor(T.hl[:, 1:2], T.pc[:], T.pl[:], A.subtract))
-    e_mk = ev(V.tensor_scalar(T.mk[:], T.ij[:], 0.0, None, A.is_equal))
-    e_tb = ev(V.tensor_scalar(T.tb[:], T.ii[:], 128.0, -EPS, A.is_lt, A.mult))
-
-    e_t = []
-    for i in range(2):
-        wt("v", e_x[i])
-        e_t.append(quant(pair("tq", 128 * i, 128 * i + 128), T.xt[:, 512 * i:512 * i + 512]))
-    wt("g", *e_t)
-    k = send(nx2, [(u8(T.ww[:, CT:CT + 256]), u8(T.tq[:]))], "rt")
-    k += send(nx2, [(T.wws[:, CT:CT + 256], T.tqs[:])], "rt")
-    r_t = ("rt", k)
-    wt("s", l_u)
+    e_x = ev(Y.dma_start(T.xt[:], T.x[:]), 16)
+    e_u = ev(Y.dma_start(T.bb[:, UT:UT + 4], T.u[:, 0:4]), 16)
     e_v = [ev(Y.dma_start(T.vt[:, 1024 * i:1024 * i + 1024], T.v[:, 1024 * i:1024 * i + 1024]), 16) for i in range(2)]
 
-    zeros = T.oh[:, 256:384]
-    wt("v", e_h, e_z, e_mk)
-    wt("a", e_h, e_z)
-    e_j = evs(S.activation(T.jt[:, 0:512:4], zeros, AF.Identity, bias=T.hl[:, 1:2]),
-              S.activation(T.jt[:, 2:512:4], zeros, AF.Identity, bias=T.hl[:, 0:1]),
-              S.activation(T.jt[:, 3:512:4], zeros, AF.Identity, bias=T.hl[:, 0:1]),
-              V.tensor_scalar(T.jt[:, 1:512:4], zeros, T.hl[:, 1:2], 128.0, A.add, A.add))
-    e_a = evs(V.tensor_scalar(T.hl[:, 2:3], T.hl[:, 0:1], -1024.0, 15360.0, A.mult, A.add),
-              *[V.tensor_scalar(T.aa[:, 128 * h:128 * h + 128], T.mk[:], 66560.0, -1024.0, A.mult, A.add) for h in range(2)])
-    e_zc = ev(V.tensor_scalar(T.zt[:, 4:516:4], T.ii[:], 128.0, None, A.is_equal))
-    e_k = ev(V.memset(T.kt[:], 0.0))
-    e_c2 = ev(V.memset(T.c2[:], -1.0))
-    e_z2 = evs(V.memset(T.nm[:, 0:256], 0.0), V.memset(T.fl[:, 324:512], 0.0))
-    wt("v", e_j)
-    e_jq = quant(pair("mq", 0, 128), T.jt[:])
-    wt("v", e_zc)
-    e_e = evs(*[V.quantize_mx(T.eq[:, 128 * b:128 * b + 128], T.eqs[:, 128 * b:128 * b + 128], T.zt[:, 4 - b:516 - b])
-                for b in range(4)])
-    wt("v", e_k)
-    e_k = evs(*[V.tensor_scalar(T.kt[:, t:512:4], T.mk[:], 384.0, None, A.mult) for t in range(2)])
-    wt("v", e_zo)
-    wt("a", e_zo, e_uq)
-    wt("v", e_uq)
-    e_n2 = evs(pick_c(pair("un2", 0, 256), pair("uq", 0, 2), T.zo[:]), pick_s(pair("un2", 0, 256), pair("uq", 0, 2), T.zo[:]))
-    wt("v", e_k)
-    e_kq = quant(pair("pw", 256, 384), T.kt[:])
+    e_ii = ev(g.iota(T.ii[:], [[1, 128]], 128, -1))
+    e_jj = evs(g.iota(T.jj[:], [[0, 4], [128, 2]], 0, 1), iota(T.sp[:], [[0, 2], [-2, 2], [0, 2]], 1),
+               iota(T.i16[:], [[16, 24]], -128))
+    e_z = ev(V.memset(T.bb[:, ZT:UT], 0.0))
+    e_zo = evs(V.memset(T.zo[:, 0:8], 28), V.memset(T.zo[:, 8:16], 29))
+    e_c2 = ev(V.memset(T.c2[:, 289:320:2], -256.0))
+    wt("v", e_ii, e_z)
+    e_ij = ev(V.tensor_scalar(T.ij[:], T.ii[:], 15, None, A.bitwise_and))
+    e_id = ev(V.tensor_scalar(T.bb[:, ZT + 4:ZT + 516:4], T.ii[:], 128.0, None, A.is_equal))
+    e_tb = ev(V.tensor_scalar(T.tb[:], T.ii[:], 128.0, -EPS, A.is_lt, A.mult))
+    ev(V.tensor_scalar(T.c2[:, 129:160:2], T.ii[:, 0:16], 128.5, 1024.0, A.subtract, A.mult), 1, e_c2)
+    wt("v", e_ij, e_jj)
+    e_mk = ev(V.tensor_scalar(T.mk[:], T.ij[:], 0.0, None, A.is_equal))
+    e_ja = evs(V.tensor_scalar(T.ja[:, 0:4], T.jj[:, 0:4], 240, None, A.bitwise_and),
+               V.tensor_scalar(T.ja[:, 4:8], T.jj[:, 4:8], 15, None, A.bitwise_and))
+    wt("a", e_mk)
+    e_k = evs(*[S.activation(T.kt[:, t:512:4], T.mk[:], AF.Copy, scale=256.0) for t in range(2)],
+              *[S.activation(T.kt[:, t:512:4], T.mk[:], AF.Identity, bias=16.0, scale=0.0) for t in range(2, 4)])
 
-    wt("g", e_c2)
-    e_c = [ev(g.affine_select(T.c2[:, C2 * h:C2 * h + 32], T.c2[:, C2 * h:C2 * h + 32], [[-16, 16], [0, 2]], A.is_ge, -256.0,
-                              128 * h, 1)) for h in range(2)]
-    e_c2 = evs(*[g.iota(T.c2[:, C2 * h + 32:C2 * h + 162], [[2, 65], [0, 2]], -129, 0, allow_small_or_imprecise_dtypes=True)
-                 for h in range(2)])
-    for h in range(2):
-        wt("g", e_c[h])
-        ev(g.affine_select(T.c2[:, C2 * h:C2 * h + 32], T.c2[:, C2 * h:C2 * h + 32], [[16, 16], [0, 2]], A.is_ge, -256.0,
-                           15 - 128 * h, -1), 1, e_c2)
-    e_jr = evs(g.iota(T.jr[:], [[1, 256]], 64, 0, allow_small_or_imprecise_dtypes=True),
-               g.iota(T.vl[:], [[1, 64]], 0, 0, allow_small_or_imprecise_dtypes=True))
-
-    BLK = ((0, 0), (0, 1), (1, 1), (1, 0))
-
-    def bank(i, a=0, b=128):
-        return T.pr[:, 512 * i + a:512 * i + b]
-
-    def row(i, un, q):
-        mm(bank(i), pair(un, 0, 128), pair(q, 128 * BLK[i][1], 128 * BLK[i][1] + 128), True, False)
-
-    def col(i, un, q):
-        return ev(mm(bank(i), pair(q, 128 * BLK[i][0], 128 * BLK[i][0] + 128), pair(un, 128, 256), False, True))
-
-    def cmp_own(h, e, gb):
-        wt("v", e, e_tb)
-        return ev(V.tensor_tensor(gb[:, 128 * h:128 * h + 128], bank(2 * h), T.tb[:], A.is_gt))
-
-    def count_own(h, e, gb, sc, e_o, sg):
-        wt("v", e, e_o)
-        s = slice(128 * h, 128 * h + 128)
-        return ev(V.tensor_tensor_scan(sc[:, s], gb[:, s], gb[:, s], sg[:, h:h + 1], A.add, A.add))
-
-    def count_other(h, e, jk, sg):
-        wt("a", e)
-        return ev(S.activation(jk[:, 128 * h:128 * h + 128], bank(2 * h + 1), AF.Sign, bias=(EPS if h else -EPS),
-                               accum_out=sg[:, h:h + 1]))
-
-    wt("v", r_u)
-    wt("a", r_u)
-    e_n = [evs(pick_c(pair("un1", 128 * i, 128 * i + 128), pair("ul", 0, 2), T.zo[:, 8 * i:8 * i + 8]),
-               pick_s(pair("un1", 128 * i, 128 * i + 128), pair("ul", 0, 2), T.zo[:, 8 * i:8 * i + 8])) for i in range(2)]
-    wt("t", e_n[0], *e_t)
-    for i in range(4):
-        row(i, "un1", "tq")
-    wt("t", e_n[1])
-    e_d = {i: col(i, "un1", "tq") for i in (1, 0, 3, 2)}
-    e_g0 = cmp_own(0, e_d[0], T.g1)
-    e_g1 = cmp_own(1, e_d[2], T.g1)
-    e_o = [count_other(h, e_d[2 * h + 1], T.jk1, T.sg1) for h in range(2)]
-    e_s = [count_own(0, e_g0, T.g1, T.sc1, e_o[0], T.sg1), count_own(1, e_g1, T.g1, T.sc1, e_o[1], T.sg1)]
-    wt("v", e_mp)
-    e_oh = None
-    for h in range(2):
-        wt("v", e_s[h])
-        e_oh = ev(V.tensor_scalar(T.oh[:, h:256:2], T.mp[:], T.sc1[:, 128 * h + 127:128 * h + 128], None, A.is_equal), 1, e_oh)
-    wt("v", e_oh)
-    e_ohq = quant(pair("ohq", 0, 128), T.oh[:])
-    wt("t", e_ohq, e_jq)
-    e_l = ev(mm(bank(0), pair("mq", 0, 128), pair("ohq", 0, 128)))
-    wt("v", e_l, e_a)
-    e_l = ev(V.tensor_tensor_scan(T.sl[:], T.aa[:, 0:64], bank(0, 0, 64), 0.0, A.add, A.min))
-    wt("v", e_l)
-    e_l = ev(V.tensor_scalar(T.l1[:], T.sl[:, 15:64:16], T.hl[:, 2:3], None, A.add))
-    wt("v", e_l)
-    wt("a", e_l)
-    e_p = evs(pick_c(pair("eq", 512, 576), pair("tq", 0, 256), T.l1[:]), pick_s(pair("eq", 512, 576), pair("tq", 0, 256), T.l1[:]))
-    wt("g", e_p, e_e)
-    r_p = ("rp", send(nxt, [(u8(T.pw[:, CP:CP + 64]), u8(T.eq[:, 512:576])), (T.pws[:, 0:256], T.eqs[:, 320:576])], "rp", "lp"))
-    r_l = ("rl", send(nx2, [(T.ll[:], T.l1[:])], "rl"))
-    wt("s", ("lp", r_p[1]))
+    wt("v", e_x)
+    e_t = quant(pair("tq", 0, 256), T.xt[:])
+    wt("g", e_t)
+    k = send(u8(T.aw[:, 0:256]), u8(T.tq[:]), "r0", "lt")
+    k += send(T.aws[:, 0:256], T.tqs[:], "r0", "lt")
+    r_0 = ("r0", k)
+    wt("s", ("lt", k))
     e_w = ev(Y.dma_start(T.wt[:], T.w[:]), 16)
+    for h in range(2):
+        ev(iota(T.c2[:, 160 * h:160 * h + 128], [[2, 64], [-2, 2]], -127), 1, e_c2)
 
-    free = [[], []]
-
-    def prods(i, src, w):
-        b = 1024 * (i % 2)
-        wt("t", e_vq[i // 2], *free[i % 2])
-        e_1 = ev(mm(T.pm[:, b:b + w], pair("vq", 128 * i, 128 * i + 128), src))
-        wt("t", e_e)
-        e_2 = ev(mm(T.pm[:, b + 512:b + 512 + w], pair("eq", 128 * i, 128 * i + 128), src))
-        return e_1, e_2
-
-    def relu(i, e, rl, w):
-        b = 1024 * (i % 2)
-        wt("a", e[0])
-        return ev(S.activation(rl[:, w * i:w * i + w], T.pm[:, b:b + w], AF.Relu, scale=0.05))
-
-    def add(i, e, e_r, rl, nb, w):
-        b = 1024 * (i % 2) + 512
-        z = 4 * max(w, 128)
-        wt("v", e[1], e_r)
-        e_s = ev(V.tensor_tensor(nb[:, z - 4 * w + i:z:4], T.pm[:, b:b + w], rl[:, w * i:w * i + w], A.add))
-        free[i % 2] = [e_s]
-        return e_s
-
-    def make(i, src, rl, nb, w):
-        e = prods(i, src, max(w, 128))
-        return add(i, e, relu(i, e, rl, w), rl, nb, w)
-
+    wt("v", e_ja, e_u)
+    e_j = evs(V.tensor_tensor(T.bb[:, UT + 8:UT + 16], T.ja[:], T.sp[:], A.mult),
+              V.tensor_scalar(T.bb[:, UT + 4:UT + 8], T.bb[:, UT:UT + 4], -1.0, None, A.mult))
+    hi, lo = T.bb[:, UT + 8:UT + 9], T.bb[:, UT + 12:UT + 13]
+    wt("v", e_id)
+    e_e = evs(*[V.quantize_mx(T.eq[:, 128 * b:128 * b + 128], T.eqs[:, 128 * b:128 * b + 128], T.bb[:, ZT + 4 - b:ZT + 516 - b])
+                for b in range(2)])
+    wt("v", e_j)
+    e_uq = quant(pair("uq", 0, 128), T.bb[:, BB - 512:BB])
+    for h in range(2):
+        ev(V.tensor_scalar(T.c2[:, 160 * h + 128:160 * h + 160:2], T.i16[:, 8 - 8 * h:24 - 8 * h], hi, -256.0,
+                           A.not_equal, A.mult), 1, e_c2)
+    for b in range(2, 4):
+        ev(V.quantize_mx(T.eq[:, 128 * b:128 * b + 128], T.eqs[:, 128 * b:128 * b + 128], T.bb[:, ZT + 4 - b:ZT + 516 - b]), 1, e_e)
+    wt("v", e_zo, e_uq)
+    wt("a", e_zo, e_uq)
+    e_un = evs(pick_c(pair("un", 0, 256), pair("uq", 96, 128), T.zo[:]), pick_s(pair("un", 0, 256), pair("uq", 96, 128), T.zo[:]))
+    wt("v", e_k)
+    e_kq = quant(pair("kq", 0, 128), T.kt[:])
     e_vq = []
     for i in range(2):
         wt("v", e_v[i])
         e_vq.append(quant(pair("vq", 256 * i, 256 * i + 256), T.vt[:, 1024 * i:1024 * i + 1024]))
 
-    wt("t", r_t)
-    e_0 = [make(i, pair("ww", CT, CT + 256), T.r0, T.n0, 256) for i in range(1)]
+    BLK = ((0, 0), (0, 1), (1, 1), (1, 0))
 
-    wt("t", r_p, e_kq)
-    e_m = [make(i, pair("pw", CP, CP + 128), T.r1, T.nm, 64) for i in range(4)]
-    wt("v", e_z2, *e_m)
-    e_m = quant(pair("mq", 128, 256), T.nm[:])
-    wt("g", e_m, e_jq)
-    r_m = ("rm", send(nxt, [(u8(T.ww[:, CM:CM + 64]), u8(T.mq[:, 192:256])), (T.wws[:, 0:256], T.mqs[:])], "rm"))
+    def bank(i, a=0, b=128):
+        return (T.pr, T.pm)[i // 4][:, 512 * (i % 4) + a:512 * (i % 4) + b]
 
-    wt("v", r_l, e_jr)
-    e_sc = ev(V.tensor_copy(T.jr[:].indirect(T.ll[:]), T.vl[:]))
-    e_lf = ev(V.tensor_copy(T.lf[0:16, :], T.ll[0:16, :]))
-    wt("s", e_lf)
-    e_out = ev(Y.dma_start(T.li[0:1, :], T.lf[0:16, :]), 16)
-    e_0.append(make(1, pair("ww", CT, CT + 256), T.r0, T.n0, 256))
-    wt("v", e_sc)
-    e_sc = ev(V.tensor_tensor_scan(T.so[:], T.aa[:], T.jr[:], 0.0, A.add, A.min))
-    e_0.append(make(2, pair("ww", CT, CT + 256), T.r0, T.n0, 256))
-    wt("v", e_sc)
-    e_o1 = evs(V.tensor_scalar(T.o1[:], T.so[:, 15:256:16], T.hl[:, 2:3], None, A.add),
-               V.tensor_scalar(T.o1f[:], T.so[:, 15:256:16], T.hl[:, 2:3], None, A.add))
-    e_0.append(make(3, pair("ww", CT, CT + 256), T.r0, T.n0, 256))
-    wt("v", *e_0)
-    e_0 = quant(pair("ww", CN, CN + 256), T.n0[:])
+    RB, DB = (4, 6, 4, 3), (5, 7, 5, 2)
+
+    def stop(w, arrived, fq, gb, sc, jk, sg, rl, nb, off, t, before):
+        old = pair(w, 0, 256)
+
+        def prods(i, *free):
+            wt("t", e_vq[i // 2], e_e, *free)
+            e_1 = ev(mm(bank(RB[i], 0, 256), pair("vq", 128 * i, 128 * i + 128), old))
+            e_2 = ev(mm(bank(DB[i], 0, 256), pair("eq", 128 * i, 128 * i + 128), old))
+            return e_1, e_2
+
+        def relu(i, e, a=0, b=256):
+            wt("a", e[0])
+            return ev(S.activation(rl[:, 256 * i + a:256 * i + b], bank(RB[i], a, b), AF.Relu, scale=0.05))
+
+        def add(i, e, e_r, a=0, b=256):
+            wt("v", e[1], e_r)
+            return ev(V.tensor_tensor(nb[:, 4 * a + i:4 * b:4], bank(DB[i], a, b), rl[:, 256 * i + a:256 * i + b], A.add))
+
+        def block(i):
+            a, b = 128 * BLK[i][0], 128 * BLK[i][1]
+            mm(bank(i), pair("un", 0, 128), pair(w, b, b + 128), True, False)
+            return ev(mm(bank(i), pair(w, a, a + 128), pair("un", 128, 256), False, True))
+
+        def cmp_own(h):
+            wt("v", e_d[2 * h], e_tb)
+            return ev(V.tensor_tensor(gb[:, 128 * h:128 * h + 128], bank(2 * h), T.tb[:], A.is_gt))
+
+        def count_other(h):
+            wt("a", e_d[2 * h + 1])
+            return ev(S.activation(jk[:, 128 * h:128 * h + 128], bank(2 * h + 1), AF.Sign, bias=(EPS if h else -EPS),
+                                   accum_out=sg[:, h:h + 1]))
+
+        def count_own(h, e):
+            wt("v", e, e_o[h])
+            s = slice(128 * h, 128 * h + 128)
+            return ev(V.tensor_tensor_scan(sc[:, s], gb[:, s], gb[:, s], sg[:, h:h + 1], A.add, A.add))
+
+        def steps(h, e, e_f):
+            wt("v", e, e_c2)
+            return ev(V.tensor_scalar(T.bb[:, h:320:2], T.c2[:, 160 * h:160 * h + 160], sc[:, 128 * h + 127:128 * h + 128],
+                                      None, A.is_gt), 1, e_f)
+
+        wt("t", arrived, e_un, *before)
+        e_p = [prods(0)]
+        e_d = {i: block(i) for i in (1, 0, 3, 2)}
+        e_r = [relu(0, e_p[0])]
+        e_o = [count_other(h) for h in range(2)]
+        e_a = [add(0, e_p[0], e_r[0])]
+        e_g = [cmp_own(h) for h in range(2)]
+        e_p.append(prods(1))
+        e_p.append(prods(2, e_a[0]))
+        e_p.append(prods(3, e_g[1], e_o[1]))
+        e_r += [relu(1, e_p[1]), relu(2, e_p[2])]
+        e_r3 = [relu(3, e_p[3], 128 * h, 128 * h + 128) for h in range(2)]
+        e_s = [count_own(h, e_g[h]) for h in range(2)]
+        e_f = steps(1, e_s[1], steps(0, e_s[0], None))
+        e_a.append(add(1, e_p[1], e_r[1]))
+        wt("v", e_f)
+        e_f = quant(pair(fq, 0, 128), T.bb[:, 0:512])
+        wt("t", e_f, e_kq)
+        e_m = ev(mm(bank(0), pair("kq", 0, 128), pair(fq, 0, 128)))
+        e_l = ev(mm(bank(1), pair(fq, 0, 128), pair("uq", 0, 128)))
+        e_a.append(add(2, e_p[2], e_r[2]))
+        e_a3 = [add(3, e_p[3], e_r3[h], 128 * h, 128 * h + 128) for h in range(2)]
+        wt("v", e_m)
+        e_of = ev(V.tensor_scalar(off[:], bank(0, 64, 80), lo, None, A.add))
+        e_q = []
+        for h in range(2):
+            wt("v", e_a3[h], *e_a)
+            e_q.append(quant(pair(w, 256 + 128 * h, 384 + 128 * h), nb[:, 512 * h:512 * h + 512]))
+        e_c, e_n = [], []
+        for h in range(2):
+            wt("v", e_of, e_q[h])
+            wt("a", e_of, e_q[h])
+            a = (pair(t, 128 * h, 128 * h + 128), pair(w, 0, 384 + 128 * h), off[:, 8 * h:8 * h + 8])
+            e_c.append(ev(pick_c(*a)))
+            e_n.append(ev(pick_s(*a)))
+        return e_c, e_n, e_l, [e_of] + e_a + e_a3
+
+    def places(e_l, out):
+        wt("v", e_l)
+        return ev(V.tensor_scalar(out[:], bank(1, 126, 127), bank(1, 127, 128), None, A.add))
+
+    e_c, e_n, e_l, fr = stop("aw", r_0, "f1", T.g1, T.sc1, T.jk1, T.sg1, T.r1, T.n1, T.o1, "t1", [])
+    wt("g", *e_c)
+    k = send(u8(T.bw[:, 0:256]), u8(T.t1[:]), "r1")
+    wt("g", *e_n)
+    k += send(T.bws[:, 0:256], T.t1s[:], "r1")
+    r_1 = ("r1", k)
+    e_l = places(e_l, T.p1)
+    wt("g", e_l)
+    r_l = ("rl", send(T.ll[:], T.p1[:], "rl"))
     wt("v", e_w)
     e_wq = quant(pair("wq", 0, 128), T.wt[:])
+    wt("s", r_l)
+    e_out = ev(Y.dma_start(T.li[0:1, :], T.ll[0:64, :]), 16)
 
-    src = pair("ww", CM, CM + 128)
-    wt("t", r_m)
-    e_pr = [prods(i, src, 128) for i in range(2)]
-    wt("v", r_m, r_t, e_o1)
-    wt("a", r_m, r_t, e_o1)
-    e_t1 = [evs(pick_c(pair("t1", 128 * h, 128 * h + 128), pair("ww", CM, CX), T.o1[:, 8 * h:8 * h + 8]),
-                pick_s(pair("t1", 128 * h, 128 * h + 128), pair("ww", CM, CX), T.o1[:, 8 * h:8 * h + 8])) for h in range(2)]
-    e_d = {}
-    wt("t", e_n2, e_l)
-    for i in (0, 1, 3, 2):
-        wt("t", e_t1[min(i, 1)])
-        row(i, "un2", "t1")
-        e_d[i] = col(i, "un2", "t1")
-    e_r = [relu(i, e_pr[i], T.r2, 64) for i in range(2)]
-    wt("v", e_m)
-    e_x = [add(0, e_pr[0], e_r[0], T.r2, T.nm, 64)]
-    e_g0 = cmp_own(0, e_d[0], T.g2)
-    e_x.append(add(1, e_pr[1], e_r[1], T.r2, T.nm, 64))
-    e_pr += [prods(i, src, 128) for i in range(2, 4)]
-    e_o = [count_other(h, e_d[2 * h + 1], T.jk2, T.sg2) for h in range(2)]
-    e_s = [count_own(0, e_g0, T.g2, T.sc2, e_o[0], T.sg2)]
-    e_g1 = cmp_own(1, e_d[2], T.g2)
-    e_s.append(count_own(1, e_g1, T.g2, T.sc2, e_o[1], T.sg2))
-    e_r += [relu(i, e_pr[i], T.r2, 64) for i in range(2, 4)]
-    wt("v", e_c2)
-    e_f = None
-    for h in range(2):
-        wt("v", e_s[h])
-        e_f = ev(V.tensor_scalar(T.fl[:, h:324:2], T.c2[:, C2 * h:C2 * h + 162], T.sc2[:, 128 * h + 127:128 * h + 128],
-                                 None, A.is_gt), 1, e_f)
-    wt("v", e_f)
-    e_f = quant(pair("flq", 0, 128), T.fl[:])
-    wt("t", e_f, e_kq)
-    e_k = ev(mm(bank(0), pair("pw", 256, 384), pair("flq", 0, 128)))
-    e_j = ev(mm(bank(1), pair("mq", 0, 128), pair("flq", 0, 128)))
-    e_x += [add(i, e_pr[i], e_r[i], T.r2, T.nm, 64) for i in range(2, 4)]
-    wt("v", e_k)
-    e_k = ev(V.tensor_tensor(T.o2f[:], bank(0, 0, 16), T.o1f[:], A.add))
-    wt("v", *e_x)
-    e_x = quant(pair("ww", CX, CX + 128), T.nm[:])
-    wt("v", e_k)
-    e_k = ev(V.tensor_copy(T.o2[:], T.o2f[:]))
-    wt("a", e_j)
-    e_la = ev(S.activation(T.la[0:1, :], T.pr[0:1, 512 + 16:512 + 80], AF.Copy))
-    wt("v", e_k, e_x, e_0)
-    wt("a", e_k, e_x, e_0)
-    e_tc, e_ts = [], []
-    for h in range(2):
-        e_tc.append(ev(pick_c(pair("t2", 128 * h, 128 * h + 128), pair("ww", CM, WW), T.o2[:, 8 * h:8 * h + 8])))
-        e_ts.append(ev(pick_s(pair("t2", 128 * h, 128 * h + 128), pair("ww", CM, WW), T.o2[:, 8 * h:8 * h + 8])))
+    e_c, e_n, e_l, fr = stop("bw", r_1, "f2", T.g2, T.sc2, T.jk2, T.sg2, T.r2, T.n2, T.o2, "t2", fr + [e_l])
 
     e_y = []
     wt("t", e_wq)
     for h in range(2):
-        wt("t", e_tc[h], e_ts[h])
-        e_y.append(ev(mm(bank(2 + h), pair("wq", 0, 128), pair("t2", 128 * h, 128 * h + 128))))
-    wt("s", *e_tc)
+        wt("t", e_c[h], e_n[h])
+        e_y.append(ev(mm(bank(6 + h), pair("wq", 0, 128), pair("t2", 128 * h, 128 * h + 128))))
+    wt("s", *e_c)
     ev(Y.dma_start(T.oc[:], u8(T.t2[:])), 16, e_out)
-    wt("v", e_y[0])
-    e_z0 = ev(V.tensor_copy(T.yt[:, 0:128], bank(2)))
-    wt("a", e_y[1])
-    e_z1 = ev(S.activation(T.yt[:, 128:256], bank(3), AF.Copy))
-    wt("v", e_la)
-    e_lb = ev(V.tensor_tensor(T.lb[0:1, :], T.pr[0:1, 512 + 17:512 + 81], T.la[0:1, :], A.subtract))
-    wt("s", *e_ts)
+    e_l = places(e_l, T.p2)
+    wt("a", e_y[0])
+    e_z0 = ev(S.activation(T.yt[:, 0:128], bank(6), AF.Copy))
+    wt("v", e_y[1])
+    e_z1 = ev(V.tensor_copy(T.yt[:, 128:256], bank(7)))
+    wt("s", *e_n)
     for q in range(4):
         ev(Y.dma_start(T.osc[4 * q:4 * q + 4, :], T.t2s[32 * q:32 * q + 4, :]), 16, e_out)
-    wt("s", e_z0)
-    ev(Y.dma_start(T.y[:, 0:128], T.yt[:, 0:128]), 16, e_out)
-    wt("a", e_z1)
-    ev(S.dma_start(T.y[:, 128:256], T.yt[:, 128:256]), 16, e_out)
-    wt("s", e_lb)
-    ev(Y.dma_start(T.li[1:2, :], T.lb[0:1, :]), 16, e_out)
+    wt("a", e_z0, e_z1)
+    ev(S.dma_start(T.y[:], T.yt[:]), 16, e_out)
+    wt("s", e_l)
+    ev(Y.dma_start(T.li[1:2, :], T.p2[0:64, :]), 16, e_out)
 
     done = {e for (_, e) in known}
     wt("s", *[e for e in made if e[0] not in done])

@@ -5,7 +5,7 @@ A = AluOpType
 AF = ActivationFunctionType
 F8, U8, BF, F32, I32, U16 = "float8_e4m3fn_x4", "uint8", "bfloat16", "float32", "int32", "uint16"
 EPS = 2.0 ** -110
-ZT, UT, BB = 320, 840, 856
+UT, ZT, BB = 320, 336, 856
 
 SCRATCH = {}
 
@@ -15,31 +15,31 @@ def _pair(n, w):
     SCRATCH[n + "s"] = ("sbuf", [128, w], U8)
 
 
-for _n, _w in (("uq", 128), ("un", 256), ("vq", 512), ("wq", 128), ("eq", 512), ("kq", 128), ("tq", 256), ("aw", 512),
-               ("bw", 512), ("f1", 128), ("f2", 128), ("t1", 256), ("t2", 256)):
+for _n, _w in (("uq", 128), ("un", 256), ("ul", 8), ("um", 256), ("vq", 512), ("wq", 128), ("eq", 512), ("kq", 128),
+               ("tq", 256), ("aw", 512), ("bw", 576), ("f1", 128), ("f2", 128), ("t1", 256), ("t2", 256)):
     _pair(_n, _w)
 for _n, _w, _d in (("xt", 1024, BF), ("bb", BB, BF), ("vt", 2048, BF), ("wt", 512, BF), ("kt", 512, BF), ("n1", 1024, BF),
                    ("n2", 1024, BF), ("tb", 128, BF), ("mk", 128, BF), ("c2", 320, BF), ("g1", 256, BF), ("g2", 256, BF),
                    ("sc1", 256, BF), ("sc2", 256, BF), ("jk1", 256, BF), ("jk2", 256, BF), ("sg1", 2, F32), ("sg2", 2, F32),
                    ("r1", 1024, F32), ("r2", 1024, F32), ("ii", 128, I32), ("ij", 128, I32), ("jj", 8, I32), ("ja", 8, I32),
-                   ("sp", 8, F32), ("i16", 24, F32), ("zo", 16, U16), ("o1", 16, U16), ("o2", 16, U16), ("p1", 1, F32),
-                   ("p2", 1, F32), ("ll", 1, F32), ("yt", 256, F32)):
+                   ("sp", 8, F32), ("i16", 24, F32), ("zo", 16, U16), ("o1", 16, U16), ("o2", 16, U16), ("pp", 2, F32),
+                   ("ll", 2, F32), ("pj", 4, F32), ("yt", 256, F32)):
     SCRATCH[_n] = ("sbuf", [128, _w], _d)
 for _n, _w in (("pr", 2048), ("pm", 2048)):
     SCRATCH[_n] = ("psum", [128, _w], F32)
 
-NEV = 140
-SEMAPHORES = ["s%d" % _i for _i in range(NEV)] + ["lo", "lt", "r0", "r1", "rl"]
+NEV = 143
+SEMAPHORES = ["s%d" % _i for _i in range(NEV)] + ["lo", "lt", "ru", "ra", "rb", "rf", "rl"]
 
 
 def rank_program(g, core, T, topo):
     rank = T.rank_of(core)
     if rank is None:
         return
-    nxt = T.cores[(rank + 1) % len(T.cores)]
+    nxt, prv = T.cores[(rank + 1) % len(T.cores)], T.cores[(rank - 1) % len(T.cores)]
     Q = {"g": g, "v": g.vector, "a": g.scalar, "s": g.sync, "t": g.tensor}
     V, S, P, Y = g.vector, g.scalar, g.tensor, g.sync
-    made, known, nloc = [], {}, [0]
+    made, known, nloc, E = [], {}, {"lo": 0, "lt": 0}, {}
 
     def ev(ins, k=1, e=None):
         if e is None:
@@ -49,15 +49,9 @@ def rank_program(g, core, T, topo):
         e[1] += k
         return e
 
-    def evs(*ins):
-        e = None
-        for i in ins:
-            e = ev(i, 1, e)
-        return e
-
     def wt(q, *es):
         for e in es:
-            if e is not None and (q, e[0]) not in known:
+            if (q, e[0]) not in known:
                 known[(q, e[0])] = 1
                 Q[q].wait_ge(T.sem[e[0]], e[1])
 
@@ -65,9 +59,19 @@ def rank_program(g, core, T, topo):
         rid, pid, _ = topo.addr(nxt)
         g.remote_dma(out, in_, T.sem[sem], T.sem[loc], pid, rid, topo.mask(core, nxt))
         k = len(topo.engines(core, nxt))
-        if loc == "lo":
-            nloc[0] += k
+        nloc[loc] += k
         return k
+
+    def send2(dst, pairs, sem, loc="lo"):
+        rid, pid, _ = topo.addr(dst)
+        es = topo.engines(core, dst)
+        h = len(es) // 2
+        g.remote_dma_fused([RemoteDMATransfer(dst_ids=[DstId(rid=rid, pnc=pid)],
+                                              dma_engine_mask=sum(1 << e for e in es[i * h:i * h + h]),
+                                              remote_sem=T.sem[sem], srcs=[s], dsts=[d], alu_op=0)
+                            for i, (d, s) in enumerate(pairs)], local_sem=T.sem[loc])
+        nloc[loc] += 2 * h
+        return (sem, 2 * h)
 
     def u8(v):
         return v.bitcast(dt.uint8)
@@ -93,189 +97,282 @@ def rank_program(g, core, T, topo):
     def iota(out, pattern, base, cm=0):
         return g.iota(out, pattern, base, cm, allow_small_or_imprecise_dtypes=True)
 
-    e_x = ev(Y.dma_start(T.xt[:], T.x[:]), 16)
-    e_u = ev(Y.dma_start(T.bb[:, UT:UT + 4], T.u[:, 0:4]), 16)
-    e_v = [ev(Y.dma_start(T.vt[:, 1024 * i:1024 * i + 1024], T.v[:, 1024 * i:1024 * i + 1024]), 16) for i in range(2)]
+    def send_tile(dst, src, e_c, e_s, sem, loc="lo"):
+        wt("g", *e_c)
+        k = send(u8(dst[0]), u8(src[0]), sem, loc)
+        wt("g", *e_s)
+        return (sem, k + send(dst[1], src[1], sem, loc))
 
-    e_ii = ev(g.iota(T.ii[:], [[1, 128]], 128, -1))
-    e_jj = evs(g.iota(T.jj[:], [[0, 4], [128, 2]], 0, 1), iota(T.sp[:], [[0, 2], [-2, 2], [0, 2]], 1),
-               iota(T.i16[:], [[16, 24]], -128))
-    e_z = ev(V.memset(T.bb[:, ZT:UT], 0.0))
-    e_zo = evs(V.memset(T.zo[:, 0:8], 28), V.memset(T.zo[:, 8:16], 29))
-    e_c2 = ev(V.memset(T.c2[:, 289:320:2], -256.0))
-    wt("v", e_ii, e_z)
-    e_ij = ev(V.tensor_scalar(T.ij[:], T.ii[:], 15, None, A.bitwise_and))
-    e_id = ev(V.tensor_scalar(T.bb[:, ZT + 4:ZT + 516:4], T.ii[:], 128.0, None, A.is_equal))
-    e_tb = ev(V.tensor_scalar(T.tb[:], T.ii[:], 128.0, -EPS, A.is_lt, A.mult))
-    ev(V.tensor_scalar(T.c2[:, 129:160:2], T.ii[:, 0:16], 128.5, 1024.0, A.subtract, A.mult), 1, e_c2)
-    wt("v", e_ij, e_jj)
-    e_mk = ev(V.tensor_scalar(T.mk[:], T.ij[:], 0.0, None, A.is_equal))
-    e_ja = evs(V.tensor_scalar(T.ja[:, 0:4], T.jj[:, 0:4], 240, None, A.bitwise_and),
-               V.tensor_scalar(T.ja[:, 4:8], T.jj[:, 4:8], 15, None, A.bitwise_and))
-    wt("a", e_mk)
-    e_k = evs(*[S.activation(T.kt[:, t:512:4], T.mk[:], AF.Copy, scale=256.0) for t in range(2)],
-              *[S.activation(T.kt[:, t:512:4], T.mk[:], AF.Identity, bias=16.0, scale=0.0) for t in range(2, 4)])
-
-    wt("v", e_x)
-    e_t = quant(pair("tq", 0, 256), T.xt[:])
-    wt("g", e_t)
-    k = send(u8(T.aw[:, 0:256]), u8(T.tq[:]), "r0", "lt")
-    k += send(T.aws[:, 0:256], T.tqs[:], "r0", "lt")
-    r_0 = ("r0", k)
-    wt("s", ("lt", k))
-    e_w = ev(Y.dma_start(T.wt[:], T.w[:]), 16)
-    for h in range(2):
-        ev(iota(T.c2[:, 160 * h:160 * h + 128], [[2, 64], [-2, 2]], -127), 1, e_c2)
-
-    wt("v", e_ja, e_u)
-    e_j = evs(V.tensor_tensor(T.bb[:, UT + 8:UT + 16], T.ja[:], T.sp[:], A.mult),
-              V.tensor_scalar(T.bb[:, UT + 4:UT + 8], T.bb[:, UT:UT + 4], -1.0, None, A.mult))
     hi, lo = T.bb[:, UT + 8:UT + 9], T.bb[:, UT + 12:UT + 13]
-    wt("v", e_id)
-    e_e = evs(*[V.quantize_mx(T.eq[:, 128 * b:128 * b + 128], T.eqs[:, 128 * b:128 * b + 128], T.bb[:, ZT + 4 - b:ZT + 516 - b])
-                for b in range(2)])
-    wt("v", e_j)
-    e_uq = quant(pair("uq", 0, 128), T.bb[:, BB - 512:BB])
-    for h in range(2):
-        ev(V.tensor_scalar(T.c2[:, 160 * h + 128:160 * h + 160:2], T.i16[:, 8 - 8 * h:24 - 8 * h], hi, -256.0,
-                           A.not_equal, A.mult), 1, e_c2)
-    for b in range(2, 4):
-        ev(V.quantize_mx(T.eq[:, 128 * b:128 * b + 128], T.eqs[:, 128 * b:128 * b + 128], T.bb[:, ZT + 4 - b:ZT + 516 - b]), 1, e_e)
-    wt("v", e_zo, e_uq)
-    wt("a", e_zo, e_uq)
-    e_un = evs(pick_c(pair("un", 0, 256), pair("uq", 96, 128), T.zo[:]), pick_s(pair("un", 0, 256), pair("uq", 96, 128), T.zo[:]))
-    wt("v", e_k)
-    e_kq = quant(pair("kq", 0, 128), T.kt[:])
-    e_vq = []
-    for i in range(2):
-        wt("v", e_v[i])
-        e_vq.append(quant(pair("vq", 256 * i, 256 * i + 256), T.vt[:, 1024 * i:1024 * i + 1024]))
+    ident = T.bb[:, ZT + 4:ZT + 516:4]
 
-    BLK = ((0, 0), (0, 1), (1, 1), (1, 0))
+    def c2f(h):
+        return lambda: V.tensor_scalar(T.c2[:, 160 * h + 128:160 * h + 160:2], T.i16[:, 8 - 8 * h:24 - 8 * h], hi, -256.0,
+                                       A.not_equal, A.mult)
 
-    def bank(i, a=0, b=128):
+    def kf(t):
+        if t < 2:
+            return lambda: S.activation(T.kt[:, t:512:4], T.mk[:], AF.Copy, scale=256.0)
+        return lambda: S.activation(T.kt[:, t:512:4], T.mk[:], AF.Identity, bias=16.0, scale=0.0)
+
+    def qf(dst, src):
+        return lambda: V.quantize_mx(dst[0], dst[1], src)
+
+    xu = (pair("un", 0, 256), pair("uq", 0, 2), T.zo[:])
+    CALLS = {
+        "x": ("s", (), lambda: Y.dma_start(T.xt[:], T.x[:]), 16),
+        "u": ("s", (), lambda: Y.dma_start(T.bb[:, UT:UT + 4], T.u[:, 0:4]), 16),
+        "v0": ("s", (), lambda: Y.dma_start(T.vt[:, 0:1024], T.v[:, 0:1024]), 16),
+        "v1": ("s", (), lambda: Y.dma_start(T.vt[:, 1024:2048], T.v[:, 1024:2048]), 16),
+        "w": ("s", ("lt",), lambda: Y.dma_start(T.wt[:], T.w[:]), 16),
+        "jj": ("g", (), lambda: g.iota(T.jj[:], [[0, 4], [128, 2]], 0, 1), 1),
+        "sp": ("g", (), lambda: iota(T.sp[:], [[0, 2], [-2, 2], [0, 2]], 1), 1),
+        "ii": ("g", (), lambda: g.iota(T.ii[:], [[1, 128]], 128, -1), 1),
+        "i16": ("g", (), lambda: iota(T.i16[:], [[16, 24]], -128), 1),
+        "cl0": ("g", (), lambda: iota(T.c2[:, 0:128], [[2, 64], [-2, 2]], -127), 1),
+        "cl1": ("g", (), lambda: iota(T.c2[:, 160:288], [[2, 64], [-2, 2]], -127), 1),
+        "id": ("g", ("z",), lambda: g.affine_select(ident, ident, [[1, 128]], A.not_equal, 1.0, 0, -1), 1),
+        "z": ("v", (), lambda: V.memset(T.bb[:, ZT:BB], 0.0), 1),
+        "zo0": ("v", (), lambda: V.memset(T.zo[:, 0:8], 0), 1),
+        "zo1": ("v", (), lambda: V.memset(T.zo[:, 8:16], 1), 1),
+        "cm": ("v", (), lambda: V.memset(T.c2[:, 289:320:2], -256.0), 1),
+        "ja0": ("v", ("jj",), lambda: V.tensor_scalar(T.ja[:, 0:4], T.jj[:, 0:4], 240, None, A.bitwise_and), 1),
+        "ja1": ("v", ("jj",), lambda: V.tensor_scalar(T.ja[:, 4:8], T.jj[:, 4:8], 15, None, A.bitwise_and), 1),
+        "ij": ("v", ("ii",), lambda: V.tensor_scalar(T.ij[:], T.ii[:], 15, None, A.bitwise_and), 1),
+        "j": ("v", ("ja0", "ja1", "sp"), lambda: V.tensor_tensor(T.bb[:, UT + 8:UT + 16], T.ja[:], T.sp[:], A.mult), 1),
+        "mk": ("v", ("ij",), lambda: V.tensor_scalar(T.mk[:], T.ij[:], 0.0, None, A.is_equal), 1),
+        "nu": ("a", ("u",), lambda: S.activation(T.bb[:, UT + 4:UT + 8], T.bb[:, UT:UT + 4], AF.Copy, scale=-1.0), 1),
+        "tq": ("v", ("x",), qf(pair("tq", 0, 256), T.xt[:]), 1),
+        "uq": ("v", ("nu", "j", "id"), qf(pair("uq", 0, 128), T.bb[:, UT:UT + 512]), 1),
+        "tb": ("v", ("ii",), lambda: V.tensor_scalar(T.tb[:], T.ii[:], 128.0, -EPS, A.is_lt, A.mult), 1),
+        "cc": ("v", ("ii",), lambda: V.tensor_scalar(T.c2[:, 129:160:2], T.ii[:, 0:16], 128.5, 1024.0, A.subtract, A.mult), 1),
+        "cf0": ("v", ("i16", "j"), c2f(0), 1),
+        "cf1": ("v", ("i16", "j"), c2f(1), 1),
+        "unc": ("v", ("zo0", "zo1", "uq"), lambda: pick_c(*xu), 1),
+        "uns": ("a", ("zo0", "zo1", "uq"), lambda: pick_s(*xu), 1),
+        "kq": ("v", ("k0", "k1", "k2", "k3"), qf(pair("kq", 0, 128), T.kt[:]), 1),
+    }
+    for b in range(4):
+        CALLS["k%d" % b] = ("a", ("mk",), kf(b), 1)
+        CALLS["e%d" % b] = ("v", ("id",), qf(pair("eq", 128 * b, 128 * b + 128), T.bb[:, ZT + 4 - b:ZT + 516 - b]), 1)
+        CALLS["q%d" % b] = ("v", ("v%d" % (b // 2),), qf(pair("vq", 128 * b, 128 * b + 128), T.vt[:, 512 * b:512 * b + 512]), 1)
+
+    def c(name):
+        q, waits, call, k = CALLS[name]
+        wt(q, *[E[x] for x in waits])
+        E[name] = ev(call(), k)
+
+    def send_t0():
+        E["in", 1] = send_tile(pair("aw", 0, 256), pair("tq", 0, 256), [E["tq"]], [], "ra", "lt")
+
+    def send_u():
+        wt("g", E["uq"], *([] if E["in", 1] else []))
+        E["ru"] = send2(prv, [(u8(T.ul[:, 0:2]), u8(T.uq[:, 0:2])), (T.uls[:, 0:8], T.uqs[:, 0:8])], "ru", "lt")
+        E["lt"] = ("lt", nloc["lt"])
+
+    free, held, left = list(range(8)), {}, {b: [] for b in range(8)}
+
+    def take(name, reads):
+        b = free.pop(0)
+        wt("t", *left[b])
+        held[name] = [b, reads, []]
+
+    def bank(name, a=0, b=128):
+        i = held[name][0]
         return (T.pr, T.pm)[i // 4][:, 512 * (i % 4) + a:512 * (i % 4) + b]
 
-    RB, DB = (4, 6, 4, 3), (5, 7, 5, 2)
+    def read(name, e, n=1):
+        x = held[name]
+        x[1] -= n
+        x[2].append(e)
+        if x[1] == 0:
+            left[x[0]] = x[2]
+            free.append(x[0])
+        return e
 
-    def stop(w, arrived, fq, gb, sc, jk, sg, rl, nb, off, t, before):
-        old = pair(w, 0, 256)
+    ST = {1: ("aw", 0, T.r1, T.n1, T.o1, "t1"), 2: ("bw", 64, T.r2, T.n2, T.o2, "t2")}
+    RK = {1: ("un", "aw", T.g1, T.sc1, T.jk1, T.sg1, "f1"), 2: ("um", "t1", T.g2, T.sc2, T.jk2, T.sg2, "f2")}
+    BLK = ((0, 0), (0, 1), (1, 1), (1, 0))
 
-        def prods(i, *free):
-            wt("t", e_vq[i // 2], e_e, *free)
-            e_1 = ev(mm(bank(RB[i], 0, 256), pair("vq", 128 * i, 128 * i + 128), old))
-            e_2 = ev(mm(bank(DB[i], 0, 256), pair("eq", 128 * i, 128 * i + 128), old))
-            return e_1, e_2
+    def cols(h):
+        return (0, 256) if h is None else (128 * h, 128 * h + 128)
 
-        def relu(i, e, a=0, b=256):
-            wt("a", e[0])
-            return ev(S.activation(rl[:, 256 * i + a:256 * i + b], bank(RB[i], a, b), AF.Relu, scale=0.05))
+    def pv(s, i):
+        w, c0 = ST[s][:2]
+        wt("t", E["in", s], E["q%d" % i])
+        take(("v", s, i), 2)
+        E["v", s, i] = ev(mm(bank(("v", s, i), 0, 256), pair("vq", 128 * i, 128 * i + 128), pair(w, c0, c0 + 256)))
 
-        def add(i, e, e_r, a=0, b=256):
-            wt("v", e[1], e_r)
-            return ev(V.tensor_tensor(nb[:, 4 * a + i:4 * b:4], bank(DB[i], a, b), rl[:, 256 * i + a:256 * i + b], A.add))
+    def pe(s, i):
+        w, c0 = ST[s][:2]
+        wt("t", E["in", s], E["e%d" % i])
+        take(("e", s, i), 2)
+        E["e", s, i] = ev(mm(bank(("e", s, i), 0, 256), pair("eq", 128 * i, 128 * i + 128), pair(w, c0, c0 + 256)))
 
-        def block(i):
-            a, b = 128 * BLK[i][0], 128 * BLK[i][1]
-            mm(bank(i), pair("un", 0, 128), pair(w, b, b + 128), True, False)
-            return ev(mm(bank(i), pair(w, a, a + 128), pair("un", 128, 256), False, True))
+    def relu(s, i, h=None, q="a"):
+        a, b = cols(h)
+        wt(q, E["v", s, i])
+        out, in_ = ST[s][2][:, 256 * i + a:256 * i + b], bank(("v", s, i), a, b)
+        e = ev(S.activation(out, in_, AF.Relu, scale=0.05) if q == "a" else V.tensor_scalar(out, in_, 0.0, 0.05, A.max, A.mult))
+        read(("v", s, i), e, (b - a) // 128)
+        for k in range(a // 128, b // 128):
+            E["r", s, i, k] = e
 
-        def cmp_own(h):
-            wt("v", e_d[2 * h], e_tb)
-            return ev(V.tensor_tensor(gb[:, 128 * h:128 * h + 128], bank(2 * h), T.tb[:], A.is_gt))
+    def add(s, i, h=None):
+        a, b = cols(h)
+        wt("v", E["e", s, i], *[E["r", s, i, k] for k in range(a // 128, b // 128)])
+        e = ev(V.tensor_tensor(ST[s][3][:, 4 * a + i:4 * b:4], bank(("e", s, i), a, b), ST[s][2][:, 256 * i + a:256 * i + b], A.add))
+        read(("e", s, i), e, (b - a) // 128)
+        for k in range(a // 128, b // 128):
+            E["a", s, i, k] = e
 
-        def count_other(h):
-            wt("a", e_d[2 * h + 1])
-            return ev(S.activation(jk[:, 128 * h:128 * h + 128], bank(2 * h + 1), AF.Sign, bias=(EPS if h else -EPS),
-                                   accum_out=sg[:, h:h + 1]))
+    def pack(s, h=None):
+        a, b = cols(h)
+        w, c0 = ST[s][:2]
+        wt("v", *[E["a", s, i, k] for i in range(4) for k in range(a // 128, b // 128)])
+        e = quant(pair(w, c0 + 256 + a, c0 + 256 + b), ST[s][3][:, 4 * a:4 * b])
+        for k in range(a // 128, b // 128):
+            E["q", s, k] = e
 
-        def count_own(h, e):
-            wt("v", e, e_o[h])
-            s = slice(128 * h, 128 * h + 128)
-            return ev(V.tensor_tensor_scan(sc[:, s], gb[:, s], gb[:, s], sg[:, h:h + 1], A.add, A.add))
+    def pick(s, q, h=None):
+        a, b = cols(h)
+        w, c0 = ST[s][:2]
+        wt(q, E["off", s], *[E["q", s, k] for k in range(b // 128)])
+        e = ev((pick_c if q == "v" else pick_s)(pair(ST[s][5], a, b), pair(w, c0, c0 + 256 + b), ST[s][4][:, a // 16:b // 16]))
+        for k in range(a // 128, b // 128):
+            E[q, "t", s, k] = e
 
-        def steps(h, e, e_f):
-            wt("v", e, e_c2)
-            return ev(V.tensor_scalar(T.bb[:, h:320:2], T.c2[:, 160 * h:160 * h + 160], sc[:, 128 * h + 127:128 * h + 128],
-                                      None, A.is_gt), 1, e_f)
+    def tile(s, k):
+        return [E["in", 1]] if s == 1 else [E[q, "t", 1, k] for q in "va"]
 
-        wt("t", arrived, e_un, *before)
-        e_p = [prods(0)]
-        e_d = {i: block(i) for i in (1, 0, 3, 2)}
-        e_r = [relu(0, e_p[0])]
-        e_o = [count_other(h) for h in range(2)]
-        e_a = [add(0, e_p[0], e_r[0])]
-        e_g = [cmp_own(h) for h in range(2)]
-        e_p.append(prods(1))
-        e_p.append(prods(2, e_a[0]))
-        e_p.append(prods(3, e_g[1], e_o[1]))
-        e_r += [relu(1, e_p[1]), relu(2, e_p[2])]
-        e_r3 = [relu(3, e_p[3], 128 * h, 128 * h + 128) for h in range(2)]
-        e_s = [count_own(h, e_g[h]) for h in range(2)]
-        e_f = steps(1, e_s[1], steps(0, e_s[0], None))
-        e_a.append(add(1, e_p[1], e_r[1]))
-        wt("v", e_f)
-        e_f = quant(pair(fq, 0, 128), T.bb[:, 0:512])
-        wt("t", e_f, e_kq)
-        e_m = ev(mm(bank(0), pair("kq", 0, 128), pair(fq, 0, 128)))
-        e_l = ev(mm(bank(1), pair(fq, 0, 128), pair("uq", 0, 128)))
-        e_a.append(add(2, e_p[2], e_r[2]))
-        e_a3 = [add(3, e_p[3], e_r3[h], 128 * h, 128 * h + 128) for h in range(2)]
-        wt("v", e_m)
-        e_of = ev(V.tensor_scalar(off[:], bank(0, 64, 80), lo, None, A.add))
-        e_q = []
-        for h in range(2):
-            wt("v", e_a3[h], *e_a)
-            e_q.append(quant(pair(w, 256 + 128 * h, 384 + 128 * h), nb[:, 512 * h:512 * h + 512]))
-        e_c, e_n = [], []
-        for h in range(2):
-            wt("v", e_of, e_q[h])
-            wt("a", e_of, e_q[h])
-            a = (pair(t, 128 * h, 128 * h + 128), pair(w, 0, 384 + 128 * h), off[:, 8 * h:8 * h + 8])
-            e_c.append(ev(pick_c(*a)))
-            e_n.append(ev(pick_s(*a)))
-        return e_c, e_n, e_l, [e_of] + e_a + e_a3
+    def row(s, i):
+        un, w = RK[s][:2]
+        wt("t", *tile(s, BLK[i][1]), *([E["unc"], E["uns"]] if s == 1 else [E["um", "v", 0], E["um", "a", 0]]))
+        take(("d", s, i), 1)
+        b = 128 * BLK[i][1]
+        mm(bank(("d", s, i)), pair(un, 0, 128), pair(w, b, b + 128), True, False)
 
-    def places(e_l, out):
-        wt("v", e_l)
-        return ev(V.tensor_scalar(out[:], bank(1, 126, 127), bank(1, 127, 128), None, A.add))
+    def col(s, i):
+        un, w = RK[s][:2]
+        wt("t", *tile(s, BLK[i][0]), *([E["unc"], E["uns"]] if s == 1 else [E["um", "v", 1], E["um", "a", 1]]))
+        a = 128 * BLK[i][0]
+        E["d", s, i] = ev(mm(bank(("d", s, i)), pair(w, a, a + 128), pair(un, 128, 256), False, True))
 
-    e_c, e_n, e_l, fr = stop("aw", r_0, "f1", T.g1, T.sc1, T.jk1, T.sg1, T.r1, T.n1, T.o1, "t1", [])
-    wt("g", *e_c)
-    k = send(u8(T.bw[:, 0:256]), u8(T.t1[:]), "r1")
-    wt("g", *e_n)
-    k += send(T.bws[:, 0:256], T.t1s[:], "r1")
-    r_1 = ("r1", k)
-    e_l = places(e_l, T.p1)
-    wt("g", e_l)
-    r_l = ("rl", send(T.ll[:], T.p1[:], "rl"))
-    wt("v", e_w)
-    e_wq = quant(pair("wq", 0, 128), T.wt[:])
-    wt("s", r_l)
-    e_out = ev(Y.dma_start(T.li[0:1, :], T.ll[0:64, :]), 16)
+    def own(s, h):
+        wt("v", E["d", s, 2 * h], E["tb"])
+        E["g", s, h] = read(("d", s, 2 * h), ev(V.tensor_tensor(RK[s][2][:, 128 * h:128 * h + 128], bank(("d", s, 2 * h)),
+                                                                T.tb[:], A.is_gt)))
 
-    e_c, e_n, e_l, fr = stop("bw", r_1, "f2", T.g2, T.sc2, T.jk2, T.sg2, T.r2, T.n2, T.o2, "t2", fr + [e_l])
+    def other(s, h):
+        wt("a", E["d", s, 2 * h + 1])
+        E["o", s, h] = read(("d", s, 2 * h + 1), ev(S.activation(RK[s][4][:, 128 * h:128 * h + 128], bank(("d", s, 2 * h + 1)),
+                                                                 AF.Sign, bias=(EPS if h else -EPS),
+                                                                 accum_out=RK[s][5][:, h:h + 1])))
 
-    e_y = []
-    wt("t", e_wq)
-    for h in range(2):
-        wt("t", e_c[h], e_n[h])
-        e_y.append(ev(mm(bank(6 + h), pair("wq", 0, 128), pair("t2", 128 * h, 128 * h + 128))))
-    wt("s", *e_c)
-    ev(Y.dma_start(T.oc[:], u8(T.t2[:])), 16, e_out)
-    e_l = places(e_l, T.p2)
-    wt("a", e_y[0])
-    e_z0 = ev(S.activation(T.yt[:, 0:128], bank(6), AF.Copy))
-    wt("v", e_y[1])
-    e_z1 = ev(V.tensor_copy(T.yt[:, 128:256], bank(7)))
-    wt("s", *e_n)
-    for q in range(4):
-        ev(Y.dma_start(T.osc[4 * q:4 * q + 4, :], T.t2s[32 * q:32 * q + 4, :]), 16, e_out)
-    wt("a", e_z0, e_z1)
-    ev(S.dma_start(T.y[:], T.yt[:]), 16, e_out)
-    wt("s", e_l)
-    ev(Y.dma_start(T.li[1:2, :], T.p2[0:64, :]), 16, e_out)
+    def count(s, h):
+        wt("v", E["g", s, h], E["o", s, h])
+        gb, x = RK[s][2], slice(128 * h, 128 * h + 128)
+        E["s", s, h] = ev(V.tensor_tensor_scan(RK[s][3][:, x], gb[:, x], gb[:, x], RK[s][5][:, h:h + 1], A.add, A.add))
+
+    def steps(s, h):
+        wt("v", E["s", s, h], E["cl%d" % h], E["cf%d" % h], E["cm" if h else "cc"], *([E["f", 1]] if s == 2 else []))
+        E["x", s, h] = ev(V.tensor_scalar(T.bb[:, h:320:2], T.c2[:, 160 * h:160 * h + 160],
+                                          RK[s][3][:, 128 * h + 127:128 * h + 128], None, A.is_gt))
+
+    def flags(s):
+        wt("v", E["x", s, 0], E["x", s, 1], E["uq"])
+        E["f", s] = quant(pair(RK[s][6], 0, 128), T.bb[:, 0:512])
+
+    def lists(s):
+        wt("t", E["f", s], E["uq"])
+        take(("l", s), 1)
+        E["l", s] = ev(mm(bank(("l", s)), pair(RK[s][6], 0, 128), pair("uq", 0, 128)))
+
+    def places(s):
+        wt("a", E["l", s])
+        E["p", s] = read(("l", s), ev(S.activation(T.pj[:, 2 * s - 2:2 * s], bank(("l", s), 2, 4), AF.Copy,
+                                                   accum_out=T.pp[:, s - 1:s])))
+
+    def turn(s):
+        wt("t", E["kq"], E["f", 1] if s == 1 else E["rf"])
+        take(("k", s), 1)
+        E["k", s] = ev(mm(bank(("k", s)), pair("kq", 0, 128), pair("f1", 0, 128) if s == 1 else pair("bw", 48, 176)))
+
+    def offsets(s):
+        wt("v", E["k", s], E["j"])
+        a = 64 if s == 1 else 0
+        E["off", s] = read(("k", s), ev(V.tensor_scalar(ST[s][4][:], bank(("k", s), a, a + 16), lo, None, A.add)))
+
+    def spread(q, h=None):
+        a, b = cols(h)
+        wt(q, E["ru"], E["zo0"], E["zo1"])
+        e = ev((pick_c if q == "v" else pick_s)(pair("um", a, b), pair("ul", 0, 2), T.zo[:, a // 16:b // 16]))
+        for k in range(a // 128, b // 128):
+            E["um", q, k] = e
+
+    def send_t1():
+        E["in", 2] = send_tile(pair("bw", 64, 320), pair("t1", 0, 256), [E["v", "t", 1, k] for k in range(2)],
+                               [E["a", "t", 1, k] for k in range(2)], "rb")
+
+    def send_flags():
+        wt("g", E["f", 2])
+        E["rf"] = send2(nxt, [(u8(T.bw[:, 48:64]), u8(T.f2[:, 64:80])), (T.bws[:, 0:64], T.f2s[:, 16:80])], "rf")
+
+    def send_lists():
+        wt("g", E["p", 1], E["p", 2])
+        E["rl"] = ("rl", send(T.ll[:], T.pp[:], "rl"))
+
+    def quant_w():
+        wt("v", E["w"])
+        E["wq"] = quant(pair("wq", 0, 128), T.wt[:])
+
+    def y_mm(h=None):
+        a, b = cols(h)
+        wt("t", E["wq"], *[E[q, "t", 2, k] for q in "va" for k in range(a // 128, b // 128)])
+        take(("y", h), 1)
+        E["y", h] = ev(mm(bank(("y", h), 0, b - a), pair("wq", 0, 128), pair("t2", a, b)))
+
+    def y_copy(q, h=None):
+        a, b = cols(h)
+        wt(q, E["y", h])
+        out, in_ = T.yt[:, a:b], bank(("y", h), 0, b - a)
+        e = read(("y", h), ev(V.tensor_copy(out, in_) if q == "v" else S.activation(out, in_, AF.Copy)))
+        for k in range(a // 128, b // 128):
+            E["z", k] = e
+
+    def store(q, out, in_, *es):
+        wt(q, *es)
+        E["out"] = ev(Q[q].dma_start(out, in_), 16, E.get("out"))
+
+    def store_li(q, h):
+        store(q, T.li[h:h + 1, :], T.ll[0:64, h:h + 1], E["rl"])
+
+    def store_oc(q):
+        store(q, T.oc[:], u8(T.t2[:]), E["v", "t", 2, 0], E["v", "t", 2, 1])
+
+    def store_osc(q, k):
+        store(q, T.osc[4 * k:4 * k + 4, :], T.t2s[32 * k:32 * k + 4, :], E["a", "t", 2, 0], E["a", "t", 2, 1])
+
+    def store_y(q):
+        store(q, T.y[:], T.yt[:], E["z", 0], E["z", 1])
+
+    c("z");c("ii");c("x");c("id");c("u");c("zo0");c("v0");c("zo1");c("cm");c("jj");c("nu");c("e0");c("ja0");c("v1")
+    c("tq");c("ja1");c("ij");c("i16");c("e3");c("mk");c("sp");c("j");c("e1");c("uq");send_t0();send_u();c("q2")
+    c("k0");c("cf0");c("cl0");c("e2");c("cl1");c("unc");c("q1");c("uns");c("w");row(1,3);c("q0");c("k2");row(1,0)
+    pv(1,0);c("k3");c("tb");c("k1");col(1,0);c("kq");c("cc");col(1,3);row(1,2);col(1,2);row(1,1);col(1,1);pe(1,0)
+    pv(1,1);spread("v",0);own(1,0);pe(1,1);relu(1,0);c("q3");other(1,1);pv(1,2);own(1,1);pv(1,3);c("cf1");pe(1,2)
+    other(1,0);add(1,0,0);pe(1,3);count(1,0);count(1,1);add(1,0,1);relu(1,1,0);relu(1,1,1);relu(1,2,0);steps(1,0)
+    steps(1,1);relu(1,2,1);add(1,1,1);add(1,1,0);flags(1);relu(1,3,0);turn(1);add(1,2,0);relu(1,3,1);add(1,3,0)
+    add(1,2,1);add(1,3,1);pack(1,0);offsets(1);pack(1,1);spread("a",1);spread("a",0);pick(1,"v",0);pick(1,"v",1)
+    lists(1);pick(1,"a",0);spread("v",1);pick(1,"a",1);row(2,2);places(1);row(2,3);row(2,1);quant_w();col(2,2)
+    own(2,1);row(2,0);col(2,3);other(2,1);col(2,1);col(2,0);send_t1();pv(2,0);own(2,0);count(2,1);pv(2,2);other(2,0)
+    pv(2,1);count(2,0);pv(2,3);steps(2,1);relu(2,0);pe(2,0);steps(2,0);flags(2);send_flags();pe(2,1);relu(2,1)
+    lists(2);add(2,0);pe(2,2);relu(2,2);add(2,1);pe(2,3);relu(2,3,0);places(2);send_lists();add(2,2,0);add(2,3,0)
+    add(2,2,1);relu(2,3,1);store_li("s",0);add(2,3,1);turn(2);pack(2,0);offsets(2);pack(2,1);pick(2,"a",0)
+    pick(2,"v",0);store_li("s",1);pick(2,"v",1);y_mm(0);pick(2,"a",1);y_mm(1);y_copy("v",1);store_osc("a",1)
+    store_osc("a",0);y_copy("a",0);store_oc("s");store_osc("s",2);store_y("a");store_osc("s",3)
 
     done = {e for (_, e) in known}
-    wt("s", *[e for e in made if e[0] not in done])
-    g.wait_ge(T.sem.lo, nloc[0])
+    wt("s", *[e for e in made if e[0] not in done and e is not E["out"]])
+    wt("s", E["out"])
+    g.wait_ge(T.sem.lo, nloc["lo"])

@@ -5,6 +5,7 @@ A = AluOpType
 AF = ActivationFunctionType
 F8, U8, BF, F32, I32, U16 = "float8_e4m3fn_x4", "uint8", "bfloat16", "float32", "int32", "uint16"
 EPS = 2.0 ** -110
+TIE = 2.0 ** -100
 UT, ZT, BB = 320, 336, 856
 
 SCRATCH = {}
@@ -15,21 +16,27 @@ def _pair(n, w):
     SCRATCH[n + "s"] = ("sbuf", [128, w], U8)
 
 
-for _n, _w in (("uq", 128), ("un", 256), ("ul", 8), ("um", 256), ("vq", 512), ("wq", 128), ("eq", 512), ("kq", 128),
-               ("tq", 256), ("aw", 512), ("bw", 576), ("f1", 128), ("f2", 128), ("t1", 256), ("t2", 256)):
+for _n, _w in (("un", 258), ("uq", 128), ("ul", 8), ("um", 256), ("vq", 512), ("wq", 128), ("eq", 512), ("kq", 128), ("tq", 384),
+               ("aw", 512), ("bw", 576), ("ff", 192), ("t1", 256), ("t2", 256)):
     _pair(_n, _w)
-for _n, _w, _d in (("xt", 1024, BF), ("bb", BB, BF), ("vt", 2048, BF), ("wt", 512, BF), ("kt", 512, BF), ("n1", 1024, BF),
-                   ("n2", 1024, BF), ("tb", 128, BF), ("mk", 128, BF), ("c2", 320, BF), ("g1", 256, BF), ("g2", 256, BF),
-                   ("sc1", 256, BF), ("sc2", 256, BF), ("jk1", 256, BF), ("jk2", 256, BF), ("sg1", 2, F32), ("sg2", 2, F32),
-                   ("r1", 1024, F32), ("r2", 1024, F32), ("ii", 128, I32), ("ij", 128, I32), ("jj", 8, I32), ("ja", 8, I32),
-                   ("sp", 8, F32), ("i16", 24, F32), ("zo", 16, U16), ("o1", 16, U16), ("o2", 16, U16), ("pp", 2, F32),
-                   ("ll", 2, F32), ("pj", 4, F32), ("yt", 256, F32)):
+for _n, _w, _d in (("xt", 1024, BF), ("bb", BB, BF), ("ut", 1032, BF), ("vt", 2048, BF), ("wt", 512, BF),
+                   ("kt", 512, BF), ("n1", 1024, BF), ("n2", 1024, BF), ("tb", 128, BF), ("mk", 128, BF), ("c2", 320, BF),
+                   ("c3", 320, BF), ("tt", 512, BF),
+                   ("g1", 256, BF), ("g2", 256, BF), ("sc1", 256, F32), ("sc2", 256, F32), ("sb1", 256, BF), ("sb2", 256, BF),
+                   ("jk1", 256, BF), ("jk2", 256, BF),
+                   ("sg1", 2, F32), ("sg2", 2, F32), ("r1", 1024, F32), ("r2", 1024, F32), ("ii", 128, I32), ("ij", 128, I32),
+                   ("jj", 8, I32), ("ja", 8, I32), ("sp", 8, F32), ("i16", 24, F32), ("zo", 16, U16), ("o1", 16, U16),
+                   ("o2", 16, U16), ("pp", 1, F32), ("ll", 1, F32), ("pj", 2, F32), ("pk", 2, F32), ("yt", 256, F32), ("yw", 512, F32)):
     SCRATCH[_n] = ("sbuf", [128, _w], _d)
 for _n, _w in (("pr", 2048), ("pm", 2048)):
     SCRATCH[_n] = ("psum", [128, _w], F32)
 
-NEV = 143
-SEMAPHORES = ["s%d" % _i for _i in range(NEV)] + ["lo", "lt", "ru", "ra", "rb", "rf", "rl"]
+NEV = 141
+SEMAPHORES = ["s%d" % _i for _i in range(NEV)] + ["lo", "lt", "ru", "in10", "in11", "in20", "in21", "rf", "rl"]
+
+START = 'x z jj tq id e u vb ja ii ij nu q3 sc1 j tb mk rep un ss1 va cl0 col100 row100 col111 k row111 sendu zo row110 q1 col110 q0 col101 cl1 row101 v10 q2 cf kq e10 own10 v12 oth11 oth10 own11 cnt10 cnt11 r100 v11 spreadv step11 step10 v130 r101 e12 a10 flags1 r120 r121 e130 v131 e11 turn1 r130 r11 a12 a130 e131 a11 r131 off1 a131 spreada pack10 pack11 pc10 ps10 pc11 sc20 col200 row200 own20 row210 ps11 col211 row201 row211 w ss2 col201 col210 sc21 v200 own21 cna20 v220 wq cnt21 v201 oth20 step20 v21 oth21 e20 step21 r200 flags2 rv201 v221 rv211 rv210 list sendflags e21 v230 r220 e22 r221 place a200 a201 v231 e23 a210 a211 a22 r230 turn2 a230 r231 a231 sendlist pack20 off2 ps20 pack21 ps21 pc20 osca2 ym0 osca1 li pc21 oc yv0 osc0 ym1 yv1 y osca3'.split()
+START = 'x u va vb ii z ij mk jj nu tq ja tb id rep sc1 ss1 zo cl0 j e cf q0 un q1 k q3 cl1 kq q2 sendu w col100 row100 row111 col111 col101 own10 col110 row101 row110 oth10 own11 v10 v12 e10 oth11 cnt10 r100 cnt11 r101 v11 e12 v13 spreadv step11 step10 r12 a10 r11 e11 r13 flags1 e130 e131 spreada turn1 a12 a11 a130 a131 off1 pack10 pack11 pc10 ps10 sc20 pc11 col200 ps11 wq row200 own20 ss2 row210 col211 row211 row201 col201 own21 col210 sc21 v200 v230 v201 cnt20 v21 oth20 cnt21 oth21 e20 r200 r201 step20 r21 step21 v22 flags2 e21 r220 e22 a20 a210 a211 v231 a220 r230 e230 e231 yy01 r221 a230 r231 sendflagsb a221 list a231 place turn2 sendlist pack20 pack21 yy00 off2 pc2 li yy10 ywa01 ywa00 ywa10 yy11 ywa11 pw2 oc ypa0 ypa1 y osc2 osc0 osca1 osca3'.split()
+STOP1, AHEAD, STOP2 = [], [], []
 
 
 def rank_program(g, core, T, topo):
@@ -40,6 +47,8 @@ def rank_program(g, core, T, topo):
     Q = {"g": g, "v": g.vector, "a": g.scalar, "s": g.sync, "t": g.tensor}
     V, S, P, Y = g.vector, g.scalar, g.tensor, g.sync
     made, known, nloc, E = [], {}, {"lo": 0, "lt": 0}, {}
+    ORDER = START + STOP1 + AHEAD + STOP2
+    local = int("list1" in ORDER)
 
     def ev(ins, k=1, e=None):
         if e is None:
@@ -82,296 +91,417 @@ def rank_program(g, core, T, topo):
     def pair(name, a, b):
         return T[name][:, a:b], T[name + "s"][:, a:b]
 
+    def cols(h):
+        return (0, 256) if h is None else (128 * h, 128 * h + 128)
+
+    def halves(h):
+        return (0, 1) if h is None else (h,)
+
     def quant(dst, src):
-        return ev(V.quantize_mx(dst[0], dst[1], src))
+        return V.quantize_mx(dst[0], dst[1], src)
 
     def mm(out, lhs, rhs, start=True, stop=True):
         return P.matmul_mx(out, lhs[0], lhs[1], rhs[0], rhs[1], start, stop)
 
-    def pick_c(dst, win, off):
-        return V.tensor_copy(u32(dst[0]), u32(win[0]).indirect(off))
+    picked = []
 
-    def pick_s(dst, win, off):
+    def gather(q, dst, win, off, key):
+        picked.append(key)
+        if q == "v":
+            return V.tensor_copy(u32(dst[0]), u32(win[0]).indirect(off))
+        if q == "w":
+            return V.tensor_copy(dst[1], win[1].indirect(off))
         return S.activation(dst[1], win[1].indirect(off), AF.Copy)
 
     def iota(out, pattern, base, cm=0):
         return g.iota(out, pattern, base, cm, allow_small_or_imprecise_dtypes=True)
 
-    def send_tile(dst, src, e_c, e_s, sem, loc="lo"):
-        wt("g", *e_c)
-        k = send(u8(dst[0]), u8(src[0]), sem, loc)
-        wt("g", *e_s)
-        return (sem, k + send(dst[1], src[1], sem, loc))
-
-    hi, lo = T.bb[:, UT + 8:UT + 9], T.bb[:, UT + 12:UT + 13]
+    hi, lo = T.ut[:, 0:1], T.ut[:, 4:5]
     ident = T.bb[:, ZT + 4:ZT + 516:4]
+    zeros = T.bb[:, ZT + 1:ZT + 513:4]
 
-    def c2f(h):
-        return lambda: V.tensor_scalar(T.c2[:, 160 * h + 128:160 * h + 160:2], T.i16[:, 8 - 8 * h:24 - 8 * h], hi, -256.0,
-                                       A.not_equal, A.mult)
+    def cf():
+        return ([V.tensor_scalar(T.c2[:, 160 * h + 128:160 * h + 160:2], T.i16[:, 8 - 8 * h:24 - 8 * h], hi, -256.0,
+                                 A.not_equal, A.mult) for h in (0, 1)] +
+                [V.tensor_scalar(T.c2[:, 129:160:2], T.ii[:, 0:16], 128.5, 1024.0, A.subtract, A.mult),
+                 V.memset(T.c2[:, 289:320:2], -256.0)])
 
-    def kf(t):
-        if t < 2:
-            return lambda: S.activation(T.kt[:, t:512:4], T.mk[:], AF.Copy, scale=256.0)
-        return lambda: S.activation(T.kt[:, t:512:4], T.mk[:], AF.Identity, bias=16.0, scale=0.0)
+    def kf():
+        return ([S.activation(T.kt[:, t:512:4], T.mk[:], AF.Copy, scale=256.0) for t in (0, 1)] +
+                [S.activation(T.kt[:, t:512:4], T.mk[:], AF.Identity, bias=16.0, scale=0.0) for t in (2, 3)])
+
+    def rep():
+        return [S.activation(T.ut[:, 8 + 512 * (t // 4) + t % 4:520 + 512 * (t // 4):4], zeros, AF.Identity,
+                             bias=T.bb[:, UT + t:UT + t + 1]) for t in range(8)]
+
+    CALLS = {
+        "x": ("s", (), lambda: [Y.dma_start(T.xt[:], T.x[:])], 16),
+        "x0": ("s", (), lambda: [Y.dma_start(T.xt[:, 0:512], T.x[:, 0:512])], 16),
+        "x1": ("s", (), lambda: [Y.dma_start(T.xt[:, 512:1024], T.x[:, 512:1024])], 16),
+        "u": ("s", (), lambda: [Y.dma_start(T.bb[:, UT:UT + 4], T.u[:, 0:4])], 16),
+        "ua": ("a", (), lambda: [S.dma_start(T.bb[:, UT:UT + 4], T.u[:, 0:4])], 16),
+        "v": ("s", (), lambda: [Y.dma_start(T.vt[:], T.v[:])], 16),
+        "va": ("s", (), lambda: [Y.dma_start(T.vt[:, 0:1024], T.v[:, 0:1024])], 16),
+        "vb": ("s", (), lambda: [Y.dma_start(T.vt[:, 1024:2048], T.v[:, 1024:2048])], 16),
+        "w": ("s", ("lt",), lambda: [Y.dma_start(T.wt[:], T.w[:])], 16),
+        "jj": ("g", (), lambda: [g.iota(T.jj[:], [[0, 4], [128, 2]], 0, 1), iota(T.sp[:], [[0, 2], [-2, 2], [0, 2]], 1),
+                                 iota(T.i16[:], [[16, 24]], -128)], 1),
+        "ii": ("g", (), lambda: [g.iota(T.ii[:], [[1, 128]], 128, -1)], 1),
+        "cl0": ("g", (), lambda: [iota(T.c2[:, 0:128], [[2, 64], [-2, 2]], -127)], 1),
+        "cl1": ("a", ("cl0",), lambda: [S.activation(T.c2[:, 160:288], T.c2[:, 0:128], AF.Copy)], 1),
+        "id": ("g", ("z",), lambda: [g.affine_select(ident, ident, [[1, 128]], A.not_equal, 1.0, 0, -1)], 1),
+        "z": ("v", (), lambda: [V.memset(T.bb[:, UT + 8:BB], 0.0)], 1),
+        "zo": ("v", (), lambda: [V.memset(T.zo[:, 0:8], 0), V.memset(T.zo[:, 8:16], 1)], 1),
+        "ja": ("v", ("jj",), lambda: [V.tensor_scalar(T.ja[:, 0:4], T.jj[:, 0:4], 240, None, A.bitwise_and),
+                                      V.tensor_scalar(T.ja[:, 4:8], T.jj[:, 4:8], 15, None, A.bitwise_and)], 1),
+        "ij": ("v", ("ii",), lambda: [V.tensor_scalar(T.ij[:], T.ii[:], 15, None, A.bitwise_and)], 1),
+        "j": ("v", ("ja",), lambda: [V.tensor_tensor(T.ut[:, 0:8], T.ja[:], T.sp[:], A.mult)], 1),
+        "mk": ("v", ("ij",), lambda: [V.tensor_scalar(T.mk[:], T.ij[:], 0.0, None, A.is_equal)], 1),
+        "nu": ("a", ("u",), lambda: [S.activation(T.bb[:, UT + 4:UT + 8], T.bb[:, UT:UT + 4], AF.Copy, scale=-1.0)], 1),
+        "rep": ("a", ("nu", "id"), rep, 1),
+        "tq": ("v", ("x",), lambda: [quant(pair("tq", 128, 384), T.xt[:])], 1),
+        "tq0": ("v", ("x0",), lambda: [quant(pair("tq", 128, 256), T.xt[:, 0:512])], 1),
+        "tq1": ("v", ("x1",), lambda: [quant(pair("tq", 256, 384), T.xt[:, 512:1024])], 1),
+        "t0": ("v", (), lambda: [V.memset(T.tt[:], 0.0)], 1),
+        "t1": ("v", ("t0", "ii"), lambda: [V.tensor_scalar(T.tt[:, 0:512:4], T.ii[:], 127.5, -TIE, A.subtract, A.mult)], 1),
+        "tz": ("v", ("t1",), lambda: [quant(pair("tq", 0, 128), T.tt[:])], 1),
+        "c3": ("a", ("cl1", "cf"), lambda: [S.activation(T.c3[:], T.c2[:], AF.Identity, bias=-128.0)], 1),
+        "uq": ("v", ("nu", "id"), lambda: [quant(pair("uq", 0, 128), T.bb[:, UT:UT + 512])], 1),
+        "un": ("v", ("rep", "j"), lambda: [quant(pair("un", 0, 258), T.ut[:])], 1),
+        "tb": ("v", ("ii",), lambda: [V.tensor_scalar(T.tb[:], T.ii[:], 128.0, -EPS, A.is_lt, A.mult)], 1),
+        "cf": ("v", ("ii", "j"), cf, 1),
+        "e": ("v", ("id",), lambda: [quant(pair("eq", 128 * b, 128 * b + 128), T.bb[:, ZT + 4 - b:ZT + 516 - b]) for b in range(4)], 1),
+        "k": ("a", ("mk",), kf, 1),
+        "kq": ("v", ("k",), lambda: [quant(pair("kq", 0, 128), T.kt[:])], 1),
+        "wq": ("v", ("w",), lambda: [quant(pair("wq", 0, 128), T.wt[:])], 1),
+    }
+    ALSO = {"x": ("x0", "x1"), "tq": ("tq0", "tq1"), "v": ("va", "vb"), "ua": ("u",)}
 
     def qf(dst, src):
-        return lambda: V.quantize_mx(dst[0], dst[1], src)
+        return lambda: [quant(dst, src)]
 
-    xu = (pair("un", 0, 256), pair("uq", 0, 2), T.zo[:])
-    CALLS = {
-        "x": ("s", (), lambda: Y.dma_start(T.xt[:], T.x[:]), 16),
-        "u": ("s", (), lambda: Y.dma_start(T.bb[:, UT:UT + 4], T.u[:, 0:4]), 16),
-        "v0": ("s", (), lambda: Y.dma_start(T.vt[:, 0:1024], T.v[:, 0:1024]), 16),
-        "v1": ("s", (), lambda: Y.dma_start(T.vt[:, 1024:2048], T.v[:, 1024:2048]), 16),
-        "w": ("s", ("lt",), lambda: Y.dma_start(T.wt[:], T.w[:]), 16),
-        "jj": ("g", (), lambda: g.iota(T.jj[:], [[0, 4], [128, 2]], 0, 1), 1),
-        "sp": ("g", (), lambda: iota(T.sp[:], [[0, 2], [-2, 2], [0, 2]], 1), 1),
-        "ii": ("g", (), lambda: g.iota(T.ii[:], [[1, 128]], 128, -1), 1),
-        "i16": ("g", (), lambda: iota(T.i16[:], [[16, 24]], -128), 1),
-        "cl0": ("g", (), lambda: iota(T.c2[:, 0:128], [[2, 64], [-2, 2]], -127), 1),
-        "cl1": ("g", (), lambda: iota(T.c2[:, 160:288], [[2, 64], [-2, 2]], -127), 1),
-        "id": ("g", ("z",), lambda: g.affine_select(ident, ident, [[1, 128]], A.not_equal, 1.0, 0, -1), 1),
-        "z": ("v", (), lambda: V.memset(T.bb[:, ZT:BB], 0.0), 1),
-        "zo0": ("v", (), lambda: V.memset(T.zo[:, 0:8], 0), 1),
-        "zo1": ("v", (), lambda: V.memset(T.zo[:, 8:16], 1), 1),
-        "cm": ("v", (), lambda: V.memset(T.c2[:, 289:320:2], -256.0), 1),
-        "ja0": ("v", ("jj",), lambda: V.tensor_scalar(T.ja[:, 0:4], T.jj[:, 0:4], 240, None, A.bitwise_and), 1),
-        "ja1": ("v", ("jj",), lambda: V.tensor_scalar(T.ja[:, 4:8], T.jj[:, 4:8], 15, None, A.bitwise_and), 1),
-        "ij": ("v", ("ii",), lambda: V.tensor_scalar(T.ij[:], T.ii[:], 15, None, A.bitwise_and), 1),
-        "j": ("v", ("ja0", "ja1", "sp"), lambda: V.tensor_tensor(T.bb[:, UT + 8:UT + 16], T.ja[:], T.sp[:], A.mult), 1),
-        "mk": ("v", ("ij",), lambda: V.tensor_scalar(T.mk[:], T.ij[:], 0.0, None, A.is_equal), 1),
-        "nu": ("a", ("u",), lambda: S.activation(T.bb[:, UT + 4:UT + 8], T.bb[:, UT:UT + 4], AF.Copy, scale=-1.0), 1),
-        "tq": ("v", ("x",), qf(pair("tq", 0, 256), T.xt[:]), 1),
-        "uq": ("v", ("nu", "j", "id"), qf(pair("uq", 0, 128), T.bb[:, UT:UT + 512]), 1),
-        "tb": ("v", ("ii",), lambda: V.tensor_scalar(T.tb[:], T.ii[:], 128.0, -EPS, A.is_lt, A.mult), 1),
-        "cc": ("v", ("ii",), lambda: V.tensor_scalar(T.c2[:, 129:160:2], T.ii[:, 0:16], 128.5, 1024.0, A.subtract, A.mult), 1),
-        "cf0": ("v", ("i16", "j"), c2f(0), 1),
-        "cf1": ("v", ("i16", "j"), c2f(1), 1),
-        "unc": ("v", ("zo0", "zo1", "uq"), lambda: pick_c(*xu), 1),
-        "uns": ("a", ("zo0", "zo1", "uq"), lambda: pick_s(*xu), 1),
-        "kq": ("v", ("k0", "k1", "k2", "k3"), qf(pair("kq", 0, 128), T.kt[:]), 1),
-    }
     for b in range(4):
-        CALLS["k%d" % b] = ("a", ("mk",), kf(b), 1)
-        CALLS["e%d" % b] = ("v", ("id",), qf(pair("eq", 128 * b, 128 * b + 128), T.bb[:, ZT + 4 - b:ZT + 516 - b]), 1)
-        CALLS["q%d" % b] = ("v", ("v%d" % (b // 2),), qf(pair("vq", 128 * b, 128 * b + 128), T.vt[:, 512 * b:512 * b + 512]), 1)
+        CALLS["q%d" % b] = ("v", ("v" + "ab"[b // 2],), qf(pair("vq", 128 * b, 128 * b + 128), T.vt[:, 512 * b:512 * b + 512]), 1)
 
-    def c(name):
-        q, waits, call, k = CALLS[name]
+    def const(name):
+        q, waits, calls, k = CALLS[name]
+        if name == "w":
+            assert landed(1) and (local or E["ru"])
+            E["lt"] = ("lt", nloc["lt"])
         wt(q, *[E[x] for x in waits])
-        E[name] = ev(call(), k)
+        for ins in calls():
+            E[name] = ev(ins, k, E.get(name))
+        for x in ALSO.get(name, ()):
+            E[x] = E[name]
 
-    def send_t0():
-        E["in", 1] = send_tile(pair("aw", 0, 256), pair("tq", 0, 256), [E["tq"]], [], "ra", "lt")
+    ST = {1: ("aw", 0, T.r1, T.n1, T.o1, "t1"), 2: ("bw", 64, T.r2, T.n2, T.o2, "t2")}
+    RK = {1: (pair("un", 2, 130), pair("un", 130, 258), "aw", T.g1, T.sc1, T.jk1, T.sg1, T.sb1),
+          2: (pair("um", 0, 128), pair("um", 128, 256), "t1", T.g2, T.sc2, T.jk2, T.sg2, T.sb2)}
+    if local:
+        RK[2] = RK[1][:2] + RK[2][2:]
 
-    def send_u():
-        wt("g", E["uq"], *([] if E["in", 1] else []))
-        E["ru"] = send2(prv, [(u8(T.ul[:, 0:2]), u8(T.uq[:, 0:2])), (T.uls[:, 0:8], T.uqs[:, 0:8])], "ru", "lt")
-        E["lt"] = ("lt", nloc["lt"])
+    pieces = {}
+
+    def hand_on(k):
+        def f(s, h=None):
+            (a, b), (w, c0) = cols(h), ST[s][:2]
+            wt("g", *[E["tq%d" % x] if s == 1 else E["va"[k], "t", 1, x] for x in halves(h)])
+            dst, src = pair(w, c0 + a, c0 + b)[k], (pair("tq", 128 + a, 128 + b) if s == 1 else pair("t1", a, b))[k]
+            sem = "in%d%d" % (s, halves(h)[0])
+            assert not [1 for key in known if key[1] == sem]
+            e = E.setdefault(sem, [sem, 0])
+            e[1] += send(dst, src, sem, "lt" if s == 1 else "lo") if k else send(u8(dst), u8(src), sem, "lt" if s == 1 else "lo")
+            for x in halves(h):
+                pieces[s, k, x] = e
+        return f
+
+    def landed(s, h=None):
+        return [pieces[s, k, x] for k in (0, 1) for x in halves(h)]
+
+    def send_u(name, a):
+        def f():
+            wt("g", E[name])
+            E["ru"] = send2(prv, [(u8(T.ul[:, 0:2]), u8(T[name][:, a:a + 2])), (T.uls[:, 0:8], T[name + "s"][:, a:a + 8])], "ru", "lt")
+        return f
 
     free, held, left = list(range(8)), {}, {b: [] for b in range(8)}
 
-    def take(name, reads):
+    def take(name, parts=1):
         b = free.pop(0)
         wt("t", *left[b])
-        held[name] = [b, reads, []]
+        held[name] = [b, parts, []]
 
-    def bank(name, a=0, b=128):
+    def bank(name, a=0, b=128, rows=slice(0, 128)):
         i = held[name][0]
-        return (T.pr, T.pm)[i // 4][:, 512 * (i % 4) + a:512 * (i % 4) + b]
+        return (T.pr, T.pm)[i // 4][rows, 512 * (i % 4) + a:512 * (i % 4) + b]
 
-    def read(name, e, n=1):
-        x = held[name]
-        x[1] -= n
+    def read(name, ins, parts=1):
+        x, e = held[name], ev(ins)
+        x[1] -= parts
         x[2].append(e)
         if x[1] == 0:
             left[x[0]] = x[2]
             free.append(x[0])
         return e
 
-    ST = {1: ("aw", 0, T.r1, T.n1, T.o1, "t1"), 2: ("bw", 64, T.r2, T.n2, T.o2, "t2")}
-    RK = {1: ("un", "aw", T.g1, T.sc1, T.jk1, T.sg1, "f1"), 2: ("um", "t1", T.g2, T.sc2, T.jk2, T.sg2, "f2")}
-    BLK = ((0, 0), (0, 1), (1, 1), (1, 0))
+    where = {}
 
-    def cols(h):
-        return (0, 256) if h is None else (128 * h, 128 * h + 128)
+    def product(key, waits, lhs, rhs, h):
+        wt("t", *waits)
+        take(key + (h,), len(halves(h)))
+        e = ev(mm(bank(key + (h,), 0, 128 * len(halves(h))), lhs, rhs))
+        for k in halves(h):
+            E[key + (k,)], where[key + (k,)] = e, (key + (h,), 128 * k - cols(h)[0])
 
-    def pv(s, i):
-        w, c0 = ST[s][:2]
-        wt("t", E["in", s], E["q%d" % i])
-        take(("v", s, i), 2)
-        E["v", s, i] = ev(mm(bank(("v", s, i), 0, 256), pair("vq", 128 * i, 128 * i + 128), pair(w, c0, c0 + 256)))
+    def behind(q, key, h, call):
+        name, a = where[key + halves(h)[:1]]
+        assert name == where[key + halves(h)[-1:]][0]
+        other = [e for e in held[name][2]]
+        wt(q, E[key + halves(h)[:1]], *[e for e in other if reader[e[0]] != q])
+        e = read(name, call(bank(name, a, a + 128 * len(halves(h)))), len(halves(h)))
+        reader[e[0]] = q
+        return e
 
-    def pe(s, i):
-        w, c0 = ST[s][:2]
-        wt("t", E["in", s], E["e%d" % i])
-        take(("e", s, i), 2)
-        E["e", s, i] = ev(mm(bank(("e", s, i), 0, 256), pair("eq", 128 * i, 128 * i + 128), pair(w, c0, c0 + 256)))
+    reader = {}
 
-    def relu(s, i, h=None, q="a"):
-        a, b = cols(h)
-        wt(q, E["v", s, i])
-        out, in_ = ST[s][2][:, 256 * i + a:256 * i + b], bank(("v", s, i), a, b)
-        e = ev(S.activation(out, in_, AF.Relu, scale=0.05) if q == "a" else V.tensor_scalar(out, in_, 0.0, 0.05, A.max, A.mult))
-        read(("v", s, i), e, (b - a) // 128)
-        for k in range(a // 128, b // 128):
-            E["r", s, i, k] = e
+    def prod(kind, name):
+        def f(s, i, h=None):
+            (a, b), (w, c0) = cols(h), ST[s][:2]
+            product((kind, s, i), landed(s, h) + [E["q%d" % i if kind == "v" else "e"]], pair(name, 128 * i, 128 * i + 128),
+                    pair(w, c0 + a, c0 + b), h)
+        return f
+
+    def part(s, i, h):
+        return ST[s][2][:, 256 * i + cols(h)[0]:256 * i + cols(h)[1]]
+
+    def relu(q):
+        def f(s, i, h=None):
+            e = behind(q, ("v", s, i), h, lambda p: S.activation(part(s, i, h), p, AF.Relu, scale=0.05) if q == "a" else
+                       V.tensor_scalar(part(s, i, h), p, 0.0, 0.05, A.max, A.mult))
+            for k in halves(h):
+                E["r", s, i, k] = e
+        return f
 
     def add(s, i, h=None):
         a, b = cols(h)
-        wt("v", E["e", s, i], *[E["r", s, i, k] for k in range(a // 128, b // 128)])
-        e = ev(V.tensor_tensor(ST[s][3][:, 4 * a + i:4 * b:4], bank(("e", s, i), a, b), ST[s][2][:, 256 * i + a:256 * i + b], A.add))
-        read(("e", s, i), e, (b - a) // 128)
-        for k in range(a // 128, b // 128):
+        wt("v", *[E["r", s, i, k] for k in halves(h)])
+        e = behind("v", ("e", s, i), h, lambda p: V.tensor_tensor(ST[s][3][:, 4 * a + i:4 * b:4], p, part(s, i, h), A.add))
+        for k in halves(h):
             E["a", s, i, k] = e
 
     def pack(s, h=None):
-        a, b = cols(h)
-        w, c0 = ST[s][:2]
-        wt("v", *[E["a", s, i, k] for i in range(4) for k in range(a // 128, b // 128)])
-        e = quant(pair(w, c0 + 256 + a, c0 + 256 + b), ST[s][3][:, 4 * a:4 * b])
-        for k in range(a // 128, b // 128):
+        (a, b), (w, c0) = cols(h), ST[s][:2]
+        wt("v", *[E["a", s, i, k] for i in range(4) for k in halves(h)])
+        e = ev(quant(pair(w, c0 + 256 + a, c0 + 256 + b), ST[s][3][:, 4 * a:4 * b]))
+        for k in halves(h):
             E["q", s, k] = e
 
-    def pick(s, q, h=None):
-        a, b = cols(h)
-        w, c0 = ST[s][:2]
-        wt(q, E["off", s], *[E["q", s, k] for k in range(b // 128)])
-        e = ev((pick_c if q == "v" else pick_s)(pair(ST[s][5], a, b), pair(w, c0, c0 + 256 + b), ST[s][4][:, a // 16:b // 16]))
-        for k in range(a // 128, b // 128):
-            E[q, "t", s, k] = e
+    def pick(q):
+        def f(s, h=None):
+            (a, b), (w, c0) = cols(h), ST[s][:2]
+            wt(q.replace("w", "v"), E["off", s], *(landed(s) + [E["q", s, k] for k in range(b // 128)]))
+            e = ev(gather(q, pair(ST[s][5], a, b), pair(w, c0, c0 + 256 + b), ST[s][4][:, a // 16:b // 16], (s, h)))
+            for k in halves(h):
+                E[q.replace("w", "a"), "t", s, k] = e
+        return f
 
-    def tile(s, k):
-        return [E["in", 1]] if s == 1 else [E[q, "t", 1, k] for q in "va"]
+    def diff(kind):
+        def f(s, j, k):
+            name, h = ("d", s, j, k), (k if kind == "row" else j)
+            wt("t", *(landed(s, h) + [E["un"]] if s == 1 or local else [E[q, "t", 1, h] for q in "va"] + [E["um", q, int(kind == "col")] for q in "va"]))
+            first = name not in held
+            if first:
+                take(name)
+            tile = pair("bw", 64 + 128 * h, 192 + 128 * h) if s == 2 and local else pair(RK[s][2], *cols(h))
+            tied = j == k and "tie%d%d" % (s, j) in ORDER
+            ins = mm(bank(name), *((RK[s][0], tile) if kind == "row" else (tile, RK[s][1])), first, not first and not tied)
+            if not first:
+                E[name] = None if tied else ev(ins)
+        return f
 
-    def row(s, i):
-        un, w = RK[s][:2]
-        wt("t", *tile(s, BLK[i][1]), *([E["unc"], E["uns"]] if s == 1 else [E["um", "v", 0], E["um", "a", 0]]))
-        take(("d", s, i), 1)
-        b = 128 * BLK[i][1]
-        mm(bank(("d", s, i)), pair(un, 0, 128), pair(w, b, b + 128), True, False)
+    def tie(s, h):
+        name = ("d", s, h, h)
+        assert E[name] is None
+        wt("t", E["e"], E["tz"], E["tq0"])
+        E[name] = ev(mm(bank(name, 0, 130), pair("eq", 0, 128), pair("tq", 0, 130), False, True))
 
-    def col(s, i):
-        un, w = RK[s][:2]
-        wt("t", *tile(s, BLK[i][0]), *([E["unc"], E["uns"]] if s == 1 else [E["um", "v", 1], E["um", "a", 1]]))
-        a = 128 * BLK[i][0]
-        E["d", s, i] = ev(mm(bank(("d", s, i)), pair(w, a, a + 128), pair(un, 128, 256), False, True))
+    def sign(s, h):
+        name = ("d", s, h, h)
+        assert E[name]
+        wt("a", E[name])
+        E["s", s, h] = read(name, S.activation(RK[s][7][:, 128 * h:128 * h + 128], bank(name), AF.Sign,
+                                               accum_out=RK[s][4][:, 128 * h + 127:128 * h + 128]))
+        E["c3", s, h] = E["c3"]
 
     def own(s, h):
-        wt("v", E["d", s, 2 * h], E["tb"])
-        E["g", s, h] = read(("d", s, 2 * h), ev(V.tensor_tensor(RK[s][2][:, 128 * h:128 * h + 128], bank(("d", s, 2 * h)),
-                                                                T.tb[:], A.is_gt)))
+        name = ("d", s, h, h)
+        wt("v", E[name], E["tb"])
+        E["g", s, h] = read(name, V.tensor_tensor(RK[s][3][:, 128 * h:128 * h + 128], bank(name), T.tb[:], A.is_gt))
 
     def other(s, h):
-        wt("a", E["d", s, 2 * h + 1])
-        E["o", s, h] = read(("d", s, 2 * h + 1), ev(S.activation(RK[s][4][:, 128 * h:128 * h + 128], bank(("d", s, 2 * h + 1)),
-                                                                 AF.Sign, bias=(EPS if h else -EPS),
-                                                                 accum_out=RK[s][5][:, h:h + 1])))
+        name = ("d", s, h, 1 - h)
+        wt("a", E[name])
+        E["o", s, h] = read(name, S.activation(RK[s][5][:, 128 * h:128 * h + 128], bank(name), AF.Sign, bias=(EPS if h else -EPS),
+                                               accum_out=RK[s][6][:, h:h + 1]))
 
     def count(s, h):
+        wt("v", E["g", s, h])
+        x = slice(128 * h, 128 * h + 128)
+        E["s", s, h] = ev(V.tensor_tensor_scan(RK[s][4][:, x], RK[s][3][:, x], RK[s][3][:, x], 0.0, A.add, A.add))
+
+    def count_a(s, h):
+        wt("a", E["g", s, h])
+        x = slice(128 * h, 128 * h + 128)
+        E["s", s, h] = ev(S.activation(RK[s][7][:, x], RK[s][3][:, x], AF.Copy, scale=2.0,
+                                       accum_out=RK[s][4][:, 128 * h + 127:128 * h + 128]))
+
+    def count_on(s, h):
         wt("v", E["g", s, h], E["o", s, h])
-        gb, x = RK[s][2], slice(128 * h, 128 * h + 128)
-        E["s", s, h] = ev(V.tensor_tensor_scan(RK[s][3][:, x], gb[:, x], gb[:, x], RK[s][5][:, h:h + 1], A.add, A.add))
+        x = slice(128 * h, 128 * h + 128)
+        E["s", s, h] = ev(V.tensor_tensor_scan(RK[s][7][:, x], RK[s][3][:, x], RK[s][3][:, x], RK[s][6][:, h:h + 1], A.add, A.add))
+        E["on", s, h] = 1
 
     def steps(s, h):
-        wt("v", E["s", s, h], E["cl%d" % h], E["cf%d" % h], E["cm" if h else "cc"], *([E["f", 1]] if s == 2 else []))
-        E["x", s, h] = ev(V.tensor_scalar(T.bb[:, h:320:2], T.c2[:, 160 * h:160 * h + 160],
-                                          RK[s][3][:, 128 * h + 127:128 * h + 128], None, A.is_gt))
+        wt("v", E["s", s, h], E["o", s, h], E["cl%d" % h], E["cf"], *([E["f", 1]] if s == 2 else []))
+        out, edges, x = T.bb[:, h:320:2], T.c2[:, 160 * h:160 * h + 160], slice(128 * h + 127, 128 * h + 128)
+        if ("c3", s, h) in E:
+            wt("v", E["c3"])
+            edges = T.c3[:, 160 * h:160 * h + 160]
+        E["x", s] = ev(V.tensor_scalar(out, edges, RK[s][7][:, x], None, A.is_gt) if ("on", s, h) in E else
+                       V.tensor_scalar(out, edges, RK[s][4][:, x], RK[s][6][:, h:h + 1], A.subtract, A.is_gt), 1, E.get(("x", s)))
 
     def flags(s):
-        wt("v", E["x", s, 0], E["x", s, 1], E["uq"])
-        E["f", s] = quant(pair(RK[s][6], 0, 128), T.bb[:, 0:512])
+        assert E["x", s][1] == 2
+        wt("v", E["x", s], E["id"], E["nu"], *([E["k", 1]] + [E["l", 1] for _ in range(local)] if s == 2 else []))
+        E["f", s] = ev(quant(pair("ff", 64 * s - 64, 64 * s + 64), T.bb[:, 0:512]))
 
-    def lists(s):
-        wt("t", E["f", s], E["uq"])
-        take(("l", s), 1)
-        E["l", s] = ev(mm(bank(("l", s)), pair(RK[s][6], 0, 128), pair("uq", 0, 128)))
+    def lists(s=2):
+        wt("t", E["f", s], E["un"])
+        take(("l", s))
+        E["l", s] = ev(mm(bank(("l", s)), pair("ff", 0, 128), pair("un", 0, 128)))
 
-    def places(s):
+    def places(s=2):
         wt("a", E["l", s])
-        E["p", s] = read(("l", s), ev(S.activation(T.pj[:, 2 * s - 2:2 * s], bank(("l", s), 2, 4), AF.Copy,
-                                                   accum_out=T.pp[:, s - 1:s])))
+        if local and s == 2:
+            wt("a", E["rl"])
+            E["rl"] = read(("l", s), S.activation(T.pk[64:128, :], bank(("l", s), 0, 2, slice(64, 128)), AF.Copy,
+                                                  accum_out=T.ll[64:128, :]))
+            E["both"] = 1
+        else:
+            E["p"] = read(("l", s), S.activation(T.pj[:], bank(("l", s), 0, 2), AF.Copy, accum_out=T.pp[:]))
 
     def turn(s):
-        wt("t", E["kq"], E["f", 1] if s == 1 else E["rf"])
-        take(("k", s), 1)
-        E["k", s] = ev(mm(bank(("k", s)), pair("kq", 0, 128), pair("f1", 0, 128) if s == 1 else pair("bw", 48, 176)))
+        wt("t", E["kq"], *([E["f", s]] if s == 1 or local else [E["rf"]] + landed(2, 0)))
+        take(("k", s))
+        E["k", s] = ev(mm(bank(("k", s)), pair("kq", 0, 128),
+                          pair("ff", 64 * s - 64, 64 * s + 64) if s == 1 or local else pair("bw", 48, 176)))
 
     def offsets(s):
         wt("v", E["k", s], E["j"])
-        a = 64 if s == 1 else 0
-        E["off", s] = read(("k", s), ev(V.tensor_scalar(ST[s][4][:], bank(("k", s), a, a + 16), lo, None, A.add)))
+        a = 64 if s == 1 or local else 0
+        E["off", s] = read(("k", s), V.tensor_scalar(ST[s][4][:], bank(("k", s), a, a + 16), lo, None, A.add))
 
-    def spread(q, h=None):
-        a, b = cols(h)
-        wt(q, E["ru"], E["zo0"], E["zo1"])
-        e = ev((pick_c if q == "v" else pick_s)(pair("um", a, b), pair("ul", 0, 2), T.zo[:, a // 16:b // 16]))
-        for k in range(a // 128, b // 128):
-            E["um", q, k] = e
-
-    def send_t1():
-        E["in", 2] = send_tile(pair("bw", 64, 320), pair("t1", 0, 256), [E["v", "t", 1, k] for k in range(2)],
-                               [E["a", "t", 1, k] for k in range(2)], "rb")
+    def spread(q):
+        def f(h=None):
+            a, b = cols(h)
+            wt(q.replace("w", "v"), E["ru"], E["zo"])
+            e = ev(gather(q, pair("um", a, b), pair("ul", 0, 2), T.zo[:, a // 16:b // 16], ("u", h)))
+            for k in halves(h):
+                E["um", q.replace("w", "a"), k] = e
+        return f
 
     def send_flags():
+        assert landed(2)
         wt("g", E["f", 2])
-        E["rf"] = send2(nxt, [(u8(T.bw[:, 48:64]), u8(T.f2[:, 64:80])), (T.bws[:, 0:64], T.f2s[:, 16:80])], "rf")
+        E["rf"] = send2(nxt, [(u8(T.bw[:, 48:64]), u8(T.ff[:, 128:144])), (T.bws[:, 0:64], T.ffs[:, 80:144])], "rf")
 
-    def send_lists():
-        wt("g", E["p", 1], E["p", 2])
+    def send_flags2():
+        assert landed(2)
+        wt("g", E["f", 2])
+        E["rf"] = ("rf", send(u8(T.bw[:, 48:64]), u8(T.ff[:, 128:144]), "rf") + send(T.bws[:, 48:64], T.ffs[:, 128:144], "rf"))
+
+    def send_list():
+        assert landed(2) and (local or E["rf"])
+        wt("g", E["p"])
         E["rl"] = ("rl", send(T.ll[:], T.pp[:], "rl"))
 
-    def quant_w():
-        wt("v", E["w"])
-        E["wq"] = quant(pair("wq", 0, 128), T.wt[:])
+    def copy(q, out, in_):
+        return V.tensor_copy(out, in_) if q == "v" else S.activation(out, in_, AF.Copy)
 
     def y_mm(h=None):
-        a, b = cols(h)
-        wt("t", E["wq"], *[E[q, "t", 2, k] for q in "va" for k in range(a // 128, b // 128)])
-        take(("y", h), 1)
-        E["y", h] = ev(mm(bank(("y", h), 0, b - a), pair("wq", 0, 128), pair("t2", a, b)))
+        product(("ym",), [E["wq"]] + [E[q, "t", 2, k] for q in "va" for k in halves(h)], pair("wq", 0, 128), pair("t2", *cols(h)), h)
 
-    def y_copy(q, h=None):
+    def y_copy(q):
+        def f(h=None):
+            e = behind(q, ("ym",), h, lambda p: copy(q, T.yt[:, cols(h)[0]:cols(h)[1]], p))
+            for k in halves(h):
+                E["y", k] = e
+        return f
+
+    def yy_mm(n, h=None):
         a, b = cols(h)
-        wt(q, E["y", h])
-        out, in_ = T.yt[:, a:b], bank(("y", h), 0, b - a)
-        e = read(("y", h), ev(V.tensor_copy(out, in_) if q == "v" else S.activation(out, in_, AF.Copy)))
-        for k in range(a // 128, b // 128):
-            E["z", k] = e
+        product(("yy", n), [E["wq"]] + ([E["q", 2, k] for k in halves(h)] if n else landed(2, h)), pair("wq", 0, 128),
+                pair("bw", 64 + 256 * n + a, 64 + 256 * n + b), h)
+
+    def yy_copy(q):
+        def f(n, h=None):
+            e = behind(q, ("yy", n), h, lambda p: copy(q, T.yw[:, 256 * n + cols(h)[0]:256 * n + cols(h)[1]], p))
+            for k in halves(h):
+                E["yw", n, k] = e
+        return f
+
+    def yy_pick(q):
+        def f(h=None):
+            a, b = cols(h)
+            wt(q, E["off", 2], *([E["yw", 0, k] for k in (0, 1)] + [E["yw", 1, k] for k in range(b // 128)]))
+            e = ev(copy(q, T.yt[:, a:b], T.yw[:, 0:256 + b].indirect(T.o2[:, a // 16:b // 16])))
+            for k in halves(h):
+                E["y", k] = e
+        return f
 
     def store(q, out, in_, *es):
         wt(q, *es)
         E["out"] = ev(Q[q].dma_start(out, in_), 16, E.get("out"))
 
-    def store_li(q, h):
-        store(q, T.li[h:h + 1, :], T.ll[0:64, h:h + 1], E["rl"])
-
     def store_oc(q):
-        store(q, T.oc[:], u8(T.t2[:]), E["v", "t", 2, 0], E["v", "t", 2, 1])
-
-    def store_osc(q, k):
-        store(q, T.osc[4 * k:4 * k + 4, :], T.t2s[32 * k:32 * k + 4, :], E["a", "t", 2, 0], E["a", "t", 2, 1])
+        def f(h=None):
+            a, b = cols(h)
+            store(q, T.oc[:, 4 * a:4 * b], u8(T.t2[:, a:b]), *[E["v", "t", 2, k] for k in halves(h)])
+        return f
 
     def store_y(q):
-        store(q, T.y[:], T.yt[:], E["z", 0], E["z", 1])
+        def f(h=None):
+            a, b = cols(h)
+            store(q, T.y[:, a:b], T.yt[:, a:b], *[E["y", k] for k in halves(h)])
+        return f
 
-    c("z");c("ii");c("x");c("id");c("u");c("zo0");c("v0");c("zo1");c("cm");c("jj");c("nu");c("e0");c("ja0");c("v1")
-    c("tq");c("ja1");c("ij");c("i16");c("e3");c("mk");c("sp");c("j");c("e1");c("uq");send_t0();send_u();c("q2")
-    c("k0");c("cf0");c("cl0");c("e2");c("cl1");c("unc");c("q1");c("uns");c("w");row(1,3);c("q0");c("k2");row(1,0)
-    pv(1,0);c("k3");c("tb");c("k1");col(1,0);c("kq");c("cc");col(1,3);row(1,2);col(1,2);row(1,1);col(1,1);pe(1,0)
-    pv(1,1);spread("v",0);own(1,0);pe(1,1);relu(1,0);c("q3");other(1,1);pv(1,2);own(1,1);pv(1,3);c("cf1");pe(1,2)
-    other(1,0);add(1,0,0);pe(1,3);count(1,0);count(1,1);add(1,0,1);relu(1,1,0);relu(1,1,1);relu(1,2,0);steps(1,0)
-    steps(1,1);relu(1,2,1);add(1,1,1);add(1,1,0);flags(1);relu(1,3,0);turn(1);add(1,2,0);relu(1,3,1);add(1,3,0)
-    add(1,2,1);add(1,3,1);pack(1,0);offsets(1);pack(1,1);spread("a",1);spread("a",0);pick(1,"v",0);pick(1,"v",1)
-    lists(1);pick(1,"a",0);spread("v",1);pick(1,"a",1);row(2,2);places(1);row(2,3);row(2,1);quant_w();col(2,2)
-    own(2,1);row(2,0);col(2,3);other(2,1);col(2,1);col(2,0);send_t1();pv(2,0);own(2,0);count(2,1);pv(2,2);other(2,0)
-    pv(2,1);count(2,0);pv(2,3);steps(2,1);relu(2,0);pe(2,0);steps(2,0);flags(2);send_flags();pe(2,1);relu(2,1)
-    lists(2);add(2,0);pe(2,2);relu(2,2);add(2,1);pe(2,3);relu(2,3,0);places(2);send_lists();add(2,2,0);add(2,3,0)
-    add(2,2,1);relu(2,3,1);store_li("s",0);add(2,3,1);turn(2);pack(2,0);offsets(2);pack(2,1);pick(2,"a",0)
-    pick(2,"v",0);store_li("s",1);pick(2,"v",1);y_mm(0);pick(2,"a",1);y_mm(1);y_copy("v",1);store_osc("a",1)
-    store_osc("a",0);y_copy("a",0);store_oc("s");store_osc("s",2);store_y("a");store_osc("s",3)
+    def store_osc(q):
+        def f(k):
+            store(q, T.osc[4 * k:4 * k + 4, :], T.t2s[32 * k:32 * k + 4, :], E["a", "t", 2, 0], E["a", "t", 2, 1])
+        return f
 
+    STEP = {"v": prod("v", "vq"), "e": prod("e", "eq"), "r": relu("a"), "rv": relu("v"), "a": add, "pack": pack,
+            "pc": pick("v"), "ps": pick("a"), "pw": pick("w"),
+            "row": diff("row"), "col": diff("col"), "own": own, "oth": other, "cnt": count, "cno": count_on, "tie": tie, "sgn": sign, "cna": count_a, "step": steps,
+            "flags": flags,
+            "list": lists, "place": places, "turn": turn, "off": offsets, "spreadv": spread("v"), "spreada": spread("a"), "spreadw": spread("w"),
+            "sc": hand_on(0), "ss": hand_on(1), "sendu": send_u("un", 129), "senduq": send_u("uq", 0),
+            "hold": lambda: wt("g", E["g", 2, 1]),
+            "sendflags": send_flags, "sendflagsb": send_flags2, "sendlist": send_list,
+            "ym": y_mm, "yv": y_copy("v"), "ya": y_copy("a"), "yy": yy_mm, "ywv": yy_copy("v"), "ywa": yy_copy("a"),
+            "ypv": yy_pick("v"), "ypa": yy_pick("a"), "oc": store_oc("s"), "oca": store_oc("a"), "y": store_y("s"),
+            "yya": store_y("a"), "osc": store_osc("s"), "osca": store_osc("a"),
+            "li": lambda: store("s", T.li[:], T.ll[:], E["rl"], *[E["rl"] for _ in range(local and E["both"])]),
+            "lia": lambda: store("a", T.li[:], T.ll[:], E["rl"], *[E["rl"] for _ in range(local and E["both"])])}
+
+    for name in START + STOP1 + AHEAD + STOP2:
+        word = name.rstrip("0123456789")
+        if name in CALLS:
+            const(name)
+        else:
+            STEP[word](*[int(d) for d in name[len(word):]])
+
+    assert not [key for key in picked if picked.count(key) != 2]
     done = {e for (_, e) in known}
     wt("s", *[e for e in made if e[0] not in done and e is not E["out"]])
     wt("s", E["out"])

@@ -5,8 +5,7 @@ A = AluOpType
 AF = ActivationFunctionType
 F8, U8, BF, F32, I32, U16 = "float8_e4m3fn_x4", "uint8", "bfloat16", "float32", "int32", "uint16"
 EPS = 2.0 ** -110
-TIE = 2.0 ** -100
-UT, ZT, BB = 320, 336, 856
+ZT, BB = 336, 856
 
 SCRATCH = {}
 
@@ -16,27 +15,30 @@ def _pair(n, w):
     SCRATCH[n + "s"] = ("sbuf", [128, w], U8)
 
 
-for _n, _w in (("un", 258), ("uq", 128), ("ul", 8), ("um", 256), ("vq", 512), ("wq", 128), ("eq", 512), ("kq", 128), ("tq", 384),
+for _n, _w in (("un", 258), ("uq", 128), ("ul", 16), ("um", 256), ("vq", 512), ("wq", 128), ("eq", 512), ("kq", 128), ("tq", 256),
                ("aw", 512), ("bw", 576), ("ff", 192), ("t1", 256), ("t2", 256)):
     _pair(_n, _w)
-for _n, _w, _d in (("xt", 1024, BF), ("bb", BB, BF), ("ut", 1032, BF), ("vt", 2048, BF), ("wt", 512, BF),
-                   ("kt", 512, BF), ("n1", 1024, BF), ("n2", 1024, BF), ("tb", 128, BF), ("mk", 128, BF), ("c2", 320, BF),
-                   ("c3", 320, BF), ("tt", 512, BF),
+for _n, _w, _d in (("xt", 1024, BF), ("bb", BB, BF), ("ub", 4, BF), ("ut", 1036, BF), ("vt", 2048, BF), ("wt", 512, BF),
+                   ("kt", 512, BF), ("n1", 1024, BF), ("n2", 1024, BF), ("tb", 128, BF), ("ib", 128, BF), ("c2", 320, BF),
                    ("g1", 256, BF), ("g2", 256, BF), ("sc1", 256, F32), ("sc2", 256, F32), ("sb1", 256, BF), ("sb2", 256, BF),
-                   ("jk1", 256, BF), ("jk2", 256, BF),
-                   ("sg1", 2, F32), ("sg2", 2, F32), ("r1", 1024, F32), ("r2", 1024, F32), ("ii", 128, I32), ("ij", 128, I32),
+                   ("jk1", 256, BF), ("jk2", 256, BF), ("sg1", 2, F32), ("sg2", 2, F32), ("r1", 1024, F32), ("r2", 1024, F32),
                    ("jj", 8, I32), ("ja", 8, I32), ("sp", 8, F32), ("i16", 24, F32), ("zo", 16, U16), ("o1", 16, U16),
-                   ("o2", 16, U16), ("pp", 1, F32), ("ll", 1, F32), ("pj", 2, F32), ("pk", 2, F32), ("yt", 256, F32), ("yw", 512, F32)):
+                   ("o2", 16, U16), ("pp", 1, F32), ("ll", 1, F32), ("pj", 2, F32), ("yt", 256, F32), ("yw", 512, F32)):
     SCRATCH[_n] = ("sbuf", [128, _w], _d)
 for _n, _w in (("pr", 2048), ("pm", 2048)):
     SCRATCH[_n] = ("psum", [128, _w], F32)
 
-NEV = 141
-SEMAPHORES = ["s%d" % _i for _i in range(NEV)] + ["lo", "lt", "ru", "in10", "in11", "in20", "in21", "rf", "rl"]
+SEMAPHORES = ["s%d" % _i for _i in range(141)] + ["lo", "lt", "ru", "in10", "in11", "in20", "in21", "rf", "rl"]
 
-START = 'x z jj tq id e u vb ja ii ij nu q3 sc1 j tb mk rep un ss1 va cl0 col100 row100 col111 k row111 sendu zo row110 q1 col110 q0 col101 cl1 row101 v10 q2 cf kq e10 own10 v12 oth11 oth10 own11 cnt10 cnt11 r100 v11 spreadv step11 step10 v130 r101 e12 a10 flags1 r120 r121 e130 v131 e11 turn1 r130 r11 a12 a130 e131 a11 r131 off1 a131 spreada pack10 pack11 pc10 ps10 pc11 sc20 col200 row200 own20 row210 ps11 col211 row201 row211 w ss2 col201 col210 sc21 v200 own21 cna20 v220 wq cnt21 v201 oth20 step20 v21 oth21 e20 step21 r200 flags2 rv201 v221 rv211 rv210 list sendflags e21 v230 r220 e22 r221 place a200 a201 v231 e23 a210 a211 a22 r230 turn2 a230 r231 a231 sendlist pack20 off2 ps20 pack21 ps21 pc20 osca2 ym0 osca1 li pc21 oc yv0 osc0 ym1 yv1 y osca3'.split()
-START = 'x u va vb ii z ij mk jj nu tq ja tb id rep sc1 ss1 zo cl0 j e cf q0 un q1 k q3 cl1 kq q2 sendu w col100 row100 row111 col111 col101 own10 col110 row101 row110 oth10 own11 v10 v12 e10 oth11 cnt10 r100 cnt11 r101 v11 e12 v13 spreadv step11 step10 r12 a10 r11 e11 r13 flags1 e130 e131 spreada turn1 a12 a11 a130 a131 off1 pack10 pack11 pc10 ps10 sc20 pc11 col200 ps11 wq row200 own20 ss2 row210 col211 row211 row201 col201 own21 col210 sc21 v200 v230 v201 cnt20 v21 oth20 cnt21 oth21 e20 r200 r201 step20 r21 step21 v22 flags2 e21 r220 e22 a20 a210 a211 v231 a220 r230 e230 e231 yy01 r221 a230 r231 sendflagsb a221 list a231 place turn2 sendlist pack20 pack21 yy00 off2 pc2 li yy10 ywa01 ywa00 ywa10 yy11 ywa11 pw2 oc ypa0 ypa1 y osc2 osc0 osca1 osca3'.split()
-STOP1, AHEAD, STOP2 = [], [], []
+START = ("x0 u x1 va vb z ii jj id tb e0 tq0 sc10 up kb cm zo ja e3 tq1 j nu e1 km uq um ss1 kd sc11 sendu e2 w cl0 q0 q1 un "
+         "cf k q2 cl1 q3 kq").split()
+STOP1 = ("v100 row100 col100 col101 own10 col111 cna10 row111 rv100 row110 col110 own11 row101 v12 oth10 spreadv oth11 cnt11 "
+         "step10 e100 a100 v11 e12 v13 e11 step11 v101 r120 e13 a120 r121 r11 a121 flags1 r13 e101 a11 r101 a130 a101 spreada "
+         "a131 pack10 turn1 off1 pack11 pc10 ps10 pc11 ps11").split()
+AHEAD = ("sc20 row200 col200 ss2 col201 row211 sc21 wq col211 row201 oth20 col210 own20 row210 oth21 own21 v210 v200 e200 v22 "
+         "r210 v211 r200 e210 e22 v23 cnt20 cnt21 step20 step21 r220 flags2 sendflags").split()
+STOP2 = ("e211 a210 v201 a220 e230 r211 r221 a200 a211 a221 e231 r230 e201 a230 r231 r201 list place yy0 ywa00 a231 a201 "
+         "pack20 pack21 turn2 sendlist off2 li yy10 ywa10 yy11 ywa11 ywv01 yp0 pc2 pw2 yp1 oc y osc2 osca3 osca0 osca1").split()
 
 
 def rank_program(g, core, T, topo):
@@ -47,40 +49,31 @@ def rank_program(g, core, T, topo):
     Q = {"g": g, "v": g.vector, "a": g.scalar, "s": g.sync, "t": g.tensor}
     V, S, P, Y = g.vector, g.scalar, g.tensor, g.sync
     made, known, nloc, E = [], {}, {"lo": 0, "lt": 0}, {}
-    ORDER = START + STOP1 + AHEAD + STOP2
-    local = int("list1" in ORDER)
+    names, spare = {}, []
 
-    def ev(ins, k=1, e=None):
+    def ev(ins, k=1, e=None, stop=0):
         if e is None:
-            e = ["s%d" % len(made), 0]
+            e = list(spare.pop()) if stop == 2 and spare else ["s%d" % len(names), 0]
+            names[e[0]] = 1
             made.append(e)
+            if stop == 1:
+                spare.append(e)
         ins.then_inc(T.sem[e[0]], k)
         e[1] += k
         return e
 
     def wt(q, *es):
         for e in es:
-            if (q, e[0]) not in known:
-                known[(q, e[0])] = 1
+            if (q, e[0], e[1]) not in known:
+                known[q, e[0], e[1]] = 1
                 Q[q].wait_ge(T.sem[e[0]], e[1])
 
-    def send(out, in_, sem, loc="lo"):
-        rid, pid, _ = topo.addr(nxt)
-        g.remote_dma(out, in_, T.sem[sem], T.sem[loc], pid, rid, topo.mask(core, nxt))
-        k = len(topo.engines(core, nxt))
+    def send(out, in_, sem, loc="lo", dst=nxt):
+        rid, pid, _ = topo.addr(dst)
+        g.remote_dma(out, in_, T.sem[sem], T.sem[loc], pid, rid, topo.mask(core, dst))
+        k = len(topo.engines(core, dst))
         nloc[loc] += k
         return k
-
-    def send2(dst, pairs, sem, loc="lo"):
-        rid, pid, _ = topo.addr(dst)
-        es = topo.engines(core, dst)
-        h = len(es) // 2
-        g.remote_dma_fused([RemoteDMATransfer(dst_ids=[DstId(rid=rid, pnc=pid)],
-                                              dma_engine_mask=sum(1 << e for e in es[i * h:i * h + h]),
-                                              remote_sem=T.sem[sem], srcs=[s], dsts=[d], alu_op=0)
-                            for i, (d, s) in enumerate(pairs)], local_sem=T.sem[loc])
-        nloc[loc] += 2 * h
-        return (sem, 2 * h)
 
     def u8(v):
         return v.bitcast(dt.uint8)
@@ -90,6 +83,9 @@ def rank_program(g, core, T, topo):
 
     def pair(name, a, b):
         return T[name][:, a:b], T[name + "s"][:, a:b]
+
+    def send_pair(out, in_, sem, loc="lo", dst=nxt):
+        return (sem, send(u8(out[0]), u8(in_[0]), sem, loc, dst) + send(out[1], in_[1], sem, loc, dst))
 
     def cols(h):
         return (0, 256) if h is None else (128 * h, 128 * h + 128)
@@ -103,114 +99,94 @@ def rank_program(g, core, T, topo):
     def mm(out, lhs, rhs, start=True, stop=True):
         return P.matmul_mx(out, lhs[0], lhs[1], rhs[0], rhs[1], start, stop)
 
-    picked = []
+    def copy(q, out, in_):
+        return V.tensor_copy(out, in_) if q == "v" else S.activation(out, in_, AF.Copy)
 
-    def gather(q, dst, win, off, key):
-        picked.append(key)
-        if q == "v":
-            return V.tensor_copy(u32(dst[0]), u32(win[0]).indirect(off))
-        if q == "w":
-            return V.tensor_copy(dst[1], win[1].indirect(off))
-        return S.activation(dst[1], win[1].indirect(off), AF.Copy)
+    def gather(k, q, dst, win, off):
+        return copy(q, dst[1], win[1].indirect(off)) if k else V.tensor_copy(u32(dst[0]), u32(win[0]).indirect(off))
 
     def iota(out, pattern, base, cm=0):
         return g.iota(out, pattern, base, cm, allow_small_or_imprecise_dtypes=True)
 
-    hi, lo = T.ut[:, 0:1], T.ut[:, 4:5]
+    hi, lo = T.ut[:, 4:5], T.ut[:, 8:9]
     ident = T.bb[:, ZT + 4:ZT + 516:4]
     zeros = T.bb[:, ZT + 1:ZT + 513:4]
 
     def cf():
         return ([V.tensor_scalar(T.c2[:, 160 * h + 128:160 * h + 160:2], T.i16[:, 8 - 8 * h:24 - 8 * h], hi, -256.0,
                                  A.not_equal, A.mult) for h in (0, 1)] +
-                [V.tensor_scalar(T.c2[:, 129:160:2], T.ii[:, 0:16], 128.5, 1024.0, A.subtract, A.mult),
-                 V.memset(T.c2[:, 289:320:2], -256.0)])
-
-    def kf():
-        return ([S.activation(T.kt[:, t:512:4], T.mk[:], AF.Copy, scale=256.0) for t in (0, 1)] +
-                [S.activation(T.kt[:, t:512:4], T.mk[:], AF.Identity, bias=16.0, scale=0.0) for t in (2, 3)])
-
-    def rep():
-        return [S.activation(T.ut[:, 8 + 512 * (t // 4) + t % 4:520 + 512 * (t // 4):4], zeros, AF.Identity,
-                             bias=T.bb[:, UT + t:UT + t + 1]) for t in range(8)]
+                [V.tensor_scalar(T.c2[:, 129:160:2], T.ib[:, 0:16], 128.5, 1024.0, A.subtract, A.mult)])
 
     CALLS = {
-        "x": ("s", (), lambda: [Y.dma_start(T.xt[:], T.x[:])], 16),
         "x0": ("s", (), lambda: [Y.dma_start(T.xt[:, 0:512], T.x[:, 0:512])], 16),
         "x1": ("s", (), lambda: [Y.dma_start(T.xt[:, 512:1024], T.x[:, 512:1024])], 16),
-        "u": ("s", (), lambda: [Y.dma_start(T.bb[:, UT:UT + 4], T.u[:, 0:4])], 16),
-        "ua": ("a", (), lambda: [S.dma_start(T.bb[:, UT:UT + 4], T.u[:, 0:4])], 16),
-        "v": ("s", (), lambda: [Y.dma_start(T.vt[:], T.v[:])], 16),
+        "u": ("s", (), lambda: [Y.dma_start(T.ub[:], T.u[:, 0:4])], 16),
         "va": ("s", (), lambda: [Y.dma_start(T.vt[:, 0:1024], T.v[:, 0:1024])], 16),
         "vb": ("s", (), lambda: [Y.dma_start(T.vt[:, 1024:2048], T.v[:, 1024:2048])], 16),
         "w": ("s", ("lt",), lambda: [Y.dma_start(T.wt[:], T.w[:])], 16),
+        "tq0": ("v", ("x0",), lambda: [quant(pair("tq", 0, 128), T.xt[:, 0:512])], 1),
+        "tq1": ("v", ("x1",), lambda: [quant(pair("tq", 128, 256), T.xt[:, 512:1024])], 1),
+        "wq": ("v", ("w",), lambda: [quant(pair("wq", 0, 128), T.wt[:])], 1),
+        "ii": ("g", (), lambda: [iota(T.ib[:], [[1, 128]], 128, -1)], 1),
+        "z": ("v", (), lambda: [V.memset(T.bb[:, 320:BB], 0.0)], 1),
+        "id": ("v", ("z", "ii"), lambda: [V.tensor_scalar(ident, T.ib[:], 128.0, None, A.is_equal)], 1),
+        "tb": ("v", ("ii",), lambda: [V.tensor_scalar(T.tb[:], T.ib[:], 128.0, -EPS, A.is_lt, A.mult)], 1),
         "jj": ("g", (), lambda: [g.iota(T.jj[:], [[0, 4], [128, 2]], 0, 1), iota(T.sp[:], [[0, 2], [-2, 2], [0, 2]], 1),
                                  iota(T.i16[:], [[16, 24]], -128)], 1),
-        "ii": ("g", (), lambda: [g.iota(T.ii[:], [[1, 128]], 128, -1)], 1),
-        "cl0": ("g", (), lambda: [iota(T.c2[:, 0:128], [[2, 64], [-2, 2]], -127)], 1),
-        "cl1": ("a", ("cl0",), lambda: [S.activation(T.c2[:, 160:288], T.c2[:, 0:128], AF.Copy)], 1),
-        "id": ("g", ("z",), lambda: [g.affine_select(ident, ident, [[1, 128]], A.not_equal, 1.0, 0, -1)], 1),
-        "z": ("v", (), lambda: [V.memset(T.bb[:, UT + 8:BB], 0.0)], 1),
-        "zo": ("v", (), lambda: [V.memset(T.zo[:, 0:8], 0), V.memset(T.zo[:, 8:16], 1)], 1),
         "ja": ("v", ("jj",), lambda: [V.tensor_scalar(T.ja[:, 0:4], T.jj[:, 0:4], 240, None, A.bitwise_and),
                                       V.tensor_scalar(T.ja[:, 4:8], T.jj[:, 4:8], 15, None, A.bitwise_and)], 1),
-        "ij": ("v", ("ii",), lambda: [V.tensor_scalar(T.ij[:], T.ii[:], 15, None, A.bitwise_and)], 1),
-        "j": ("v", ("ja",), lambda: [V.tensor_tensor(T.ut[:, 0:8], T.ja[:], T.sp[:], A.mult)], 1),
-        "mk": ("v", ("ij",), lambda: [V.tensor_scalar(T.mk[:], T.ij[:], 0.0, None, A.is_equal)], 1),
-        "nu": ("a", ("u",), lambda: [S.activation(T.bb[:, UT + 4:UT + 8], T.bb[:, UT:UT + 4], AF.Copy, scale=-1.0)], 1),
-        "rep": ("a", ("nu", "id"), rep, 1),
-        "tq": ("v", ("x",), lambda: [quant(pair("tq", 128, 384), T.xt[:])], 1),
-        "tq0": ("v", ("x0",), lambda: [quant(pair("tq", 128, 256), T.xt[:, 0:512])], 1),
-        "tq1": ("v", ("x1",), lambda: [quant(pair("tq", 256, 384), T.xt[:, 512:1024])], 1),
-        "t0": ("v", (), lambda: [V.memset(T.tt[:], 0.0)], 1),
-        "t1": ("v", ("t0", "ii"), lambda: [V.tensor_scalar(T.tt[:, 0:512:4], T.ii[:], 127.5, -TIE, A.subtract, A.mult)], 1),
-        "tz": ("v", ("t1",), lambda: [quant(pair("tq", 0, 128), T.tt[:])], 1),
-        "c3": ("a", ("cl1", "cf"), lambda: [S.activation(T.c3[:], T.c2[:], AF.Identity, bias=-128.0)], 1),
-        "uq": ("v", ("nu", "id"), lambda: [quant(pair("uq", 0, 128), T.bb[:, UT:UT + 512])], 1),
-        "un": ("v", ("rep", "j"), lambda: [quant(pair("un", 0, 258), T.ut[:])], 1),
-        "tb": ("v", ("ii",), lambda: [V.tensor_scalar(T.tb[:], T.ii[:], 128.0, -EPS, A.is_lt, A.mult)], 1),
+        "j": ("v", ("ja",), lambda: [V.tensor_tensor(T.ut[:, 4:12], T.ja[:], T.sp[:], A.mult)], 1),
+        "nu": ("v", ("u",), lambda: [V.tensor_scalar(T.ut[:, 0:4], T.ub[:], -1.0, None, A.mult)], 1),
+        "up": ("a", ("u", "id"), lambda: [S.activation(T.ut[:, 12 + t:524:4], zeros, AF.Identity, bias=T.ub[:, t:t + 1])
+                                          for t in range(4)], 1),
+        "uq": ("v", ("up", "nu", "j"), lambda: [quant(pair("uq", 0, 128), T.ut[:, 0:512])], 1),
+        "um": ("a", ("up",), lambda: [S.activation(T.ut[:, 524:1036], T.ut[:, 12:524], AF.Copy, scale=-1.0)], 1),
+        "un": ("v", ("um", "j"), lambda: [quant(pair("un", 0, 258), T.ut[:, 4:1036])], 1),
+        "zo": ("v", ("jj",), lambda: [V.tensor_scalar(T.zo[:], T.i16[:, 0:16], 0.0, 3.0, A.is_lt, A.mult)], 1),
+        "cl0": ("g", (), lambda: [iota(T.c2[:, 0:128], [[2, 64], [-2, 2]], -127)], 1),
+        "cl1": ("a", ("cl0",), lambda: [S.activation(T.c2[:, 160:288], T.c2[:, 0:128], AF.Copy)], 1),
         "cf": ("v", ("ii", "j"), cf, 1),
-        "e": ("v", ("id",), lambda: [quant(pair("eq", 128 * b, 128 * b + 128), T.bb[:, ZT + 4 - b:ZT + 516 - b]) for b in range(4)], 1),
-        "k": ("a", ("mk",), kf, 1),
+        "cm": ("a", ("jj",), lambda: [S.activation(T.c2[:, 289:320:2], T.i16[:, 0:16], AF.Identity, bias=-256.0, scale=0.0)], 1),
+        "km": ("v", ("j",), lambda: [V.tensor_scalar(T.kt[:, t:64:4], T.i16[:, 8:24], 1.0 / 16, lo, A.mult, A.is_equal)
+                                     for t in (0, 1)], 1),
+        "kb": ("a", ("jj",), lambda: [S.activation(T.kt[:, t:64:4], T.i16[:, 0:16], AF.Identity, bias=1.0 / 16, scale=0.0)
+                                      for t in (2, 3)], 1),
+        "kd": ("a", ("km", "kb"), lambda: [S.activation(T.kt[:, 64 * n:64 * n + 64], T.kt[:, 0:64], AF.Copy) for n in (1, 2, 3)], 1),
+        "k": ("a", ("kd",), lambda: [S.activation(T.kt[:, 256:512], T.kt[:, 0:256], AF.Copy)], 1),
         "kq": ("v", ("k",), lambda: [quant(pair("kq", 0, 128), T.kt[:])], 1),
-        "wq": ("v", ("w",), lambda: [quant(pair("wq", 0, 128), T.wt[:])], 1),
     }
-    ALSO = {"x": ("x0", "x1"), "tq": ("tq0", "tq1"), "v": ("va", "vb"), "ua": ("u",)}
 
     def qf(dst, src):
         return lambda: [quant(dst, src)]
 
     for b in range(4):
         CALLS["q%d" % b] = ("v", ("v" + "ab"[b // 2],), qf(pair("vq", 128 * b, 128 * b + 128), T.vt[:, 512 * b:512 * b + 512]), 1)
+        CALLS["e%d" % b] = ("v", ("id",), qf(pair("eq", 128 * b, 128 * b + 128), T.bb[:, ZT + 4 - b:ZT + 516 - b]), 1)
 
     def const(name):
         q, waits, calls, k = CALLS[name]
-        if name == "w":
-            assert landed(1) and (local or E["ru"])
-            E["lt"] = ("lt", nloc["lt"])
+        name = "e" if name[0] == "e" else name
+        assert name != "w" or (landed(1) and E["ru"])
+        E["lt"] = ("lt", nloc["lt"])
         wt(q, *[E[x] for x in waits])
         for ins in calls():
             E[name] = ev(ins, k, E.get(name))
-        for x in ALSO.get(name, ()):
-            E[x] = E[name]
 
     ST = {1: ("aw", 0, T.r1, T.n1, T.o1, "t1"), 2: ("bw", 64, T.r2, T.n2, T.o2, "t2")}
     RK = {1: (pair("un", 2, 130), pair("un", 130, 258), "aw", T.g1, T.sc1, T.jk1, T.sg1, T.sb1),
           2: (pair("um", 0, 128), pair("um", 128, 256), "t1", T.g2, T.sc2, T.jk2, T.sg2, T.sb2)}
-    if local:
-        RK[2] = RK[1][:2] + RK[2][2:]
 
     pieces = {}
 
     def hand_on(k):
         def f(s, h=None):
             (a, b), (w, c0) = cols(h), ST[s][:2]
-            wt("g", *[E["tq%d" % x] if s == 1 else E["va"[k], "t", 1, x] for x in halves(h)])
-            dst, src = pair(w, c0 + a, c0 + b)[k], (pair("tq", 128 + a, 128 + b) if s == 1 else pair("t1", a, b))[k]
+            wt("g", *[E["tq%d" % x] if s == 1 else E["t", 1, k, x] for x in halves(h)])
+            dst, src = pair(w, c0 + a, c0 + b)[k], pair(("tq", "t1")[s - 1], a, b)[k]
             sem = "in%d%d" % (s, halves(h)[0])
-            assert not [1 for key in known if key[1] == sem]
+            assert not [key for key in known if key[1] == sem]
             e = E.setdefault(sem, [sem, 0])
-            e[1] += send(dst, src, sem, "lt" if s == 1 else "lo") if k else send(u8(dst), u8(src), sem, "lt" if s == 1 else "lo")
+            e[1] += send(dst if k else u8(dst), src if k else u8(src), sem, "lt" if s == 1 else "lo")
             for x in halves(h):
                 pieces[s, k, x] = e
         return f
@@ -218,25 +194,31 @@ def rank_program(g, core, T, topo):
     def landed(s, h=None):
         return [pieces[s, k, x] for k in (0, 1) for x in halves(h)]
 
-    def send_u(name, a):
-        def f():
-            wt("g", E[name])
-            E["ru"] = send2(prv, [(u8(T.ul[:, 0:2]), u8(T[name][:, a:a + 2])), (T.uls[:, 0:8], T[name + "s"][:, a:a + 8])], "ru", "lt")
-        return f
+    def send_u():
+        wt("g", E["uq"])
+        rid, pid, _ = topo.addr(prv)
+        es = topo.engines(core, prv)
+        n = len(es) // 2
+        sides = ((u8(T.ul[:, 0:4]), u8(T.uq[:, 0:4])), (T.uls[:, 0:16], T.uqs[:, 0:16]))
+        g.remote_dma_fused([RemoteDMATransfer(dst_ids=[DstId(rid=rid, pnc=pid)], dma_engine_mask=sum(1 << e for e in es[i * n:i * n + n]),
+                                              remote_sem=T.sem.ru, srcs=[s], dsts=[d], alu_op=0)
+                            for i, (d, s) in enumerate(sides)], local_sem=T.sem.lt)
+        nloc["lt"] += 2 * n
+        E["ru"] = ("ru", 2 * n)
 
-    free, held, left = list(range(8)), {}, {b: [] for b in range(8)}
+    free, held, left, reader, where = list(range(8)), {}, {b: [] for b in range(8)}, {}, {}
 
     def take(name, parts=1):
         b = free.pop(0)
         wt("t", *left[b])
         held[name] = [b, parts, []]
 
-    def bank(name, a=0, b=128, rows=slice(0, 128)):
+    def bank(name, a=0, b=128):
         i = held[name][0]
-        return (T.pr, T.pm)[i // 4][rows, 512 * (i % 4) + a:512 * (i % 4) + b]
+        return (T.pr, T.pm)[i // 4][:, 512 * (i % 4) + a:512 * (i % 4) + b]
 
     def read(name, ins, parts=1):
-        x, e = held[name], ev(ins)
+        x, e = held[name], ev(ins, stop=name[1] if name[0] in ("v", "e") else 0)
         x[1] -= parts
         x[2].append(e)
         if x[1] == 0:
@@ -244,29 +226,32 @@ def rank_program(g, core, T, topo):
             free.append(x[0])
         return e
 
-    where = {}
-
     def product(key, waits, lhs, rhs, h):
         wt("t", *waits)
         take(key + (h,), len(halves(h)))
-        e = ev(mm(bank(key + (h,), 0, 128 * len(halves(h))), lhs, rhs))
-        for k in halves(h):
-            E[key + (k,)], where[key + (k,)] = e, (key + (h,), 128 * k - cols(h)[0])
+        stop = key[1] if key[0] in ("v", "e") else 0
+        if stop == 2:
+            wt("t", *[E["t", 1, k, x] for k in (0, 1) for x in (0, 1)])
+        e = ev(mm(bank(key + (h,), 0, 128 * len(halves(h))), lhs, rhs), stop=stop)
+        for x in halves(h):
+            E[key + (x,)], where[key + (x,)] = e, (key + (h,), 128 * x - cols(h)[0])
 
     def behind(q, key, h, call):
         name, a = where[key + halves(h)[:1]]
         assert name == where[key + halves(h)[-1:]][0]
-        other = [e for e in held[name][2]]
-        wt(q, E[key + halves(h)[:1]], *[e for e in other if reader[e[0]] != q])
+        wt(q, E[key + halves(h)[:1]], *[e for e in held[name][2] if reader[e[0]] != q])
         e = read(name, call(bank(name, a, a + 128 * len(halves(h)))), len(halves(h)))
         reader[e[0]] = q
         return e
 
-    reader = {}
+    def mark(key, h, e):
+        for x in halves(h):
+            E[key + (x,)] = e
 
     def prod(kind, name):
         def f(s, i, h=None):
             (a, b), (w, c0) = cols(h), ST[s][:2]
+            assert kind == "v" or E["e"][1] == 4
             product((kind, s, i), landed(s, h) + [E["q%d" % i if kind == "v" else "e"]], pair(name, 128 * i, 128 * i + 128),
                     pair(w, c0 + a, c0 + b), h)
         return f
@@ -276,62 +261,40 @@ def rank_program(g, core, T, topo):
 
     def relu(q):
         def f(s, i, h=None):
-            e = behind(q, ("v", s, i), h, lambda p: S.activation(part(s, i, h), p, AF.Relu, scale=0.05) if q == "a" else
-                       V.tensor_scalar(part(s, i, h), p, 0.0, 0.05, A.max, A.mult))
-            for k in halves(h):
-                E["r", s, i, k] = e
+            mark(("r", s, i), h, behind(q, ("v", s, i), h, lambda p: S.activation(part(s, i, h), p, AF.Relu, scale=0.05)
+                                        if q == "a" else V.tensor_scalar(part(s, i, h), p, 0.0, 0.05, A.max, A.mult)))
         return f
 
     def add(s, i, h=None):
         a, b = cols(h)
-        wt("v", *[E["r", s, i, k] for k in halves(h)])
-        e = behind("v", ("e", s, i), h, lambda p: V.tensor_tensor(ST[s][3][:, 4 * a + i:4 * b:4], p, part(s, i, h), A.add))
-        for k in halves(h):
-            E["a", s, i, k] = e
+        wt("v", *[E["r", s, i, x] for x in halves(h)])
+        mark(("a", s, i), h, behind("v", ("e", s, i), h, lambda p: V.tensor_tensor(ST[s][3][:, 4 * a + i:4 * b:4], p,
+                                                                                   part(s, i, h), A.add)))
 
     def pack(s, h=None):
         (a, b), (w, c0) = cols(h), ST[s][:2]
-        wt("v", *[E["a", s, i, k] for i in range(4) for k in halves(h)])
-        e = ev(quant(pair(w, c0 + 256 + a, c0 + 256 + b), ST[s][3][:, 4 * a:4 * b]))
-        for k in halves(h):
-            E["q", s, k] = e
+        wt("v", *[E["a", s, i, x] for i in range(4) for x in halves(h)])
+        mark(("q", s), h, ev(quant(pair(w, c0 + 256 + a, c0 + 256 + b), ST[s][3][:, 4 * a:4 * b])))
 
-    def pick(q):
+    def pick(k, q):
         def f(s, h=None):
             (a, b), (w, c0) = cols(h), ST[s][:2]
-            wt(q.replace("w", "v"), E["off", s], *(landed(s) + [E["q", s, k] for k in range(b // 128)]))
-            e = ev(gather(q, pair(ST[s][5], a, b), pair(w, c0, c0 + 256 + b), ST[s][4][:, a // 16:b // 16], (s, h)))
-            for k in halves(h):
-                E[q.replace("w", "a"), "t", s, k] = e
+            wt(q, E["off", s], *(landed(s) + [E["q", s, x] for x in range(b // 128)]))
+            mark(("t", s, k), h, ev(gather(k, q, pair(ST[s][5], a, b), pair(w, c0, c0 + 256 + b), ST[s][4][:, a // 16:b // 16])))
         return f
 
     def diff(kind):
         def f(s, j, k):
             name, h = ("d", s, j, k), (k if kind == "row" else j)
-            wt("t", *(landed(s, h) + [E["un"]] if s == 1 or local else [E[q, "t", 1, h] for q in "va"] + [E["um", q, int(kind == "col")] for q in "va"]))
+            wt("t", *(landed(1, h) + [E["un"]] if s == 1 else [E["t", 1, 0, h], E["t", 1, 1, h], E["um", 0], E["um", 1]]))
             first = name not in held
             if first:
                 take(name)
-            tile = pair("bw", 64 + 128 * h, 192 + 128 * h) if s == 2 and local else pair(RK[s][2], *cols(h))
-            tied = j == k and "tie%d%d" % (s, j) in ORDER
-            ins = mm(bank(name), *((RK[s][0], tile) if kind == "row" else (tile, RK[s][1])), first, not first and not tied)
+            tile = pair(RK[s][2], *cols(h))
+            ins = mm(bank(name), *((RK[s][0], tile) if kind == "row" else (tile, RK[s][1])), first, not first)
             if not first:
-                E[name] = None if tied else ev(ins)
+                E[name] = ev(ins)
         return f
-
-    def tie(s, h):
-        name = ("d", s, h, h)
-        assert E[name] is None
-        wt("t", E["e"], E["tz"], E["tq0"])
-        E[name] = ev(mm(bank(name, 0, 130), pair("eq", 0, 128), pair("tq", 0, 130), False, True))
-
-    def sign(s, h):
-        name = ("d", s, h, h)
-        assert E[name]
-        wt("a", E[name])
-        E["s", s, h] = read(name, S.activation(RK[s][7][:, 128 * h:128 * h + 128], bank(name), AF.Sign,
-                                               accum_out=RK[s][4][:, 128 * h + 127:128 * h + 128]))
-        E["c3", s, h] = E["c3"]
 
     def own(s, h):
         name = ("d", s, h, h)
@@ -344,155 +307,92 @@ def rank_program(g, core, T, topo):
         E["o", s, h] = read(name, S.activation(RK[s][5][:, 128 * h:128 * h + 128], bank(name), AF.Sign, bias=(EPS if h else -EPS),
                                                accum_out=RK[s][6][:, h:h + 1]))
 
-    def count(s, h):
-        wt("v", E["g", s, h])
-        x = slice(128 * h, 128 * h + 128)
-        E["s", s, h] = ev(V.tensor_tensor_scan(RK[s][4][:, x], RK[s][3][:, x], RK[s][3][:, x], 0.0, A.add, A.add))
-
-    def count_a(s, h):
-        wt("a", E["g", s, h])
-        x = slice(128 * h, 128 * h + 128)
-        E["s", s, h] = ev(S.activation(RK[s][7][:, x], RK[s][3][:, x], AF.Copy, scale=2.0,
-                                       accum_out=RK[s][4][:, 128 * h + 127:128 * h + 128]))
-
-    def count_on(s, h):
-        wt("v", E["g", s, h], E["o", s, h])
-        x = slice(128 * h, 128 * h + 128)
-        E["s", s, h] = ev(V.tensor_tensor_scan(RK[s][7][:, x], RK[s][3][:, x], RK[s][3][:, x], RK[s][6][:, h:h + 1], A.add, A.add))
-        E["on", s, h] = 1
+    def count(q):
+        def f(s, h):
+            wt(q, E["g", s, h])
+            x, last = slice(128 * h, 128 * h + 128), slice(128 * h + 127, 128 * h + 128)
+            E["s", s, h] = ev(V.tensor_tensor_scan(RK[s][4][:, x], RK[s][3][:, x], RK[s][3][:, x], 0.0, A.add, A.add) if q == "v" else
+                              S.activation(RK[s][7][:, x], RK[s][3][:, x], AF.Copy, scale=2.0, accum_out=RK[s][4][:, last]))
+        return f
 
     def steps(s, h):
         wt("v", E["s", s, h], E["o", s, h], E["cl%d" % h], E["cf"], *([E["f", 1]] if s == 2 else []))
-        out, edges, x = T.bb[:, h:320:2], T.c2[:, 160 * h:160 * h + 160], slice(128 * h + 127, 128 * h + 128)
-        if ("c3", s, h) in E:
-            wt("v", E["c3"])
-            edges = T.c3[:, 160 * h:160 * h + 160]
-        E["x", s] = ev(V.tensor_scalar(out, edges, RK[s][7][:, x], None, A.is_gt) if ("on", s, h) in E else
-                       V.tensor_scalar(out, edges, RK[s][4][:, x], RK[s][6][:, h:h + 1], A.subtract, A.is_gt), 1, E.get(("x", s)))
+        wt("v", E["cm"])
+        E["x", s] = ev(V.tensor_scalar(T.bb[:, h:320:2], T.c2[:, 160 * h:160 * h + 160], RK[s][4][:, 128 * h + 127:128 * h + 128],
+                                       RK[s][6][:, h:h + 1], A.subtract, A.is_gt), 1, E.get(("x", s)))
 
     def flags(s):
         assert E["x", s][1] == 2
-        wt("v", E["x", s], E["id"], E["nu"], *([E["k", 1]] + [E["l", 1] for _ in range(local)] if s == 2 else []))
+        wt("v", E["x", s], E["id"], *([E["k", 1]] if s == 2 else []))
         E["f", s] = ev(quant(pair("ff", 64 * s - 64, 64 * s + 64), T.bb[:, 0:512]))
 
-    def lists(s=2):
-        wt("t", E["f", s], E["un"])
-        take(("l", s))
-        E["l", s] = ev(mm(bank(("l", s)), pair("ff", 0, 128), pair("un", 0, 128)))
+    def lists():
+        wt("t", E["f", 2], E["un"])
+        take(("l",))
+        E["l"] = ev(mm(bank(("l",)), pair("ff", 0, 128), pair("un", 0, 128)))
 
-    def places(s=2):
-        wt("a", E["l", s])
-        if local and s == 2:
-            wt("a", E["rl"])
-            E["rl"] = read(("l", s), S.activation(T.pk[64:128, :], bank(("l", s), 0, 2, slice(64, 128)), AF.Copy,
-                                                  accum_out=T.ll[64:128, :]))
-            E["both"] = 1
-        else:
-            E["p"] = read(("l", s), S.activation(T.pj[:], bank(("l", s), 0, 2), AF.Copy, accum_out=T.pp[:]))
+    def places():
+        wt("a", E["l"])
+        E["p"] = read(("l",), S.activation(T.pj[:], bank(("l",), 0, 2), AF.Copy, accum_out=T.pp[:]))
 
     def turn(s):
-        wt("t", E["kq"], *([E["f", s]] if s == 1 or local else [E["rf"]] + landed(2, 0)))
+        wt("t", E["kq"], *([E["f", 1]] if s == 1 else [E["rf"]] + landed(2, 0)))
         take(("k", s))
-        E["k", s] = ev(mm(bank(("k", s)), pair("kq", 0, 128),
-                          pair("ff", 64 * s - 64, 64 * s + 64) if s == 1 or local else pair("bw", 48, 176)))
+        E["k", s] = ev(mm(bank(("k", s)), pair("kq", 0, 128), pair("ff", 0, 128) if s == 1 else pair("bw", 48, 176)))
 
     def offsets(s):
         wt("v", E["k", s], E["j"])
-        a = 64 if s == 1 or local else 0
-        E["off", s] = read(("k", s), V.tensor_scalar(ST[s][4][:], bank(("k", s), a, a + 16), lo, None, A.add))
+        a = 64 if s == 1 else 0
+        E["off", s] = read(("k", s), V.tensor_scalar(ST[s][4][:], bank(("k", s), a, a + 16), 256.0, lo, A.mult, A.add))
 
-    def spread(q):
-        def f(h=None):
-            a, b = cols(h)
-            wt(q.replace("w", "v"), E["ru"], E["zo"])
-            e = ev(gather(q, pair("um", a, b), pair("ul", 0, 2), T.zo[:, a // 16:b // 16], ("u", h)))
-            for k in halves(h):
-                E["um", q.replace("w", "a"), k] = e
+    def spread(k, q):
+        def f():
+            wt(q, E["ru"], E["zo"])
+            E["um", k] = ev(gather(k, q, pair("um", 0, 256), pair("ul", 0, 4), T.zo[:]))
         return f
 
     def send_flags():
         assert landed(2)
         wt("g", E["f", 2])
-        E["rf"] = send2(nxt, [(u8(T.bw[:, 48:64]), u8(T.ff[:, 128:144])), (T.bws[:, 0:64], T.ffs[:, 80:144])], "rf")
-
-    def send_flags2():
-        assert landed(2)
-        wt("g", E["f", 2])
-        E["rf"] = ("rf", send(u8(T.bw[:, 48:64]), u8(T.ff[:, 128:144]), "rf") + send(T.bws[:, 48:64], T.ffs[:, 128:144], "rf"))
+        E["rf"] = send_pair(pair("bw", 48, 64), pair("ff", 128, 144), "rf")
 
     def send_list():
-        assert landed(2) and (local or E["rf"])
+        assert E["rf"]
         wt("g", E["p"])
         E["rl"] = ("rl", send(T.ll[:], T.pp[:], "rl"))
 
-    def copy(q, out, in_):
-        return V.tensor_copy(out, in_) if q == "v" else S.activation(out, in_, AF.Copy)
-
-    def y_mm(h=None):
-        product(("ym",), [E["wq"]] + [E[q, "t", 2, k] for q in "va" for k in halves(h)], pair("wq", 0, 128), pair("t2", *cols(h)), h)
-
-    def y_copy(q):
-        def f(h=None):
-            e = behind(q, ("ym",), h, lambda p: copy(q, T.yt[:, cols(h)[0]:cols(h)[1]], p))
-            for k in halves(h):
-                E["y", k] = e
-        return f
-
-    def yy_mm(n, h=None):
+    def y_mm(n, h=None):
         a, b = cols(h)
-        product(("yy", n), [E["wq"]] + ([E["q", 2, k] for k in halves(h)] if n else landed(2, h)), pair("wq", 0, 128),
+        product(("yy", n), [E["wq"]] + ([E["q", 2, x] for x in halves(h)] if n else landed(2, h)), pair("wq", 0, 128),
                 pair("bw", 64 + 256 * n + a, 64 + 256 * n + b), h)
 
-    def yy_copy(q):
+    def y_copy(q):
         def f(n, h=None):
-            e = behind(q, ("yy", n), h, lambda p: copy(q, T.yw[:, 256 * n + cols(h)[0]:256 * n + cols(h)[1]], p))
-            for k in halves(h):
-                E["yw", n, k] = e
+            a, b = cols(h)
+            mark(("yw", n), h, behind(q, ("yy", n), h, lambda p: copy(q, T.yw[:, 256 * n + a:256 * n + b], p)))
         return f
 
-    def yy_pick(q):
-        def f(h=None):
-            a, b = cols(h)
-            wt(q, E["off", 2], *([E["yw", 0, k] for k in (0, 1)] + [E["yw", 1, k] for k in range(b // 128)]))
-            e = ev(copy(q, T.yt[:, a:b], T.yw[:, 0:256 + b].indirect(T.o2[:, a // 16:b // 16])))
-            for k in halves(h):
-                E["y", k] = e
-        return f
+    def y_pick(h=None):
+        a, b = cols(h)
+        wt("a", E["off", 2], *([E["yw", 0, x] for x in (0, 1)] + [E["yw", 1, x] for x in range(b // 128)]))
+        mark(("y",), h, ev(copy("a", T.yt[:, a:b], T.yw[:, 0:256 + b].indirect(T.o2[:, a // 16:b // 16]))))
 
     def store(q, out, in_, *es):
         wt(q, *es)
         E["out"] = ev(Q[q].dma_start(out, in_), 16, E.get("out"))
 
-    def store_oc(q):
-        def f(h=None):
-            a, b = cols(h)
-            store(q, T.oc[:, 4 * a:4 * b], u8(T.t2[:, a:b]), *[E["v", "t", 2, k] for k in halves(h)])
-        return f
-
-    def store_y(q):
-        def f(h=None):
-            a, b = cols(h)
-            store(q, T.y[:, a:b], T.yt[:, a:b], *[E["y", k] for k in halves(h)])
-        return f
-
     def store_osc(q):
-        def f(k):
-            store(q, T.osc[4 * k:4 * k + 4, :], T.t2s[32 * k:32 * k + 4, :], E["a", "t", 2, 0], E["a", "t", 2, 1])
-        return f
+        return lambda k: store(q, T.osc[4 * k:4 * k + 4, :], T.t2s[32 * k:32 * k + 4, :], E["t", 2, 1, 0], E["t", 2, 1, 1])
 
     STEP = {"v": prod("v", "vq"), "e": prod("e", "eq"), "r": relu("a"), "rv": relu("v"), "a": add, "pack": pack,
-            "pc": pick("v"), "ps": pick("a"), "pw": pick("w"),
-            "row": diff("row"), "col": diff("col"), "own": own, "oth": other, "cnt": count, "cno": count_on, "tie": tie, "sgn": sign, "cna": count_a, "step": steps,
-            "flags": flags,
-            "list": lists, "place": places, "turn": turn, "off": offsets, "spreadv": spread("v"), "spreada": spread("a"), "spreadw": spread("w"),
-            "sc": hand_on(0), "ss": hand_on(1), "sendu": send_u("un", 129), "senduq": send_u("uq", 0),
-            "hold": lambda: wt("g", E["g", 2, 1]),
-            "sendflags": send_flags, "sendflagsb": send_flags2, "sendlist": send_list,
-            "ym": y_mm, "yv": y_copy("v"), "ya": y_copy("a"), "yy": yy_mm, "ywv": yy_copy("v"), "ywa": yy_copy("a"),
-            "ypv": yy_pick("v"), "ypa": yy_pick("a"), "oc": store_oc("s"), "oca": store_oc("a"), "y": store_y("s"),
-            "yya": store_y("a"), "osc": store_osc("s"), "osca": store_osc("a"),
-            "li": lambda: store("s", T.li[:], T.ll[:], E["rl"], *[E["rl"] for _ in range(local and E["both"])]),
-            "lia": lambda: store("a", T.li[:], T.ll[:], E["rl"], *[E["rl"] for _ in range(local and E["both"])])}
+            "pc": pick(0, "v"), "ps": pick(1, "a"), "pw": pick(1, "v"), "row": diff("row"), "col": diff("col"), "own": own,
+            "oth": other, "cnt": count("v"), "cna": count("a"), "step": steps, "flags": flags, "list": lists, "place": places,
+            "turn": turn, "off": offsets, "spreadv": spread(0, "v"), "spreada": spread(1, "a"), "sc": hand_on(0),
+            "ss": hand_on(1), "sendu": send_u, "sendflags": send_flags, "sendlist": send_list, "yy": y_mm,
+            "ywv": y_copy("v"), "ywa": y_copy("a"), "yp": y_pick, "osc": store_osc("s"), "osca": store_osc("a"),
+            "oc": lambda: store("s", T.oc[:, 0:1024], u8(T.t2[:, 0:256]), E["t", 2, 0, 0], E["t", 2, 0, 1]),
+            "y": lambda: store("s", T.y[:, 0:256], T.yt[:, 0:256], E["y", 0], E["y", 1]),
+            "li": lambda: store("s", T.li[:], T.ll[:], E["rl"])}
 
     for name in START + STOP1 + AHEAD + STOP2:
         word = name.rstrip("0123456789")
@@ -501,8 +401,7 @@ def rank_program(g, core, T, topo):
         else:
             STEP[word](*[int(d) for d in name[len(word):]])
 
-    assert not [key for key in picked if picked.count(key) != 2]
-    done = {e for (_, e) in known}
-    wt("s", *[e for e in made if e[0] not in done and e is not E["out"]])
+    done = {key[1:] for key in known}
+    wt("s", *[e for e in made if tuple(e) not in done and e is not E["out"]])
     wt("s", E["out"])
     g.wait_ge(T.sem.lo, nloc["lo"])

from concourse.bass import DstId, RemoteDMATransfer
from concourse.mybir import dt, AluOpType, ActivationFunctionType

A = AluOpType
AF = ActivationFunctionType
F8, U8, BF, F32, I32, U16 = "float8_e4m3fn_x4", "uint8", "bfloat16", "float32", "int32", "uint16"
EPS = 2.0 ** -110
ZT, BB = 336, 856

SCRATCH = {}


def _pair(n, w):
    SCRATCH[n] = ("sbuf", [128, w], F8)
    SCRATCH[n + "s"] = ("sbuf", [128, w], U8)


for _n, _w in (("un", 258), ("uq", 128), ("ul", 16), ("um", 256), ("vq", 512), ("wq", 128), ("eq", 512), ("kq", 128), ("tq", 256),
               ("aw", 512), ("bw", 576), ("ff", 192), ("t1", 256), ("t2", 256)):
    _pair(_n, _w)
for _n, _w, _d in (("xt", 1024, BF), ("bb", BB, BF), ("ub", 4, BF), ("ut", 1036, BF), ("vt", 2048, BF), ("wt", 512, BF),
                   ("kt", 512, BF), ("n1", 1024, BF), ("n2", 1024, BF), ("tb", 128, BF), ("ib", 128, BF), ("c2", 320, BF),
                   ("g1", 256, BF), ("g2", 256, BF), ("sc1", 256, F32), ("sc2", 256, F32), ("sb1", 256, BF), ("sb2", 256, BF),
                   ("jk1", 256, BF), ("jk2", 256, BF), ("sg1", 2, F32), ("sg2", 2, F32), ("r1", 1024, F32), ("r2", 1024, F32),
                   ("jj", 8, I32), ("ja", 8, I32), ("sp", 8, F32), ("i16", 24, F32), ("zo", 16, U16), ("o1", 16, U16),
                   ("o2", 16, U16), ("pp", 1, F32), ("ll", 1, F32), ("pj", 2, F32), ("yt", 256, F32), ("yw", 512, F32)):
    SCRATCH[_n] = ("sbuf", [128, _w], _d)
for _n, _w in (("pr", 2048), ("pm", 2048)):
    SCRATCH[_n] = ("psum", [128, _w], F32)

SEMAPHORES = ["s%d" % _i for _i in range(141)] + ["lo", "lt", "ru", "in10", "in11", "in20", "in21", "rf", "rl"]

START = ("x0 u x1 va vb z ii jj id tb e0 tq0 sc10 up kb cm zo ja e3 tq1 j nu e1 km uq um ss1 kd sc11 sendu e2 w cl0 q0 q1 un "
         "cf k q2 cl1 q3 kq").split()
STOP1 = ("v100 row100 col100 col101 own10 col111 cna10 row111 rv100 row110 col110 own11 row101 v12 oth10 spreadv oth11 cnt11 "
         "step10 e100 a100 v11 e12 v13 e11 step11 v101 r120 e13 a120 r121 r11 a121 flags1 r13 e101 a11 r101 a130 a101 spreada "
         "a131 pack10 turn1 off1 pack11 pc10 ps10 pc11 ps11").split()
AHEAD = ("sc20 row200 col200 ss2 col201 row211 sc21 wq col211 row201 oth20 col210 own20 row210 oth21 own21 v210 v200 e200 v22 "
         "r210 v211 r200 e210 e22 v23 cnt20 cnt21 step20 step21 r220 flags2 sendflags").split()
STOP2 = ("e211 a210 v201 a220 e230 r211 r221 a200 a211 a221 e231 r230 e201 a230 r231 r201 list place yy0 ywa00 a231 a201 "
         "pack20 pack21 turn2 sendlist off2 li yy10 ywa10 yy11 ywa11 ywv01 yp0 pc2 pw2 yp1 oc y osc2 osca3 osca0 osca1").split()


def rank_program(g, core, T, topo):
    rank = T.rank_of(core)
    if rank is None:
        return
    nxt, prv = T.cores[(rank + 1) % len(T.cores)], T.cores[(rank - 1) % len(T.cores)]
    Q = {"g": g, "v": g.vector, "a": g.scalar, "s": g.sync, "t": g.tensor}
    V, S, P, Y = g.vector, g.scalar, g.tensor, g.sync
    made, known, nloc, E = [], {}, {"lo": 0, "lt": 0}, {}
    names, spare = {}, []

    def ev(ins, k=1, e=None, stop=0):
        if e is None:
            e = list(spare.pop()) if stop == 2 and spare else ["s%d" % len(names), 0]
            names[e[0]] = 1
            made.append(e)
            if stop == 1:
                spare.append(e)
        ins.then_inc(T.sem[e[0]], k)
        e[1] += k
        return e

    def wt(q, *es):
        for e in es:
            if (q, e[0], e[1]) not in known:
                known[q, e[0], e[1]] = 1
                Q[q].wait_ge(T.sem[e[0]], e[1])

    def send(out, in_, sem, loc="lo", dst=nxt):
        rid, pid, _ = topo.addr(dst)
        g.remote_dma(out, in_, T.sem[sem], T.sem[loc], pid, rid, topo.mask(core, dst))
        k = len(topo.engines(core, dst))
        nloc[loc] += k
        return k

    def u8(v):
        return v.bitcast(dt.uint8)

    def u32(v):
        return v.bitcast(dt.uint32)

    def pair(name, a, b):
        return T[name][:, a:b], T[name + "s"][:, a:b]

    def send_pair(out, in_, sem, loc="lo", dst=nxt):
        return (sem, send(u8(out[0]), u8(in_[0]), sem, loc, dst) + send(out[1], in_[1], sem, loc, dst))

    def cols(h):
        return (0, 256) if h is None else (128 * h, 128 * h + 128)

    def halves(h):
        return (0, 1) if h is None else (h,)

    def quant(dst, src):
        return V.quantize_mx(dst[0], dst[1], src)

    def mm(out, lhs, rhs, start=True, stop=True):
        return P.matmul_mx(out, lhs[0], lhs[1], rhs[0], rhs[1], start, stop)

    def copy(q, out, in_):
        return V.tensor_copy(out, in_) if q == "v" else S.activation(out, in_, AF.Copy)

    def gather(k, q, dst, win, off):
        return copy(q, dst[1], win[1].indirect(off)) if k else V.tensor_copy(u32(dst[0]), u32(win[0]).indirect(off))

    def iota(out, pattern, base, cm=0):
        return g.iota(out, pattern, base, cm, allow_small_or_imprecise_dtypes=True)

    hi, lo = T.ut[:, 4:5], T.ut[:, 8:9]
    ident = T.bb[:, ZT + 4:ZT + 516:4]
    zeros = T.bb[:, ZT + 1:ZT + 513:4]

    def cf():
        return ([V.tensor_scalar(T.c2[:, 160 * h + 128:160 * h + 160:2], T.i16[:, 8 - 8 * h:24 - 8 * h], hi, -256.0,
                                 A.not_equal, A.mult) for h in (0, 1)] +
                [V.tensor_scalar(T.c2[:, 129:160:2], T.ib[:, 0:16], 128.5, 1024.0, A.subtract, A.mult)])

    CALLS = {
        "x0": ("s", (), lambda: [Y.dma_start(T.xt[:, 0:512], T.x[:, 0:512])], 16),
        "x1": ("s", (), lambda: [Y.dma_start(T.xt[:, 512:1024], T.x[:, 512:1024])], 16),
        "u": ("s", (), lambda: [Y.dma_start(T.ub[:], T.u[:, 0:4])], 16),
        "va": ("s", (), lambda: [Y.dma_start(T.vt[:, 0:1024], T.v[:, 0:1024])], 16),
        "vb": ("s", (), lambda: [Y.dma_start(T.vt[:, 1024:2048], T.v[:, 1024:2048])], 16),
        "w": ("s", ("lt",), lambda: [Y.dma_start(T.wt[:], T.w[:])], 16),
        "tq0": ("v", ("x0",), lambda: [quant(pair("tq", 0, 128), T.xt[:, 0:512])], 1),
        "tq1": ("v", ("x1",), lambda: [quant(pair("tq", 128, 256), T.xt[:, 512:1024])], 1),
        "wq": ("v", ("w",), lambda: [quant(pair("wq", 0, 128), T.wt[:])], 1),
        "ii": ("g", (), lambda: [iota(T.ib[:], [[1, 128]], 128, -1)], 1),
        "z": ("v", (), lambda: [V.memset(T.bb[:, 320:BB], 0.0)], 1),
        "id": ("v", ("z", "ii"), lambda: [V.tensor_scalar(ident, T.ib[:], 128.0, None, A.is_equal)], 1),
        "tb": ("v", ("ii",), lambda: [V.tensor_scalar(T.tb[:], T.ib[:], 128.0, -EPS, A.is_lt, A.mult)], 1),
        "jj": ("g", (), lambda: [g.iota(T.jj[:], [[0, 4], [128, 2]], 0, 1), iota(T.sp[:], [[0, 2], [-2, 2], [0, 2]], 1),
                                 iota(T.i16[:], [[16, 24]], -128)], 1),
        "ja": ("v", ("jj",), lambda: [V.tensor_scalar(T.ja[:, 0:4], T.jj[:, 0:4], 240, None, A.bitwise_and),
                                      V.tensor_scalar(T.ja[:, 4:8], T.jj[:, 4:8], 15, None, A.bitwise_and)], 1),
        "j": ("v", ("ja",), lambda: [V.tensor_tensor(T.ut[:, 4:12], T.ja[:], T.sp[:], A.mult)], 1),
        "nu": ("v", ("u",), lambda: [V.tensor_scalar(T.ut[:, 0:4], T.ub[:], -1.0, None, A.mult)], 1),
        "up": ("a", ("u", "id"), lambda: [S.activation(T.ut[:, 12 + t:524:4], zeros, AF.Identity, bias=T.ub[:, t:t + 1])
                                          for t in range(4)], 1),
        "uq": ("v", ("up", "nu", "j"), lambda: [quant(pair("uq", 0, 128), T.ut[:, 0:512])], 1),
        "um": ("a", ("up",), lambda: [S.activation(T.ut[:, 524:1036], T.ut[:, 12:524], AF.Copy, scale=-1.0)], 1),
        "un": ("v", ("um", "j"), lambda: [quant(pair("un", 0, 258), T.ut[:, 4:1036])], 1),
        "zo": ("v", ("jj",), lambda: [V.tensor_scalar(T.zo[:], T.i16[:, 0:16], 0.0, 3.0, A.is_lt, A.mult)], 1),
        "cl0": ("g", (), lambda: [iota(T.c2[:, 0:128], [[2, 64], [-2, 2]], -127)], 1),
        "cl1": ("a", ("cl0",), lambda: [S.activation(T.c2[:, 160:288], T.c2[:, 0:128], AF.Copy)], 1),
        "cf": ("v", ("ii", "j"), cf, 1),
        "cm": ("a", ("jj",), lambda: [S.activation(T.c2[:, 289:320:2], T.i16[:, 0:16], AF.Identity, bias=-256.0, scale=0.0)], 1),
        "km": ("v", ("j",), lambda: [V.tensor_scalar(T.kt[:, t:64:4], T.i16[:, 8:24], 1.0 / 16, lo, A.mult, A.is_equal)
                                     for t in (0, 1)], 1),
        "kb": ("a", ("jj",), lambda: [S.activation(T.kt[:, t:64:4], T.i16[:, 0:16], AF.Identity, bias=1.0 / 16, scale=0.0)
                                      for t in (2, 3)], 1),
        "kd": ("a", ("km", "kb"), lambda: [S.activation(T.kt[:, 64 * n:64 * n + 64], T.kt[:, 0:64], AF.Copy) for n in (1, 2, 3)], 1),
        "k": ("a", ("kd",), lambda: [S.activation(T.kt[:, 256:512], T.kt[:, 0:256], AF.Copy)], 1),
        "kq": ("v", ("k",), lambda: [quant(pair("kq", 0, 128), T.kt[:])], 1),
    }

    def qf(dst, src):
        return lambda: [quant(dst, src)]

    for b in range(4):
        CALLS["q%d" % b] = ("v", ("v" + "ab"[b // 2],), qf(pair("vq", 128 * b, 128 * b + 128), T.vt[:, 512 * b:512 * b + 512]), 1)
        CALLS["e%d" % b] = ("v", ("id",), qf(pair("eq", 128 * b, 128 * b + 128), T.bb[:, ZT + 4 - b:ZT + 516 - b]), 1)

    def const(name):
        q, waits, calls, k = CALLS[name]
        name = "e" if name[0] == "e" else name
        assert name != "w" or (landed(1) and E["ru"])
        E["lt"] = ("lt", nloc["lt"])
        wt(q, *[E[x] for x in waits])
        for ins in calls():
            E[name] = ev(ins, k, E.get(name))

    ST = {1: ("aw", 0, T.r1, T.n1, T.o1, "t1"), 2: ("bw", 64, T.r2, T.n2, T.o2, "t2")}
    RK = {1: (pair("un", 2, 130), pair("un", 130, 258), "aw", T.g1, T.sc1, T.jk1, T.sg1, T.sb1),
          2: (pair("um", 0, 128), pair("um", 128, 256), "t1", T.g2, T.sc2, T.jk2, T.sg2, T.sb2)}

    pieces = {}

    def hand_on(k):
        def f(s, h=None):
            (a, b), (w, c0) = cols(h), ST[s][:2]
            wt("g", *[E["tq%d" % x] if s == 1 else E["t", 1, k, x] for x in halves(h)])
            dst, src = pair(w, c0 + a, c0 + b)[k], pair(("tq", "t1")[s - 1], a, b)[k]
            sem = "in%d%d" % (s, halves(h)[0])
            assert not [key for key in known if key[1] == sem]
            e = E.setdefault(sem, [sem, 0])
            e[1] += send(dst if k else u8(dst), src if k else u8(src), sem, "lt" if s == 1 else "lo")
            for x in halves(h):
                pieces[s, k, x] = e
        return f

    def landed(s, h=None):
        return [pieces[s, k, x] for k in (0, 1) for x in halves(h)]

    def send_u():
        wt("g", E["uq"])
        rid, pid, _ = topo.addr(prv)
        es = topo.engines(core, prv)
        n = len(es) // 2
        sides = ((u8(T.ul[:, 0:4]), u8(T.uq[:, 0:4])), (T.uls[:, 0:16], T.uqs[:, 0:16]))
        g.remote_dma_fused([RemoteDMATransfer(dst_ids=[DstId(rid=rid, pnc=pid)], dma_engine_mask=sum(1 << e for e in es[i * n:i * n + n]),
                                              remote_sem=T.sem.ru, srcs=[s], dsts=[d], alu_op=0)
                            for i, (d, s) in enumerate(sides)], local_sem=T.sem.lt)
        nloc["lt"] += 2 * n
        E["ru"] = ("ru", 2 * n)

    free, held, left, reader, where = list(range(8)), {}, {b: [] for b in range(8)}, {}, {}

    def take(name, parts=1):
        b = free.pop(0)
        wt("t", *left[b])
        held[name] = [b, parts, []]

    def bank(name, a=0, b=128):
        i = held[name][0]
        return (T.pr, T.pm)[i // 4][:, 512 * (i % 4) + a:512 * (i % 4) + b]

    def read(name, ins, parts=1):
        x, e = held[name], ev(ins, stop=name[1] if name[0] in ("v", "e") else 0)
        x[1] -= parts
        x[2].append(e)
        if x[1] == 0:
            left[x[0]] = x[2]
            free.append(x[0])
        return e

    def product(key, waits, lhs, rhs, h):
        wt("t", *waits)
        take(key + (h,), len(halves(h)))
        stop = key[1] if key[0] in ("v", "e") else 0
        if stop == 2:
            wt("t", *[E["t", 1, k, x] for k in (0, 1) for x in (0, 1)])
        e = ev(mm(bank(key + (h,), 0, 128 * len(halves(h))), lhs, rhs), stop=stop)
        for x in halves(h):
            E[key + (x,)], where[key + (x,)] = e, (key + (h,), 128 * x - cols(h)[0])

    def behind(q, key, h, call):
        name, a = where[key + halves(h)[:1]]
        assert name == where[key + halves(h)[-1:]][0]
        wt(q, E[key + halves(h)[:1]], *[e for e in held[name][2] if reader[e[0]] != q])
        e = read(name, call(bank(name, a, a + 128 * len(halves(h)))), len(halves(h)))
        reader[e[0]] = q
        return e

    def mark(key, h, e):
        for x in halves(h):
            E[key + (x,)] = e

    def prod(kind, name):
        def f(s, i, h=None):
            (a, b), (w, c0) = cols(h), ST[s][:2]
            assert kind == "v" or E["e"][1] == 4
            product((kind, s, i), landed(s, h) + [E["q%d" % i if kind == "v" else "e"]], pair(name, 128 * i, 128 * i + 128),
                    pair(w, c0 + a, c0 + b), h)
        return f

    def part(s, i, h):
        return ST[s][2][:, 256 * i + cols(h)[0]:256 * i + cols(h)[1]]

    def relu(q):
        def f(s, i, h=None):
            mark(("r", s, i), h, behind(q, ("v", s, i), h, lambda p: S.activation(part(s, i, h), p, AF.Relu, scale=0.05)
                                        if q == "a" else V.tensor_scalar(part(s, i, h), p, 0.0, 0.05, A.max, A.mult)))
        return f

    def add(s, i, h=None):
        a, b = cols(h)
        wt("v", *[E["r", s, i, x] for x in halves(h)])
        mark(("a", s, i), h, behind("v", ("e", s, i), h, lambda p: V.tensor_tensor(ST[s][3][:, 4 * a + i:4 * b:4], p,
                                                                                   part(s, i, h), A.add)))

    def pack(s, h=None):
        (a, b), (w, c0) = cols(h), ST[s][:2]
        wt("v", *[E["a", s, i, x] for i in range(4) for x in halves(h)])
        mark(("q", s), h, ev(quant(pair(w, c0 + 256 + a, c0 + 256 + b), ST[s][3][:, 4 * a:4 * b])))

    def pick(k, q):
        def f(s, h=None):
            (a, b), (w, c0) = cols(h), ST[s][:2]
            wt(q, E["off", s], *(landed(s) + [E["q", s, x] for x in range(b // 128)]))
            mark(("t", s, k), h, ev(gather(k, q, pair(ST[s][5], a, b), pair(w, c0, c0 + 256 + b), ST[s][4][:, a // 16:b // 16])))
        return f

    def diff(kind):
        def f(s, j, k):
            name, h = ("d", s, j, k), (k if kind == "row" else j)
            wt("t", *(landed(1, h) + [E["un"]] if s == 1 else [E["t", 1, 0, h], E["t", 1, 1, h], E["um", 0], E["um", 1]]))
            first = name not in held
            if first:
                take(name)
            tile = pair(RK[s][2], *cols(h))
            ins = mm(bank(name), *((RK[s][0], tile) if kind == "row" else (tile, RK[s][1])), first, not first)
            if not first:
                E[name] = ev(ins)
        return f

    def own(s, h):
        name = ("d", s, h, h)
        wt("v", E[name], E["tb"])
        E["g", s, h] = read(name, V.tensor_tensor(RK[s][3][:, 128 * h:128 * h + 128], bank(name), T.tb[:], A.is_gt))

    def other(s, h):
        name = ("d", s, h, 1 - h)
        wt("a", E[name])
        E["o", s, h] = read(name, S.activation(RK[s][5][:, 128 * h:128 * h + 128], bank(name), AF.Sign, bias=(EPS if h else -EPS),
                                               accum_out=RK[s][6][:, h:h + 1]))

    def count(q):
        def f(s, h):
            wt(q, E["g", s, h])
            x, last = slice(128 * h, 128 * h + 128), slice(128 * h + 127, 128 * h + 128)
            E["s", s, h] = ev(V.tensor_tensor_scan(RK[s][4][:, x], RK[s][3][:, x], RK[s][3][:, x], 0.0, A.add, A.add) if q == "v" else
                              S.activation(RK[s][7][:, x], RK[s][3][:, x], AF.Copy, scale=2.0, accum_out=RK[s][4][:, last]))
        return f

    def steps(s, h):
        wt("v", E["s", s, h], E["o", s, h], E["cl%d" % h], E["cf"], *([E["f", 1]] if s == 2 else []))
        wt("v", E["cm"])
        E["x", s] = ev(V.tensor_scalar(T.bb[:, h:320:2], T.c2[:, 160 * h:160 * h + 160], RK[s][4][:, 128 * h + 127:128 * h + 128],
                                       RK[s][6][:, h:h + 1], A.subtract, A.is_gt), 1, E.get(("x", s)))

    def flags(s):
        assert E["x", s][1] == 2
        wt("v", E["x", s], E["id"], *([E["k", 1]] if s == 2 else []))
        E["f", s] = ev(quant(pair("ff", 64 * s - 64, 64 * s + 64), T.bb[:, 0:512]))

    def lists():
        wt("t", E["f", 2], E["un"])
        take(("l",))
        E["l"] = ev(mm(bank(("l",)), pair("ff", 0, 128), pair("un", 0, 128)))

    def places():
        wt("a", E["l"])
        E["p"] = read(("l",), S.activation(T.pj[:], bank(("l",), 0, 2), AF.Copy, accum_out=T.pp[:]))

    def turn(s):
        wt("t", E["kq"], *([E["f", 1]] if s == 1 else [E["rf"]] + landed(2, 0)))
        take(("k", s))
        E["k", s] = ev(mm(bank(("k", s)), pair("kq", 0, 128), pair("ff", 0, 128) if s == 1 else pair("bw", 48, 176)))

    def offsets(s):
        wt("v", E["k", s], E["j"])
        a = 64 if s == 1 else 0
        E["off", s] = read(("k", s), V.tensor_scalar(ST[s][4][:], bank(("k", s), a, a + 16), 256.0, lo, A.mult, A.add))

    def spread(k, q):
        def f():
            wt(q, E["ru"], E["zo"])
            E["um", k] = ev(gather(k, q, pair("um", 0, 256), pair("ul", 0, 4), T.zo[:]))
        return f

    def send_flags():
        assert landed(2)
        wt("g", E["f", 2])
        E["rf"] = send_pair(pair("bw", 48, 64), pair("ff", 128, 144), "rf")

    def send_list():
        assert E["rf"]
        wt("g", E["p"])
        E["rl"] = ("rl", send(T.ll[:], T.pp[:], "rl"))

    def y_mm(n, h=None):
        a, b = cols(h)
        product(("yy", n), [E["wq"]] + ([E["q", 2, x] for x in halves(h)] if n else landed(2, h)), pair("wq", 0, 128),
                pair("bw", 64 + 256 * n + a, 64 + 256 * n + b), h)

    def y_copy(q):
        def f(n, h=None):
            a, b = cols(h)
            mark(("yw", n), h, behind(q, ("yy", n), h, lambda p: copy(q, T.yw[:, 256 * n + a:256 * n + b], p)))
        return f

    def y_pick(h=None):
        a, b = cols(h)
        wt("a", E["off", 2], *([E["yw", 0, x] for x in (0, 1)] + [E["yw", 1, x] for x in range(b // 128)]))
        mark(("y",), h, ev(copy("a", T.yt[:, a:b], T.yw[:, 0:256 + b].indirect(T.o2[:, a // 16:b // 16]))))

    def store(q, out, in_, *es):
        wt(q, *es)
        E["out"] = ev(Q[q].dma_start(out, in_), 16, E.get("out"))

    def store_osc(q):
        return lambda k: store(q, T.osc[4 * k:4 * k + 4, :], T.t2s[32 * k:32 * k + 4, :], E["t", 2, 1, 0], E["t", 2, 1, 1])

    STEP = {"v": prod("v", "vq"), "e": prod("e", "eq"), "r": relu("a"), "rv": relu("v"), "a": add, "pack": pack,
            "pc": pick(0, "v"), "ps": pick(1, "a"), "pw": pick(1, "v"), "row": diff("row"), "col": diff("col"), "own": own,
            "oth": other, "cnt": count("v"), "cna": count("a"), "step": steps, "flags": flags, "list": lists, "place": places,
            "turn": turn, "off": offsets, "spreadv": spread(0, "v"), "spreada": spread(1, "a"), "sc": hand_on(0),
            "ss": hand_on(1), "sendu": send_u, "sendflags": send_flags, "sendlist": send_list, "yy": y_mm,
            "ywv": y_copy("v"), "ywa": y_copy("a"), "yp": y_pick, "osc": store_osc("s"), "osca": store_osc("a"),
            "oc": lambda: store("s", T.oc[:, 0:1024], u8(T.t2[:, 0:256]), E["t", 2, 0, 0], E["t", 2, 0, 1]),
            "y": lambda: store("s", T.y[:, 0:256], T.yt[:, 0:256], E["y", 0], E["y", 1]),
            "li": lambda: store("s", T.li[:], T.ll[:], E["rl"])}

    for name in START + STOP1 + AHEAD + STOP2:
        word = name.rstrip("0123456789")
        if name in CALLS:
            const(name)
        else:
            STEP[word](*[int(d) for d in name[len(word):]])

    done = {key[1:] for key in known}
    wt("s", *[e for e in made if tuple(e) not in done and e is not E["out"]])
    wt("s", E["out"])
    g.wait_ge(T.sem.lo, nloc["lo"])
